import numpy as np
import ml_dtypes


def mxq(x, axis, fmt="e4m3"):
    dtype, down = {"e4m3": (ml_dtypes.float8_e4m3fn, 7), "e5m2": (ml_dtypes.float8_e5m2, 14)}[fmt]
    v = np.moveaxis(np.asarray(x, np.float32).astype(ml_dtypes.bfloat16).astype(np.float64), axis, -1)
    blocks = v.reshape(v.shape[:-1] + (-1, 32))
    amax = np.abs(blocks).max(-1, keepdims=True)
    byte = np.maximum(np.where(amax > 0, np.frexp(amax)[1] - 1 + 127, 0) - down, 1)
    scale = np.exp2(byte - 127.0)
    codes = (blocks / scale).astype(np.float32).astype(dtype).astype(np.float64)
    return np.moveaxis((codes * scale).reshape(v.shape), -1, axis)


WIDE = False


def mx_kscale(k):
    if not WIDE:
        return np.ones(k)
    levels = np.array([10, -10, 5, -5, 0])
    if k % 512:
        return np.exp2(np.random.permutation(np.resize(levels, k // 32))).repeat(32)
    a = np.empty((k // 512, 16))
    for p in range(k // 512):
        a[p, :8] = np.random.permutation(np.resize(levels, 8))
        for g in range(8):
            far = levels[np.abs(levels - a[p, g]) >= 10]
            a[p, g + 8] = far[np.random.randint(len(far))]
    return np.exp2(a.ravel()).repeat(32)


def f64(x):
    return np.asarray(x).astype(np.float64)


def striped(idx):
    return np.tile(idx.reshape(-1, 16).T, (8, 1)).astype(np.uint16)


def unstriped(offs):
    return offs[:16].T.reshape(-1).astype(np.int64)


E2M1 = np.array([0.0, 0.5, 1.0, 1.5, 2.0, 3.0, 4.0, 6.0, -0.0, -0.5, -1.0, -1.5, -2.0, -3.0, -4.0, -6.0])


def pack_weight(w, fmt):
    k, n = w.shape
    w = f64(np.asarray(w, np.float32).astype(ml_dtypes.bfloat16)).reshape(k // 32, 32, n)
    amax = np.abs(w).max(1)
    if fmt == "e4m3":
        byte = np.frexp(amax)[1] - 1 + 127 - 7
    else:
        mant, ex = np.frexp(amax / 6.0)
        byte = np.where(mant > 0.5, ex, ex - 1) + 127
    byte = np.clip(np.where(amax > 0, byte, 1), 1, 254)
    scaled = (w * np.exp2(127.0 - byte)[:, None, :]).reshape(k, n).astype(np.float32)
    by_word = np.ascontiguousarray(scaled.reshape(k // 512, 128, 4, n).transpose(0, 1, 3, 2))
    if fmt == "e4m3":
        words = by_word.astype(ml_dtypes.float8_e4m3fn).view(np.uint8)
    else:
        c = by_word.astype(ml_dtypes.float4_e2m1fn).view(np.uint8) & 0xF
        words = (c[..., 0::2] | (c[..., 1::2] << 4)).reshape(k // 512, 128, 2 * n)
    return np.ascontiguousarray(words), np.ascontiguousarray(byte.astype(np.uint8).reshape(k // 512, 16, n))


def unpack_weight(words, scales, fmt):
    g, _, n = scales.shape
    words = np.ascontiguousarray(words).reshape(g, 128, n, -1)
    if fmt == "e4m3":
        vals = words.view(ml_dtypes.float8_e4m3fn).astype(np.float64)
    else:
        nib = np.empty((g, 128, n, 4), np.uint8)
        nib[..., 0::2] = words & 0xF
        nib[..., 1::2] = words >> 4
        vals = E2M1[nib]
    vals = vals * np.repeat(np.exp2(scales.astype(np.float64) - 127.0), 8, axis=1)[..., None]
    return vals.transpose(0, 1, 3, 2).reshape(g * 512, n)


def gelu(v):
    return 0.5 * v * (1.0 + np.tanh(np.sqrt(2.0 / np.pi) * (v + 0.044715 * v**3)))


def often(T, S):
    return np.random.permutation(T)[(T * np.random.uniform(0, 1, S) ** 4).astype(np.int64)]


K, H, N, T, S, T2, P = 512, 1536, 512, 4096, 1024, 2048, 512

def setup_inputs():
    n = np.random.standard_normal
    s = mx_kscale(K)[:, None]
    u = mx_kscale(H)[:, None]
    tab_words, tab_scales = pack_weight(n((K, T)) * s, "e4m3")
    tab2_words, tab2_scales = pack_weight(n((K, T2)) * s, "e4m3")
    ws_words, ws_scales = pack_weight(n((K, H)) / np.sqrt(K) / s, "e2m1")
    wf_words, wf_scales = pack_weight(n((K, H)) / np.sqrt(K) / s, "e4m3")
    return {
        "tab_words": tab_words, "tab_scales": tab_scales,
        "offs": striped(np.random.permutation(T)[:S]),
        "pos1": striped(often(S, P)),
        "tab2_words": tab2_words, "tab2_scales": tab2_scales,
        "offs2": striped(np.random.permutation(T2)[:P]),
        "wv": (n((K, H)) / np.sqrt(K) / s * u.T).astype(np.float32),
        "ws_words": ws_words, "ws_scales": ws_scales,
        "wf_words": wf_words, "wf_scales": wf_scales,
        "off": (n(H) * u[:, 0]).astype(np.float32),
        "wo": (n((H, N)) / np.sqrt(H) / u).astype(np.float32),
    }

def reference(tab_words, tab_scales, offs, pos1, tab2_words, tab2_scales, offs2, wv, ws_words, ws_scales, wf_words, wf_scales, off, wo):
    v = unpack_weight(tab_words, tab_scales, "e4m3")[:, unstriped(offs)]
    v2 = unpack_weight(tab2_words, tab2_scales, "e4m3")[:, unstriped(offs2)]
    ws = unpack_weight(ws_words, ws_scales, "e2m1")
    wf = unpack_weight(wf_words, wf_scales, "e4m3")
    h = mxq(f64(wv), 0, "e4m3").T @ v
    d = ws.T @ v
    b = wf.T @ v2
    hp = h[:, unstriped(pos1)]
    dp = d[:, unstriped(pos1)]
    z = hp + f64(off)[:, None] * np.minimum(np.abs(dp), np.abs(b))
    out = mxq(f64(wo), 0, "e4m3").T @ mxq(z, 0, "e4m3")
    return out

@@ -1,0 +1,251 @@
+from contextlib import ExitStack
+
+import concourse.mybir as mybir
+from concourse.masks import make_identity
+
+K, H, N, T, S, T2, M = 512, 1536, 512, 4096, 1024, 2048, 512
+FLOPS = 2 * K * H * (2 * S + M) + 2 * H * N * M
+
+F32 = mybir.dt.float32
+BF16 = mybir.dt.bfloat16
+I32 = mybir.dt.int32
+U32 = mybir.dt.uint32
+U16 = mybir.dt.uint16
+U8 = mybir.dt.uint8
+FP8X4 = mybir.dt.float8_e4m3fn_x4
+FP4X4 = mybir.dt.float4_e2m1fn_x4
+ALU = mybir.AluOpType
+ACT = mybir.ActivationFunctionType
+
+P = 128
+PACK = 4
+RUN = 4
+GROUP = P * PACK
+GROUPS = H // GROUP
+BANK = 512
+TAB2_ROW = 4
+WF_ROW = 8
+
+
+def tile_list_mesh_block_refinement_kernel(
+    tc, tab_words, tab_scales, offs, pos1, tab2_words, tab2_scales, offs2, wv,
+    ws_words, ws_scales, wf_words, wf_scales, off, wo, out,
+):
+    nc = tc.nc
+    with ExitStack() as ctx:
+        keep = ctx.enter_context(tc.tile_pool(name="keep", bufs=1))
+        ring = ctx.enter_context(tc.tile_pool(name="ring", bufs=2))
+        psum = ctx.enter_context(tc.psum_pool(name="psum", bufs=1))
+
+        def held(name, shape, dtype):
+            return keep.tile(shape, dtype, name=name, align_bytes=64)
+
+        def turn(name, shape, dtype, bufs):
+            return ring.tile(shape, dtype, name=name, bufs=bufs, align_bytes=64)
+
+        def load_scales(queue, plane, scales, row):
+            for q in range(4):
+                queue.dma_start(
+                    out=plane[32 * q + row : 32 * q + row + 4, :].bitcast(I32),
+                    in_=scales[0, 4 * q : 4 * q + 4, :].bitcast(I32),
+                )
+
+        idx = held("idx", [P, S // 16], U16)
+        idx2 = held("idx2", [P, M // 16], U16)
+        p1 = held("p1", [P, M // 16], U16)
+        tab_w = held("tab_w", [P, T], U32)
+        tab_s = held("tab_s", [P, T], U8)
+        tab2_w = held("tab2_w", [P, T2], U32)
+        tab2_s = held("tab2_s", [P, T2], U8)
+        ws_w = held("ws_w", [P, 2 * H], U8)
+        ws_s = held("ws_s", [P, H], U8)
+        wf_w = held("wf_w", [P, H], U32)
+        wf_s = held("wf_s", [P, H], U8)
+        off_rows = held("off_rows", [P, GROUPS * P], F32)
+        off_col = held("off_col", [P, GROUPS, PACK], F32)
+        ident = held("ident", [P, P], F32)
+
+        nc.vector.memset(tab_s[:].bitcast(I32), 0)
+        nc.gpsimd.memset(ws_s[:].bitcast(I32), 0)
+        nc.gpsimd.memset(off_rows[:], 0.0)
+        nc.vector.memset(tab2_s[:].bitcast(I32), 0)
+        nc.vector.memset(wf_s[:].bitcast(I32), 0)
+
+        nc.sync.dma_start(idx[:], offs)
+        nc.sync.dma_start(out=ws_w[:].bitcast(I32), in_=ws_words[0].bitcast(I32))
+        load_scales(nc.scalar, tab_s, tab_scales, 0)
+        nc.sync.dma_start(
+            out=tab_w[:].bitcast(I32),
+            in_=tab_words[0].rearrange("p t i -> p (t i)").bitcast(I32),
+        )
+        load_scales(nc.scalar, ws_s, ws_scales, 0)
+        nc.gpsimd.dma_start(
+            out=off_rows[0:PACK, :].rearrange("t (c i) -> t c i", i=RUN),
+            in_=off.rearrange("(c t i) -> t c i", t=PACK, i=RUN),
+        )
+        make_identity(nc, ident[:])
+        nc.sync.dma_start(p1[:], pos1)
+
+        def load_wv(g):
+            raw = turn("raw", [P, PACK, GROUP], F32, 5)
+            nc.sync.dma_start(
+                out=raw[:],
+                in_=wv[:, g * GROUP : (g + 1) * GROUP].rearrange("(p j) r -> p j r", j=PACK),
+            )
+            return raw
+
+        def load_wo(g):
+            raw = turn("raw", [P, PACK, N], F32, 5)
+            rows = wo[g * GROUP : (g + 1) * GROUP, :].rearrange("(c t i) n -> t c i n", t=PACK, i=RUN)
+            for t in range(PACK):
+                nc.sync.dma_start(out=raw[:, t, :], in_=rows[t])
+            return raw
+
+        wv_raw = [load_wv(0)]
+        nc.sync.dma_start(idx2[:], offs2)
+        nc.sync.dma_start(
+            out=tab2_w[:].bitcast(I32),
+            in_=tab2_words[0].rearrange("p t i -> p (t i)").bitcast(I32),
+        )
+        load_scales(nc.sync, tab2_s, tab2_scales, TAB2_ROW)
+        nc.sync.dma_start(
+            out=wf_w[:].bitcast(I32),
+            in_=wf_words[0].rearrange("p t i -> p (t i)").bitcast(I32),
+        )
+        load_scales(nc.sync, wf_s, wf_scales, WF_ROW)
+        wv_raw.append(load_wv(1))
+        wo_raw = [load_wo(0)]
+        wv_raw.append(load_wv(2))
+        wo_raw.append(load_wo(1))
+        wo_raw.append(load_wo(2))
+
+        v_s = held("v_s", [P, S], U8)
+        nc.vector.tensor_copy(v_s[:], tab_s[:].indirect(idx[:]))
+        v_w = []
+        for half in range(S // BANK):
+            words = held("v_w%d" % half, [P, BANK], U32)
+            cols = slice(half * BANK // 16, (half + 1) * BANK // 16)
+            nc.vector.tensor_copy(words[:], tab_w[:].indirect(idx[:, cols]))
+            v_w.append(words)
+
+        def reorder(name, src, g, bytes_per_col):
+            w = RUN * bytes_per_col // 4
+            dst = held("%s%d" % (name, g), [P, GROUP * bytes_per_col], U8)
+            words = src[:].bitcast(I32)
+            n = GROUP * bytes_per_col // 4
+            nc.vector.tensor_copy(
+                out=dst[:].bitcast(I32).rearrange("p (t c w) -> p t c w", t=PACK, w=w),
+                in_=words[:, g * n : (g + 1) * n].rearrange("p (c t w) -> p t c w", t=PACK, w=w),
+            )
+            return dst
+
+        def quantize(name, g, grouped):
+            codes = held("%s_codes%d" % (name, g), [P, GROUP], U32)
+            scales = held("%s_scales%d" % (name, g), [P, GROUP], U8)
+            nc.vector.quantize_mx(out=codes[:].bitcast(FP8X4), scales=scales[:], in_=grouped[:])
+            return codes, scales
+
+        def round_wv(copy, g):
+            grouped = turn("grouped", [P, PACK * GROUP], BF16, 3)
+            copy(
+                grouped[:].rearrange("p (t c i j) -> p t c j i", t=PACK, i=RUN, j=PACK),
+                wv_raw[g][:].rearrange("p j (c t i) -> p t c j i", t=PACK, i=RUN),
+            )
+            return grouped
+
+        def round_planes(copy, planes):
+            grouped = turn("grouped", [P, PACK * BANK], BF16, 3)
+            copy(
+                grouped[:].rearrange("p (c i t) -> p c t i", i=4, t=PACK),
+                planes[:].rearrange("p t (c i) -> p c t i", i=4),
+            )
+            return grouped
+
+        def product(lhs, lhs_s, rhs, rhs_s):
+            bank = psum.tile([P, BANK], F32, name="bank", bufs=4)
+            nc.tensor.matmul_mx(out=bank[:], lhsT=lhs, lhsT_scale=lhs_s, rhs=rhs, rhs_scale=rhs_s, start=True, stop=True)
+            return bank
+
+        def coarse(name, lhs, lhs_s, func):
+            window = turn(name, [P, S], F32, 5)
+            for half in range(S // BANK):
+                cols = slice(half * BANK, (half + 1) * BANK)
+                bank = product(lhs, lhs_s, v_w[half][:].bitcast(FP8X4), v_s[:, cols])
+                nc.scalar.activation(out=window[:, cols], in_=bank[:], func=func)
+            return window
+
+        def slopes(g):
+            words = reorder("ws_w", ws_w, g, 2)
+            scales = reorder("ws_s", ws_s, g, 1)
+            return [
+                coarse("d_abs", words[:, 2 * P * t : 2 * P * (t + 1)].bitcast(FP4X4), scales[:, P * t : P * (t + 1)], ACT.Abs)
+                for t in range(PACK)
+            ]
+
+        def values(g, codes, scales):
+            return [
+                coarse("h", codes[:, P * t : P * (t + 1)].bitcast(FP8X4), scales[:, P * t : P * (t + 1)], ACT.Copy)
+                for t in range(PACK)
+            ]
+
+        def fine(g, v2_w, v2_s):
+            words = reorder("wf_w", wf_w, g, 4)
+            scales = reorder("wf_s", wf_s, g, 1)
+            tiles = []
+            for t in range(PACK):
+                bank = product(
+                    words[:, 4 * P * t : 4 * P * (t + 1)].bitcast(FP8X4), scales[WF_ROW:P, P * t : P * (t + 1)],
+                    v2_w[:].bitcast(FP8X4), v2_s[TAB2_ROW:P, :],
+                )
+                b_abs = turn("b_abs", [P, M], F32, 5)
+                nc.scalar.activation(out=b_abs[:], in_=bank[:], func=ACT.Abs)
+                tiles.append(b_abs)
+            return tiles
+
+        acc = [psum.tile([P, M], F32, name="acc%d" % n) for n in range(N // P)]
+
+        d_abs = slopes(0)
+        wv_q = quantize("wv", 0, round_wv(nc.vector.tensor_copy, 0))
+        v2_s = held("v2_s", [P, M], U8)
+        nc.vector.tensor_copy(v2_s[:], tab2_s[:].indirect(idx2[:]))
+        v2_w = held("v2_w", [P, M], U32)
+        nc.vector.tensor_copy(v2_w[:], tab2_w[:].indirect(idx2[:]))
+
+        off_bank = psum.tile([P, GROUPS, P], F32, name="bank", bufs=4)
+        for g in range(GROUPS):
+            nc.tensor.transpose(off_bank[:, g, :], off_rows[:, g * P : (g + 1) * P], ident[:])
+        nc.scalar.copy(out=off_col[:], in_=off_bank[:, :, 0:PACK])
+
+        for g in range(GROUPS):
+            last = g == GROUPS - 1
+            b_abs = fine(g, v2_w, v2_s)
+            h = values(g, *wv_q)
+            z = turn("z", [P, PACK, M], F32, 2)
+            steps = []
+            for t in range(PACK):
+                picked = turn("picked", [P, M], F32, 4)
+                nc.vector.tensor_copy(picked[:], d_abs[t][:].indirect(p1[:]))
+                steps.append(picked)
+            for t in range(PACK):
+                nc.vector.tensor_tensor(steps[t][:], steps[t][:], b_abs[t][:], ALU.min)
+            for t in range(PACK):
+                nc.vector.tensor_scalar(steps[t][:], steps[t][:], off_col[:, g, t : t + 1], None, ALU.mult)
+            if not last:
+                wv_q = quantize("wv", g + 1, round_wv(nc.scalar.copy, g + 1))
+                d_abs = slopes(g + 1)
+            for t in range(PACK):
+                nc.vector.tensor_tensor(z[:, t, :], h[t][:].indirect(p1[:]), steps[t][:], ALU.add)
+            wo_codes, wo_scales = quantize("wo", g, round_planes(nc.scalar.copy, wo_raw[g]))
+            z_codes, z_scales = quantize("z", g, round_planes(nc.vector.tensor_copy if last else nc.scalar.copy, z))
+            for n in range(N // P):
+                cols = slice(n * P, (n + 1) * P)
+                nc.tensor.matmul_mx(
+                    out=acc[n][:], lhsT=wo_codes[:, cols].bitcast(FP8X4), lhsT_scale=wo_scales[:, cols],
+                    rhs=z_codes[:].bitcast(FP8X4), rhs_scale=z_scales[:], start=(g == 0), stop=last,
+                )
+
+        for n in range(N // P):
+            result = held("result%d" % n, [P, M], F32)
+            copy = nc.scalar.copy if n % 2 == 0 else nc.vector.tensor_copy
+            copy(result[:], acc[n][:])
+            nc.sync.dma_start(out=out[n * P : (n + 1) * P, :], in_=result[:])

@@ -23,6 +23,9 @@ RUN = 4
 GROUP = P * PACK
 GROUPS = H // GROUP
 BANK = 512
+BANKS = 8
+HALVES = 2
+HALF = M // HALVES
 TAB2_ROW = 4
 WF_ROW = 8
 
@@ -57,9 +60,9 @@ def tile_list_mesh_block_refinement_kernel(
         tab_s = held("tab_s", [P, T], U8)
         tab2_w = held("tab2_w", [P, T2], U32)
         tab2_s = held("tab2_s", [P, T2], U8)
-        ws_w = held("ws_w", [P, 2 * H], U8)
+        ws_w = [held("ws_raw%d" % g, [P, 2 * GROUP], U8) for g in range(GROUPS)]
         ws_s = held("ws_s", [P, H], U8)
-        wf_w = held("wf_w", [P, H], U32)
+        wf_w = [held("wf_raw%d" % g, [P, 4 * GROUP], U8) for g in range(GROUPS)]
         wf_s = held("wf_s", [P, H], U8)
         off_rows = held("off_rows", [P, GROUPS * P], F32)
         off_col = held("off_col", [P, GROUPS, PACK], F32)
@@ -71,23 +74,16 @@ def tile_list_mesh_block_refinement_kernel(
         nc.vector.memset(tab2_s[:].bitcast(I32), 0)
         nc.vector.memset(wf_s[:].bitcast(I32), 0)
 
-        nc.sync.dma_start(idx[:], offs)
-        nc.sync.dma_start(out=ws_w[:].bitcast(I32), in_=ws_words[0].bitcast(I32))
-        load_scales(nc.scalar, tab_s, tab_scales, 0)
-        nc.sync.dma_start(
-            out=tab_w[:].bitcast(I32),
-            in_=tab_words[0].rearrange("p t i -> p (t i)").bitcast(I32),
-        )
-        load_scales(nc.scalar, ws_s, ws_scales, 0)
-        nc.gpsimd.dma_start(
-            out=off_rows[0:PACK, :].rearrange("t (c i) -> t c i", i=RUN),
-            in_=off.rearrange("(c t i) -> t c i", t=PACK, i=RUN),
-        )
-        make_identity(nc, ident[:])
-        nc.sync.dma_start(p1[:], pos1)
+        tab_rows = tab_words[0].rearrange("p t i -> p (t i)").bitcast(I32)
+        ws_rows = ws_words[0].bitcast(I32)
+        wf_rows = wf_words[0].rearrange("p t i -> p (t i)").bitcast(I32)
+
+        def load_words(tiles, rows, g):
+            n = rows.shape[1] // GROUPS
+            nc.sync.dma_start(out=tiles[g][:].bitcast(I32), in_=rows[:, g * n : (g + 1) * n])
 
         def load_wv(g):
-            raw = turn("raw", [P, PACK, GROUP], F32, 5)
+            raw = turn("raw", [P, PACK, GROUP], F32, 3)
             nc.sync.dma_start(
                 out=raw[:],
                 in_=wv[:, g * GROUP : (g + 1) * GROUP].rearrange("(p j) r -> p j r", j=PACK),
@@ -95,30 +91,41 @@ def tile_list_mesh_block_refinement_kernel(
             return raw
 
         def load_wo(g):
-            raw = turn("raw", [P, PACK, N], F32, 5)
+            raw = turn("raw", [P, PACK, N], F32, 3)
             rows = wo[g * GROUP : (g + 1) * GROUP, :].rearrange("(c t i) n -> t c i n", t=PACK, i=RUN)
             for t in range(PACK):
                 nc.sync.dma_start(out=raw[:, t, :], in_=rows[t])
             return raw
 
+        nc.sync.dma_start(idx[:], offs)
+        nc.sync.dma_start(out=tab_w[:, : T // 2].bitcast(I32), in_=tab_rows[:, : T // 2])
+        load_scales(nc.sync, tab_s, tab_scales, 0)
+        load_words(ws_w, ws_rows, 0)
+        nc.sync.dma_start(out=tab_w[:, T // 2 :].bitcast(I32), in_=tab_rows[:, T // 2 :])
+        load_scales(nc.sync, ws_s, ws_scales, 0)
+        nc.gpsimd.dma_start(
+            out=off_rows[0:PACK, :].rearrange("t (c i) -> t c i", i=RUN),
+            in_=off.rearrange("(c t i) -> t c i", t=PACK, i=RUN),
+        )
+        make_identity(nc, ident[:])
+        nc.sync.dma_start(p1[:], pos1)
         wv_raw = [load_wv(0)]
         nc.sync.dma_start(idx2[:], offs2)
+        load_scales(nc.sync, tab2_s, tab2_scales, TAB2_ROW)
         nc.sync.dma_start(
             out=tab2_w[:].bitcast(I32),
             in_=tab2_words[0].rearrange("p t i -> p (t i)").bitcast(I32),
         )
-        load_scales(nc.sync, tab2_s, tab2_scales, TAB2_ROW)
-        nc.sync.dma_start(
-            out=wf_w[:].bitcast(I32),
-            in_=wf_words[0].rearrange("p t i -> p (t i)").bitcast(I32),
-        )
+        load_words(wf_w, wf_rows, 0)
         load_scales(nc.sync, wf_s, wf_scales, WF_ROW)
         wv_raw.append(load_wv(1))
+        for g in range(1, GROUPS):
+            load_words(ws_w, ws_rows, g)
+            load_words(wf_w, wf_rows, g)
         wo_raw = [load_wo(0)]
         wv_raw.append(load_wv(2))
         wo_raw.append(load_wo(1))
         wo_raw.append(load_wo(2))
-
         v_s = held("v_s", [P, S], U8)
         nc.vector.tensor_copy(v_s[:], tab_s[:].indirect(idx[:]))
         v_w = []
@@ -128,46 +135,51 @@ def tile_list_mesh_block_refinement_kernel(
             nc.vector.tensor_copy(words[:], tab_w[:].indirect(idx[:, cols]))
             v_w.append(words)
 
-        def reorder(name, src, g, bytes_per_col):
+        def reorder(name, src, bytes_per_col):
             w = RUN * bytes_per_col // 4
-            dst = held("%s%d" % (name, g), [P, GROUP * bytes_per_col], U8)
-            words = src[:].bitcast(I32)
-            n = GROUP * bytes_per_col // 4
+            dst = held(name, [P, GROUP * bytes_per_col], U8)
             nc.vector.tensor_copy(
                 out=dst[:].bitcast(I32).rearrange("p (t c w) -> p t c w", t=PACK, w=w),
-                in_=words[:, g * n : (g + 1) * n].rearrange("p (c t w) -> p t c w", t=PACK, w=w),
+                in_=src.bitcast(I32).rearrange("p (c t w) -> p t c w", t=PACK, w=w),
             )
             return dst
 
-        def quantize(name, g, grouped):
-            codes = held("%s_codes%d" % (name, g), [P, GROUP], U32)
-            scales = held("%s_scales%d" % (name, g), [P, GROUP], U8)
+        def quantize(name, grouped):
+            width = grouped.shape[1] // PACK
+            codes = held(name + "_codes", [P, width], U32)
+            scales = held(name + "_scales", [P, width], U8)
             nc.vector.quantize_mx(out=codes[:].bitcast(FP8X4), scales=scales[:], in_=grouped[:])
             return codes, scales
 
-        def round_wv(copy, g):
-            grouped = turn("grouped", [P, PACK * GROUP], BF16, 3)
-            copy(
+        def round_wv(g):
+            grouped = turn("w_bf16", [P, PACK * GROUP], BF16, 2)
+            nc.scalar.copy(
                 grouped[:].rearrange("p (t c i j) -> p t c j i", t=PACK, i=RUN, j=PACK),
                 wv_raw[g][:].rearrange("p j (c t i) -> p t c j i", t=PACK, i=RUN),
             )
             return grouped
 
-        def round_planes(copy, planes):
-            grouped = turn("grouped", [P, PACK * BANK], BF16, 3)
+        def round_planes(copy, name, planes):
+            grouped = turn(name, [P, PACK * planes.shape[2]], BF16, 2)
             copy(
                 grouped[:].rearrange("p (c i t) -> p c t i", i=4, t=PACK),
                 planes[:].rearrange("p t (c i) -> p c t i", i=4),
             )
             return grouped
 
+        used = []
+
+        def next_bank(shape):
+            used.append(len(used))
+            return psum.tile(shape, F32, name="bank%d" % (used[-1] % BANKS))
+
         def product(lhs, lhs_s, rhs, rhs_s):
-            bank = psum.tile([P, BANK], F32, name="bank", bufs=4)
+            bank = next_bank([P, BANK])
             nc.tensor.matmul_mx(out=bank[:], lhsT=lhs, lhsT_scale=lhs_s, rhs=rhs, rhs_scale=rhs_s, start=True, stop=True)
             return bank
 
-        def coarse(name, lhs, lhs_s, func):
-            window = turn(name, [P, S], F32, 5)
+        def coarse(name, bufs, lhs, lhs_s, func):
+            window = turn(name, [P, S], F32, bufs)
             for half in range(S // BANK):
                 cols = slice(half * BANK, (half + 1) * BANK)
                 bank = product(lhs, lhs_s, v_w[half][:].bitcast(FP8X4), v_s[:, cols])
@@ -175,77 +187,96 @@ def tile_list_mesh_block_refinement_kernel(
             return window
 
         def slopes(g):
-            words = reorder("ws_w", ws_w, g, 2)
-            scales = reorder("ws_s", ws_s, g, 1)
+            words = reorder("ws_w%d" % g, ws_w[g][:], 2)
+            scales = reorder("ws_s%d" % g, ws_s[:, g * GROUP : (g + 1) * GROUP], 1)
             return [
-                coarse("d_abs", words[:, 2 * P * t : 2 * P * (t + 1)].bitcast(FP4X4), scales[:, P * t : P * (t + 1)], ACT.Abs)
+                coarse("d_abs", 8, words[:, 2 * P * t : 2 * P * (t + 1)].bitcast(FP4X4), scales[:, P * t : P * (t + 1)], ACT.Abs)
                 for t in range(PACK)
             ]
 
-        def values(g, codes, scales):
+        def values(codes, scales):
             return [
-                coarse("h", codes[:, P * t : P * (t + 1)].bitcast(FP8X4), scales[:, P * t : P * (t + 1)], ACT.Copy)
+                coarse("h", 7, codes[:, P * t : P * (t + 1)].bitcast(FP8X4), scales[:, P * t : P * (t + 1)], ACT.Copy)
                 for t in range(PACK)
             ]
 
-        def fine(g, v2_w, v2_s):
-            words = reorder("wf_w", wf_w, g, 4)
-            scales = reorder("wf_s", wf_s, g, 1)
-            tiles = []
+        def fine(g):
+            words = reorder("wf_w%d" % g, wf_w[g][:], 4)
+            scales = reorder("wf_s%d" % g, wf_s[:, g * GROUP : (g + 1) * GROUP], 1)
+            b_abs = turn("b_abs", [P, PACK, M], F32, 2)
             for t in range(PACK):
                 bank = product(
                     words[:, 4 * P * t : 4 * P * (t + 1)].bitcast(FP8X4), scales[WF_ROW:P, P * t : P * (t + 1)],
                     v2_w[:].bitcast(FP8X4), v2_s[TAB2_ROW:P, :],
                 )
-                b_abs = turn("b_abs", [P, M], F32, 5)
-                nc.scalar.activation(out=b_abs[:], in_=bank[:], func=ACT.Abs)
-                tiles.append(b_abs)
-            return tiles
+                nc.scalar.activation(out=b_abs[:, t, :], in_=bank[:], func=ACT.Abs)
+            return b_abs
 
-        acc = [psum.tile([P, M], F32, name="acc%d" % n) for n in range(N // P)]
-
-        d_abs = slopes(0)
-        wv_q = quantize("wv", 0, round_wv(nc.vector.tensor_copy, 0))
-        v2_s = held("v2_s", [P, M], U8)
-        nc.vector.tensor_copy(v2_s[:], tab2_s[:].indirect(idx2[:]))
-        v2_w = held("v2_w", [P, M], U32)
-        nc.vector.tensor_copy(v2_w[:], tab2_w[:].indirect(idx2[:]))
-
-        off_bank = psum.tile([P, GROUPS, P], F32, name="bank", bufs=4)
+        off_bank = next_bank([P, GROUPS, P])
         for g in range(GROUPS):
             nc.tensor.transpose(off_bank[:, g, :], off_rows[:, g * P : (g + 1) * P], ident[:])
         nc.scalar.copy(out=off_col[:], in_=off_bank[:, :, 0:PACK])
 
+        d_abs = slopes(0)
+        v2_s = held("v2_s", [P, M], U8)
+        nc.vector.tensor_copy(v2_s[:], tab2_s[:].indirect(idx2[:]))
+        v2_w = held("v2_w", [P, M], U32)
+        nc.vector.tensor_copy(v2_w[:], tab2_w[:].indirect(idx2[:]))
+        wv_q = quantize("wv0", round_wv(0))
+
+        wo_q, z_q = [], []
         for g in range(GROUPS):
             last = g == GROUPS - 1
-            b_abs = fine(g, v2_w, v2_s)
-            h = values(g, *wv_q)
-            z = turn("z", [P, PACK, M], F32, 2)
-            steps = []
+            b_abs = fine(g)
+            h = values(*wv_q)
+            step = turn("step", [P, PACK, M], F32, 1)
             for t in range(PACK):
-                picked = turn("picked", [P, M], F32, 4)
-                nc.vector.tensor_copy(picked[:], d_abs[t][:].indirect(p1[:]))
-                steps.append(picked)
+                nc.vector.tensor_copy(step[:, t, :], d_abs[t][:].indirect(p1[:]))
+            nc.vector.tensor_tensor(step[:], step[:], b_abs[:], ALU.min)
             for t in range(PACK):
-                nc.vector.tensor_tensor(steps[t][:], steps[t][:], b_abs[t][:], ALU.min)
-            for t in range(PACK):
-                nc.vector.tensor_scalar(steps[t][:], steps[t][:], off_col[:, g, t : t + 1], None, ALU.mult)
+                nc.vector.tensor_scalar(step[:, t, :], step[:, t, :], off_col[:, g, t : t + 1], None, ALU.mult)
             if not last:
-                wv_q = quantize("wv", g + 1, round_wv(nc.scalar.copy, g + 1))
+                wv_q = quantize("wv%d" % (g + 1), round_wv(g + 1))
                 d_abs = slopes(g + 1)
-            for t in range(PACK):
-                nc.vector.tensor_tensor(z[:, t, :], h[t][:].indirect(p1[:]), steps[t][:], ALU.add)
-            wo_codes, wo_scales = quantize("wo", g, round_planes(nc.scalar.copy, wo_raw[g]))
-            z_codes, z_scales = quantize("z", g, round_planes(nc.vector.tensor_copy if last else nc.scalar.copy, z))
-            for n in range(N // P):
-                cols = slice(n * P, (n + 1) * P)
-                nc.tensor.matmul_mx(
-                    out=acc[n][:], lhsT=wo_codes[:, cols].bitcast(FP8X4), lhsT_scale=wo_scales[:, cols],
-                    rhs=z_codes[:].bitcast(FP8X4), rhs_scale=z_scales[:], start=(g == 0), stop=last,
-                )
+            parts = HALVES if last else 1
+            width = M // parts
+            z = []
+            for part in range(parts):
+                planes = turn("z", [P, PACK, width], F32, 2)
+                offsets = p1[:, part * width // 16 : (part + 1) * width // 16]
+                for t in range(PACK):
+                    nc.vector.tensor_tensor(
+                        planes[:, t, :], h[t][:].indirect(offsets), step[:, t, part * width : (part + 1) * width], ALU.add
+                    )
+                z.append(planes)
+            wo_q.append(quantize("wo%d" % g, round_planes(nc.scalar.copy, "w_bf16", wo_raw[g])))
+            rounded = [round_planes(nc.vector.tensor_copy, "z_bf16", planes) for planes in z]
+            packed = [quantize("z%d_%d" % (g, part), rounded[part]) for part in range(parts)]
+            if last:
+                z_q.append([(codes[:], scales[:]) for codes, scales in packed])
+            else:
+                codes, scales = packed[0]
+                z_q.append([
+                    (codes[:, half * HALF : (half + 1) * HALF], scales[:, half * HALF : (half + 1) * HALF])
+                    for half in range(HALVES)
+                ])
 
-        for n in range(N // P):
-            result = held("result%d" % n, [P, M], F32)
-            copy = nc.scalar.copy if n % 2 == 0 else nc.vector.tensor_copy
-            copy(result[:], acc[n][:])
-            nc.sync.dma_start(out=out[n * P : (n + 1) * P, :], in_=result[:])
+        acc = [[next_bank([P, HALF]) for n in range(N // P)] for half in range(HALVES)]
+        for g in range(GROUPS):
+            wo_codes, wo_scales = wo_q[g]
+            for half in range(HALVES):
+                z_codes, z_scales = z_q[g][half]
+                for n in range(N // P):
+                    cols = slice(n * P, (n + 1) * P)
+                    nc.tensor.matmul_mx(
+                        out=acc[half][n][:], lhsT=wo_codes[:, cols].bitcast(FP8X4), lhsT_scale=wo_scales[:, cols],
+                        rhs=z_codes.bitcast(FP8X4), rhs_scale=z_scales, start=(g == 0), stop=(g == GROUPS - 1),
+                    )
+
+        for half in range(HALVES):
+            for pair, copy in enumerate((nc.scalar.copy, nc.vector.tensor_copy)):
+                result = held("result%d_%d" % (half, pair), [P, 2, HALF], F32)
+                for n in range(2):
+                    copy(result[:, n, :], acc[half][2 * pair + n][:])
+                rows = out[2 * pair * P : 2 * (pair + 1) * P, half * HALF : (half + 1) * HALF]
+                nc.sync.dma_start(out=rows.rearrange("(n p) m -> p n m", p=P), in_=result[:])

@@ -25,6 +25,8 @@ GROUPS = H // GROUP
 BANK = 512
 BANKS = 8
 HALVES = 2
+SPANS = ((0, 1), (1, GROUPS - 1))
+TAB_FIRST = T // 4
 HALF = M // HALVES
 TAB2_ROW = 4
 WF_ROW = 8
@@ -47,10 +49,10 @@ def tile_list_mesh_block_refinement_kernel(
             return ring.tile(shape, dtype, name=name, bufs=bufs, align_bytes=64)
 
         def load_scales(queue, plane, scales, row):
-            for q in range(4):
+            for r in range(4):
                 queue.dma_start(
-                    out=plane[32 * q + row : 32 * q + row + 4, :].bitcast(I32),
-                    in_=scales[0, 4 * q : 4 * q + 4, :].bitcast(I32),
+                    out=plane[row + r : P : 32, :].bitcast(I32),
+                    in_=scales[0, r : 16 : 4, :].bitcast(I32),
                 )
 
         idx = held("idx", [P, S // 16], U16)
@@ -60,27 +62,28 @@ def tile_list_mesh_block_refinement_kernel(
         tab_s = held("tab_s", [P, T], U8)
         tab2_w = held("tab2_w", [P, T2], U32)
         tab2_s = held("tab2_s", [P, T2], U8)
-        ws_w = [held("ws_raw%d" % g, [P, 2 * GROUP], U8) for g in range(GROUPS)]
+        ws_w = [held("ws_raw%d" % first, [P, 2 * GROUP * count], U8) for first, count in SPANS]
         ws_s = held("ws_s", [P, H], U8)
-        wf_w = [held("wf_raw%d" % g, [P, 4 * GROUP], U8) for g in range(GROUPS)]
+        wf_w = [held("wf_raw%d" % first, [P, 4 * GROUP * count], U8) for first, count in SPANS]
         wf_s = held("wf_s", [P, H], U8)
         off_rows = held("off_rows", [P, GROUPS * P], F32)
         off_col = held("off_col", [P, GROUPS, PACK], F32)
         ident = held("ident", [P, P], F32)
 
         nc.vector.memset(tab_s[:].bitcast(I32), 0)
-        nc.gpsimd.memset(ws_s[:].bitcast(I32), 0)
+        nc.gpsimd.memset(tab2_s[:].bitcast(I32), 0)
+        nc.vector.memset(ws_s[:].bitcast(I32), 0)
         nc.gpsimd.memset(off_rows[:], 0.0)
-        nc.vector.memset(tab2_s[:].bitcast(I32), 0)
         nc.vector.memset(wf_s[:].bitcast(I32), 0)
 
         tab_rows = tab_words[0].rearrange("p t i -> p (t i)").bitcast(I32)
         ws_rows = ws_words[0].bitcast(I32)
         wf_rows = wf_words[0].rearrange("p t i -> p (t i)").bitcast(I32)
 
-        def load_words(tiles, rows, g):
+        def load_words(tiles, rows, span):
+            first, count = SPANS[span]
             n = rows.shape[1] // GROUPS
-            nc.sync.dma_start(out=tiles[g][:].bitcast(I32), in_=rows[:, g * n : (g + 1) * n])
+            nc.sync.dma_start(out=tiles[span][:].bitcast(I32), in_=rows[:, first * n : (first + count) * n])
 
         def load_wv(g):
             raw = turn("raw", [P, PACK, GROUP], F32, 3)
@@ -98,10 +101,10 @@ def tile_list_mesh_block_refinement_kernel(
             return raw
 
         nc.sync.dma_start(idx[:], offs)
-        nc.sync.dma_start(out=tab_w[:, : T // 2].bitcast(I32), in_=tab_rows[:, : T // 2])
+        nc.sync.dma_start(out=tab_w[:, :TAB_FIRST].bitcast(I32), in_=tab_rows[:, :TAB_FIRST])
         load_scales(nc.sync, tab_s, tab_scales, 0)
         load_words(ws_w, ws_rows, 0)
-        nc.sync.dma_start(out=tab_w[:, T // 2 :].bitcast(I32), in_=tab_rows[:, T // 2 :])
+        nc.sync.dma_start(out=tab_w[:, TAB_FIRST:].bitcast(I32), in_=tab_rows[:, TAB_FIRST:])
         load_scales(nc.sync, ws_s, ws_scales, 0)
         nc.gpsimd.dma_start(
             out=off_rows[0:PACK, :].rearrange("t (c i) -> t c i", i=RUN),
@@ -119,9 +122,8 @@ def tile_list_mesh_block_refinement_kernel(
         load_words(wf_w, wf_rows, 0)
         load_scales(nc.sync, wf_s, wf_scales, WF_ROW)
         wv_raw.append(load_wv(1))
-        for g in range(1, GROUPS):
-            load_words(ws_w, ws_rows, g)
-            load_words(wf_w, wf_rows, g)
+        load_words(ws_w, ws_rows, 1)
+        load_words(wf_w, wf_rows, 1)
         wo_raw = [load_wo(0)]
         wv_raw.append(load_wv(2))
         wo_raw.append(load_wo(1))
@@ -144,6 +146,10 @@ def tile_list_mesh_block_refinement_kernel(
             )
             return dst
 
+        def group_of(tiles, g, bytes_per_col):
+            n = GROUP * bytes_per_col
+            return tiles[0][:] if g == 0 else tiles[1][:, (g - 1) * n : g * n]
+
         def quantize(name, grouped):
             width = grouped.shape[1] // PACK
             codes = held(name + "_codes", [P, width], U32)
@@ -152,7 +158,7 @@ def tile_list_mesh_block_refinement_kernel(
             return codes, scales
 
         def round_wv(g):
-            grouped = turn("w_bf16", [P, PACK * GROUP], BF16, 2)
+            grouped = turn("w_bf16", [P, PACK * GROUP], BF16, 4)
             nc.scalar.copy(
                 grouped[:].rearrange("p (t c i j) -> p t c j i", t=PACK, i=RUN, j=PACK),
                 wv_raw[g][:].rearrange("p j (c t i) -> p t c j i", t=PACK, i=RUN),
@@ -160,7 +166,7 @@ def tile_list_mesh_block_refinement_kernel(
             return grouped
 
         def round_planes(copy, name, planes):
-            grouped = turn(name, [P, PACK * planes.shape[2]], BF16, 2)
+            grouped = turn(name, [P, PACK * planes.shape[2]], BF16, 4 if name == "w_bf16" else 2)
             copy(
                 grouped[:].rearrange("p (c i t) -> p c t i", i=4, t=PACK),
                 planes[:].rearrange("p t (c i) -> p c t i", i=4),
@@ -187,21 +193,21 @@ def tile_list_mesh_block_refinement_kernel(
             return window
 
         def slopes(g):
-            words = reorder("ws_w%d" % g, ws_w[g][:], 2)
+            words = reorder("ws_w%d" % g, group_of(ws_w, g, 2), 2)
             scales = reorder("ws_s%d" % g, ws_s[:, g * GROUP : (g + 1) * GROUP], 1)
             return [
-                coarse("d_abs", 8, words[:, 2 * P * t : 2 * P * (t + 1)].bitcast(FP4X4), scales[:, P * t : P * (t + 1)], ACT.Abs)
+                coarse("d_abs", 7, words[:, 2 * P * t : 2 * P * (t + 1)].bitcast(FP4X4), scales[:, P * t : P * (t + 1)], ACT.Abs)
                 for t in range(PACK)
             ]
 
         def values(codes, scales):
             return [
-                coarse("h", 7, codes[:, P * t : P * (t + 1)].bitcast(FP8X4), scales[:, P * t : P * (t + 1)], ACT.Copy)
+                coarse("h", 6, codes[:, P * t : P * (t + 1)].bitcast(FP8X4), scales[:, P * t : P * (t + 1)], ACT.Copy)
                 for t in range(PACK)
             ]
 
         def fine(g):
-            words = reorder("wf_w%d" % g, wf_w[g][:], 4)
+            words = reorder("wf_w%d" % g, group_of(wf_w, g, 4), 4)
             scales = reorder("wf_s%d" % g, wf_s[:, g * GROUP : (g + 1) * GROUP], 1)
             b_abs = turn("b_abs", [P, PACK, M], F32, 2)
             for t in range(PACK):
@@ -224,20 +230,31 @@ def tile_list_mesh_block_refinement_kernel(
         nc.vector.tensor_copy(v2_w[:], tab2_w[:].indirect(idx2[:]))
         wv_q = quantize("wv0", round_wv(0))
 
+        def pack_wo(g):
+            return quantize("wo%d" % g, round_planes(nc.scalar.copy, "w_bf16", wo_raw[g]))
+
+        def halves(codes, scales):
+            return [
+                (codes[:, half * HALF : (half + 1) * HALF], scales[:, half * HALF : (half + 1) * HALF])
+                for half in range(HALVES)
+            ]
+
         wo_q, z_q = [], []
         for g in range(GROUPS):
             last = g == GROUPS - 1
             b_abs = fine(g)
-            h = values(*wv_q)
             step = turn("step", [P, PACK, M], F32, 1)
             for t in range(PACK):
                 nc.vector.tensor_copy(step[:, t, :], d_abs[t][:].indirect(p1[:]))
             nc.vector.tensor_tensor(step[:], step[:], b_abs[:], ALU.min)
+            wv_now = wv_q
+            if last:
+                wo_q.append(pack_wo(g))
+            else:
+                wv_q = quantize("wv%d" % (g + 1), round_wv(g + 1))
+            h = values(*wv_now)
             for t in range(PACK):
                 nc.vector.tensor_scalar(step[:, t, :], step[:, t, :], off_col[:, g, t : t + 1], None, ALU.mult)
-            if not last:
-                wv_q = quantize("wv%d" % (g + 1), round_wv(g + 1))
-                d_abs = slopes(g + 1)
             parts = HALVES if last else 1
             width = M // parts
             z = []
@@ -249,17 +266,20 @@ def tile_list_mesh_block_refinement_kernel(
                         planes[:, t, :], h[t][:].indirect(offsets), step[:, t, part * width : (part + 1) * width], ALU.add
                     )
                 z.append(planes)
-            wo_q.append(quantize("wo%d" % g, round_planes(nc.scalar.copy, "w_bf16", wo_raw[g])))
-            rounded = [round_planes(nc.vector.tensor_copy, "z_bf16", planes) for planes in z]
-            packed = [quantize("z%d_%d" % (g, part), rounded[part]) for part in range(parts)]
             if last:
+                rounded = [
+                    round_planes(nc.scalar.copy, "w_bf16", z[0]),
+                    round_planes(nc.vector.tensor_copy, "z_bf16", z[1]),
+                ]
+                packed = [quantize("z%d_%d" % (g, part), rounded[part]) for part in range(parts)]
                 z_q.append([(codes[:], scales[:]) for codes, scales in packed])
             else:
-                codes, scales = packed[0]
-                z_q.append([
-                    (codes[:, half * HALF : (half + 1) * HALF], scales[:, half * HALF : (half + 1) * HALF])
-                    for half in range(HALVES)
-                ])
+                if g == 0:
+                    z_q.append(halves(*quantize("z%d" % g, round_planes(nc.vector.tensor_copy, "z_bf16", z[0]))))
+                d_abs = slopes(g + 1)
+                wo_q.append(pack_wo(g))
+                if g > 0:
+                    z_q.append(halves(*quantize("z%d" % g, round_planes(nc.scalar.copy, "w_bf16", z[0]))))
 
         acc = [[next_bank([P, HALF]) for n in range(N // P)] for half in range(HALVES)]
         for g in range(GROUPS):

@@ -27,6 +27,7 @@ BANKS = 8
 HALVES = 2
 SPANS = ((0, 1), (1, GROUPS - 1))
 TAB_FIRST = T // 4
+TAB_LAST = T - T // 4
 HALF = M // HALVES
 TAB2_ROW = 4
 WF_ROW = 8
@@ -66,14 +67,15 @@ def tile_list_mesh_block_refinement_kernel(
         ws_s = held("ws_s", [P, H], U8)
         wf_w = [held("wf_raw%d" % first, [P, 4 * GROUP * count], U8) for first, count in SPANS]
         wf_s = held("wf_s", [P, H], U8)
-        off_rows = held("off_rows", [P, GROUPS * P], F32)
-        off_col = held("off_col", [P, GROUPS, PACK], F32)
+        off_rows = held("off_rows", [P, GROUP], F32)
+        off_slots = held("off_slots", [P, GROUP], F32)
+        off_col = held("off_col", [P, PACK, GROUPS], F32)
         ident = held("ident", [P, P], F32)
 
         nc.vector.memset(tab_s[:].bitcast(I32), 0)
-        nc.gpsimd.memset(tab2_s[:].bitcast(I32), 0)
-        nc.vector.memset(ws_s[:].bitcast(I32), 0)
         nc.gpsimd.memset(off_rows[:], 0.0)
+        nc.vector.memset(ws_s[:].bitcast(I32), 0)
+        nc.gpsimd.memset(tab2_s[:].bitcast(I32), 0)
         nc.vector.memset(wf_s[:].bitcast(I32), 0)
 
         tab_rows = tab_words[0].rearrange("p t i -> p (t i)").bitcast(I32)
@@ -103,13 +105,11 @@ def tile_list_mesh_block_refinement_kernel(
         nc.sync.dma_start(idx[:], offs)
         nc.sync.dma_start(out=tab_w[:, :TAB_FIRST].bitcast(I32), in_=tab_rows[:, :TAB_FIRST])
         load_scales(nc.sync, tab_s, tab_scales, 0)
-        load_words(ws_w, ws_rows, 0)
-        nc.sync.dma_start(out=tab_w[:, TAB_FIRST:].bitcast(I32), in_=tab_rows[:, TAB_FIRST:])
+        nc.sync.dma_start(out=tab_w[:, TAB_FIRST:TAB_LAST].bitcast(I32), in_=tab_rows[:, TAB_FIRST:TAB_LAST])
         load_scales(nc.sync, ws_s, ws_scales, 0)
-        nc.gpsimd.dma_start(
-            out=off_rows[0:PACK, :].rearrange("t (c i) -> t c i", i=RUN),
-            in_=off.rearrange("(c t i) -> t c i", t=PACK, i=RUN),
-        )
+        load_words(ws_w, ws_rows, 0)
+        nc.sync.dma_start(out=tab_w[:, TAB_LAST:].bitcast(I32), in_=tab_rows[:, TAB_LAST:])
+        nc.scalar.dma_start(out=off_rows[0:GROUPS, :], in_=off.rearrange("(g r) -> g r", g=GROUPS))
         make_identity(nc, ident[:])
         nc.sync.dma_start(p1[:], pos1)
         wv_raw = [load_wv(0)]
@@ -128,15 +128,6 @@ def tile_list_mesh_block_refinement_kernel(
         wv_raw.append(load_wv(2))
         wo_raw.append(load_wo(1))
         wo_raw.append(load_wo(2))
-        v_s = held("v_s", [P, S], U8)
-        nc.vector.tensor_copy(v_s[:], tab_s[:].indirect(idx[:]))
-        v_w = []
-        for half in range(S // BANK):
-            words = held("v_w%d" % half, [P, BANK], U32)
-            cols = slice(half * BANK // 16, (half + 1) * BANK // 16)
-            nc.vector.tensor_copy(words[:], tab_w[:].indirect(idx[:, cols]))
-            v_w.append(words)
-
         def reorder(name, src, bytes_per_col):
             w = RUN * bytes_per_col // 4
             dst = held(name, [P, GROUP * bytes_per_col], U8)
@@ -149,6 +140,20 @@ def tile_list_mesh_block_refinement_kernel(
         def group_of(tiles, g, bytes_per_col):
             n = GROUP * bytes_per_col
             return tiles[0][:] if g == 0 else tiles[1][:, (g - 1) * n : g * n]
+
+        def reorder_ws(g):
+            words = reorder("ws_w%d" % g, group_of(ws_w, g, 2), 2)
+            return words, reorder("ws_s%d" % g, ws_s[:, g * GROUP : (g + 1) * GROUP], 1)
+
+        v_s = held("v_s", [P, S], U8)
+        nc.vector.tensor_copy(v_s[:], tab_s[:].indirect(idx[:]))
+        ws_first = reorder_ws(0)
+        v_w = []
+        for half in range(S // BANK):
+            words = held("v_w%d" % half, [P, BANK], U32)
+            cols = slice(half * BANK // 16, (half + 1) * BANK // 16)
+            nc.vector.tensor_copy(words[:], tab_w[:].indirect(idx[:, cols]))
+            v_w.append(words)
 
         def quantize(name, grouped):
             width = grouped.shape[1] // PACK
@@ -192,9 +197,7 @@ def tile_list_mesh_block_refinement_kernel(
                 nc.scalar.activation(out=window[:, cols], in_=bank[:], func=func)
             return window
 
-        def slopes(g):
-            words = reorder("ws_w%d" % g, group_of(ws_w, g, 2), 2)
-            scales = reorder("ws_s%d" % g, ws_s[:, g * GROUP : (g + 1) * GROUP], 1)
+        def slopes(words, scales):
             return [
                 coarse("d_abs", 7, words[:, 2 * P * t : 2 * P * (t + 1)].bitcast(FP4X4), scales[:, P * t : P * (t + 1)], ACT.Abs)
                 for t in range(PACK)
@@ -218,12 +221,16 @@ def tile_list_mesh_block_refinement_kernel(
                 nc.scalar.activation(out=b_abs[:, t, :], in_=bank[:], func=ACT.Abs)
             return b_abs
 
-        off_bank = next_bank([P, GROUPS, P])
-        for g in range(GROUPS):
-            nc.tensor.transpose(off_bank[:, g, :], off_rows[:, g * P : (g + 1) * P], ident[:])
-        nc.scalar.copy(out=off_col[:], in_=off_bank[:, :, 0:PACK])
+        nc.scalar.copy(
+            off_slots[:].rearrange("p (t c i) -> p t c i", t=PACK, i=RUN),
+            off_rows[:].rearrange("p (c t i) -> p t c i", t=PACK, i=RUN),
+        )
+        off_bank = next_bank([P, PACK, P])
+        for t in range(PACK):
+            nc.tensor.transpose(off_bank[:, t, :], off_slots[:, t * P : (t + 1) * P], ident[:])
+        nc.scalar.copy(out=off_col[:], in_=off_bank[:, :, 0:GROUPS])
 
-        d_abs = slopes(0)
+        d_abs = slopes(*ws_first)
         v2_s = held("v2_s", [P, M], U8)
         nc.vector.tensor_copy(v2_s[:], tab2_s[:].indirect(idx2[:]))
         v2_w = held("v2_w", [P, M], U32)
@@ -254,7 +261,7 @@ def tile_list_mesh_block_refinement_kernel(
                 wv_q = quantize("wv%d" % (g + 1), round_wv(g + 1))
             h = values(*wv_now)
             for t in range(PACK):
-                nc.vector.tensor_scalar(step[:, t, :], step[:, t, :], off_col[:, g, t : t + 1], None, ALU.mult)
+                nc.vector.tensor_scalar(step[:, t, :], step[:, t, :], off_col[:, t, g : g + 1], None, ALU.mult)
             parts = HALVES if last else 1
             width = M // parts
             z = []
@@ -274,12 +281,9 @@ def tile_list_mesh_block_refinement_kernel(
                 packed = [quantize("z%d_%d" % (g, part), rounded[part]) for part in range(parts)]
                 z_q.append([(codes[:], scales[:]) for codes, scales in packed])
             else:
-                if g == 0:
-                    z_q.append(halves(*quantize("z%d" % g, round_planes(nc.vector.tensor_copy, "z_bf16", z[0]))))
-                d_abs = slopes(g + 1)
+                z_q.append(halves(*quantize("z%d" % g, round_planes(nc.vector.tensor_copy, "z_bf16", z[0]))))
+                d_abs = slopes(*reorder_ws(g + 1))
                 wo_q.append(pack_wo(g))
-                if g > 0:
-                    z_q.append(halves(*quantize("z%d" % g, round_planes(nc.scalar.copy, "w_bf16", z[0]))))
 
         acc = [[next_bank([P, HALF]) for n in range(N // P)] for half in range(HALVES)]
         for g in range(GROUPS):

@@ -31,6 +31,7 @@ TAB_LAST = T - T // 4
 HALF = M // HALVES
 TAB2_ROW = 4
 WF_ROW = 8
+EARLY = PACK // 2
 
 
 def tile_list_mesh_block_refinement_kernel(
@@ -49,9 +50,9 @@ def tile_list_mesh_block_refinement_kernel(
         def turn(name, shape, dtype, bufs):
             return ring.tile(shape, dtype, name=name, bufs=bufs, align_bytes=64)
 
-        def load_scales(queue, plane, scales, row):
+        def load_scales(plane, scales, row):
             for r in range(4):
-                queue.dma_start(
+                nc.sync.dma_start(
                     out=plane[row + r : P : 32, :].bitcast(I32),
                     in_=scales[0, r : 16 : 4, :].bitcast(I32),
                 )
@@ -63,9 +64,9 @@ def tile_list_mesh_block_refinement_kernel(
         tab_s = held("tab_s", [P, T], U8)
         tab2_w = held("tab2_w", [P, T2], U32)
         tab2_s = held("tab2_s", [P, T2], U8)
-        ws_w = [held("ws_raw%d" % first, [P, 2 * GROUP * count], U8) for first, count in SPANS]
+        ws_raw = [held("ws_raw%d" % first, [P, 2 * GROUP * count], U8) for first, count in SPANS]
         ws_s = held("ws_s", [P, H], U8)
-        wf_w = [held("wf_raw%d" % first, [P, 4 * GROUP * count], U8) for first, count in SPANS]
+        wf_raw = [held("wf_raw%d" % first, [P, 4 * GROUP * count], U8) for first, count in SPANS]
         wf_s = held("wf_s", [P, H], U8)
         off_rows = held("off_rows", [P, GROUP], F32)
         off_slots = held("off_slots", [P, GROUP], F32)
@@ -88,7 +89,7 @@ def tile_list_mesh_block_refinement_kernel(
             nc.sync.dma_start(out=tiles[span][:].bitcast(I32), in_=rows[:, first * n : (first + count) * n])
 
         def load_wv(g):
-            raw = turn("raw", [P, PACK, GROUP], F32, 3)
+            raw = turn("raw", [P, PACK, GROUP], F32, 4)
             nc.sync.dma_start(
                 out=raw[:],
                 in_=wv[:, g * GROUP : (g + 1) * GROUP].rearrange("(p j) r -> p j r", j=PACK),
@@ -96,7 +97,7 @@ def tile_list_mesh_block_refinement_kernel(
             return raw
 
         def load_wo(g):
-            raw = turn("raw", [P, PACK, N], F32, 3)
+            raw = turn("raw", [P, PACK, N], F32, 4)
             rows = wo[g * GROUP : (g + 1) * GROUP, :].rearrange("(c t i) n -> t c i n", t=PACK, i=RUN)
             for t in range(PACK):
                 nc.sync.dma_start(out=raw[:, t, :], in_=rows[t])
@@ -104,50 +105,53 @@ def tile_list_mesh_block_refinement_kernel(
 
         nc.sync.dma_start(idx[:], offs)
         nc.sync.dma_start(out=tab_w[:, :TAB_FIRST].bitcast(I32), in_=tab_rows[:, :TAB_FIRST])
-        load_scales(nc.sync, tab_s, tab_scales, 0)
+        load_scales(tab_s, tab_scales, 0)
+        load_words(ws_raw, ws_rows, 0)
         nc.sync.dma_start(out=tab_w[:, TAB_FIRST:TAB_LAST].bitcast(I32), in_=tab_rows[:, TAB_FIRST:TAB_LAST])
-        load_scales(nc.sync, ws_s, ws_scales, 0)
-        load_words(ws_w, ws_rows, 0)
+        load_scales(ws_s, ws_scales, 0)
         nc.sync.dma_start(out=tab_w[:, TAB_LAST:].bitcast(I32), in_=tab_rows[:, TAB_LAST:])
         nc.scalar.dma_start(out=off_rows[0:GROUPS, :], in_=off.rearrange("(g r) -> g r", g=GROUPS))
         make_identity(nc, ident[:])
-        nc.sync.dma_start(p1[:], pos1)
-        wv_raw = [load_wv(0)]
-        nc.sync.dma_start(idx2[:], offs2)
-        load_scales(nc.sync, tab2_s, tab2_scales, TAB2_ROW)
         nc.sync.dma_start(
             out=tab2_w[:].bitcast(I32),
             in_=tab2_words[0].rearrange("p t i -> p (t i)").bitcast(I32),
         )
-        load_words(wf_w, wf_rows, 0)
-        load_scales(nc.sync, wf_s, wf_scales, WF_ROW)
+        nc.sync.dma_start(idx2[:], offs2)
+        nc.sync.dma_start(p1[:], pos1)
+        load_scales(tab2_s, tab2_scales, TAB2_ROW)
+        load_words(wf_raw, wf_rows, 0)
+        load_scales(wf_s, wf_scales, WF_ROW)
+        wv_raw = [load_wv(0)]
+        load_words(ws_raw, ws_rows, 1)
         wv_raw.append(load_wv(1))
-        load_words(ws_w, ws_rows, 1)
-        load_words(wf_w, wf_rows, 1)
-        wo_raw = [load_wo(0)]
+        load_words(wf_raw, wf_rows, 1)
         wv_raw.append(load_wv(2))
-        wo_raw.append(load_wo(1))
-        wo_raw.append(load_wo(2))
-        def reorder(name, src, bytes_per_col):
+        wo_raw = [load_wo(0)]
+
+        def reorder(name, src, span, bytes_per_col):
+            count = SPANS[span][1]
             w = RUN * bytes_per_col // 4
-            dst = held(name, [P, GROUP * bytes_per_col], U8)
+            dst = held("%s%d" % (name, span), [P, count * GROUP * bytes_per_col], U8)
             nc.vector.tensor_copy(
-                out=dst[:].bitcast(I32).rearrange("p (t c w) -> p t c w", t=PACK, w=w),
-                in_=src.bitcast(I32).rearrange("p (c t w) -> p t c w", t=PACK, w=w),
+                out=dst[:].bitcast(I32).rearrange("p (g t c w) -> p g t c w", g=count, t=PACK, w=w),
+                in_=src.bitcast(I32).rearrange("p (g c t w) -> p g t c w", g=count, t=PACK, w=w),
             )
             return dst
 
-        def group_of(tiles, g, bytes_per_col):
-            n = GROUP * bytes_per_col
-            return tiles[0][:] if g == 0 else tiles[1][:, (g - 1) * n : g * n]
+        def reorder_weight(name, raw, plane, span, bytes_per_col):
+            first, count = SPANS[span]
+            words = reorder(name + "_words", raw[span][:], span, bytes_per_col)
+            scales = reorder(name + "_scales", plane[:, first * GROUP : (first + count) * GROUP], span, 1)
+            return words, scales
 
-        def reorder_ws(g):
-            words = reorder("ws_w%d" % g, group_of(ws_w, g, 2), 2)
-            return words, reorder("ws_s%d" % g, ws_s[:, g * GROUP : (g + 1) * GROUP], 1)
+        def slot(ordered, g, t, bytes_per_col):
+            words, scales = ordered[min(g, 1)]
+            c = (g - SPANS[min(g, 1)][0]) * GROUP + t * P
+            return words[:, bytes_per_col * c : bytes_per_col * (c + P)], scales[:, c : c + P]
 
         v_s = held("v_s", [P, S], U8)
         nc.vector.tensor_copy(v_s[:], tab_s[:].indirect(idx[:]))
-        ws_first = reorder_ws(0)
+        ws_ordered = [reorder_weight("ws", ws_raw, ws_s, 0, 2)]
         v_w = []
         for half in range(S // BANK):
             words = held("v_w%d" % half, [P, BANK], U32)
@@ -162,21 +166,24 @@ def tile_list_mesh_block_refinement_kernel(
             nc.vector.quantize_mx(out=codes[:].bitcast(FP8X4), scales=scales[:], in_=grouped[:])
             return codes, scales
 
-        def round_wv(g):
-            grouped = turn("w_bf16", [P, PACK * GROUP], BF16, 4)
+        def pack_wv(g):
+            grouped = turn("w_bf16", [P, PACK * GROUP], BF16, 3)
             nc.scalar.copy(
                 grouped[:].rearrange("p (t c i j) -> p t c j i", t=PACK, i=RUN, j=PACK),
                 wv_raw[g][:].rearrange("p j (c t i) -> p t c j i", t=PACK, i=RUN),
             )
-            return grouped
+            return quantize("wv%d" % g, grouped)
 
-        def round_planes(copy, name, planes):
-            grouped = turn(name, [P, PACK * planes.shape[2]], BF16, 4 if name == "w_bf16" else 2)
+        def round_planes(copy, grouped, planes):
             copy(
                 grouped[:].rearrange("p (c i t) -> p c t i", i=4, t=PACK),
-                planes[:].rearrange("p t (c i) -> p c t i", i=4),
+                planes.rearrange("p t (c i) -> p c t i", i=4),
             )
             return grouped
+
+        def pack_wo(g):
+            grouped = turn("w_bf16", [P, PACK * N], BF16, 3)
+            return quantize("wo%d" % g, round_planes(nc.scalar.copy, grouped, wo_raw[g][:]))
 
         used = []
 
@@ -197,29 +204,45 @@ def tile_list_mesh_block_refinement_kernel(
                 nc.scalar.activation(out=window[:, cols], in_=bank[:], func=func)
             return window
 
-        def slopes(words, scales):
-            return [
-                coarse("d_abs", 7, words[:, 2 * P * t : 2 * P * (t + 1)].bitcast(FP4X4), scales[:, P * t : P * (t + 1)], ACT.Abs)
-                for t in range(PACK)
-            ]
+        steps = {}
 
-        def values(codes, scales):
-            return [
-                coarse("h", 6, codes[:, P * t : P * (t + 1)].bitcast(FP8X4), scales[:, P * t : P * (t + 1)], ACT.Copy)
-                for t in range(PACK)
-            ]
+        def slope(g, t):
+            if g not in steps:
+                steps[g] = turn("step", [P, PACK, M], F32, 2)
+            words, scales = slot(ws_ordered, g, t, 2)
+            window = coarse("d_abs", 6, words.bitcast(FP4X4), scales, ACT.Abs)
+            nc.vector.tensor_copy(steps[g][:, t, :], window[:].indirect(p1[:]))
 
-        def fine(g):
-            words = reorder("wf_w%d" % g, group_of(wf_w, g, 4), 4)
-            scales = reorder("wf_s%d" % g, wf_s[:, g * GROUP : (g + 1) * GROUP], 1)
+        def limit(g):
             b_abs = turn("b_abs", [P, PACK, M], F32, 2)
             for t in range(PACK):
-                bank = product(
-                    words[:, 4 * P * t : 4 * P * (t + 1)].bitcast(FP8X4), scales[WF_ROW:P, P * t : P * (t + 1)],
-                    v2_w[:].bitcast(FP8X4), v2_s[TAB2_ROW:P, :],
-                )
+                words, scales = slot(wf_ordered, g, t, 4)
+                bank = product(words.bitcast(FP8X4), scales[WF_ROW:P, :], v2_w[:].bitcast(FP8X4), v2_s[TAB2_ROW:P, :])
                 nc.scalar.activation(out=b_abs[:, t, :], in_=bank[:], func=ACT.Abs)
             return b_abs
+
+        def offset(g, b_abs, engine):
+            step = steps[g]
+            nc.vector.tensor_tensor(step[:], step[:], b_abs[:], ALU.min)
+            for t in range(PACK):
+                engine.tensor_scalar(step[:, t, :], step[:, t, :], off_col[:, t, g : g + 1], 0.0, ALU.mult, ALU.add)
+
+        def value(g, t):
+            codes, scales = wv_q[g]
+            return coarse("h", 5, codes[:, P * t : P * (t + 1)].bitcast(FP8X4), scales[:, P * t : P * (t + 1)], ACT.Copy)
+
+        def refine(g, t, h, planes, part, parts):
+            width = M // parts
+            offsets = p1[:, part * width // 16 : (part + 1) * width // 16]
+            nc.vector.tensor_tensor(
+                planes[:, t, :], h[:].indirect(offsets), steps[g][:, t, part * width : (part + 1) * width], ALU.add
+            )
+
+        def halves(codes, scales):
+            return [
+                (codes[:, half * HALF : (half + 1) * HALF], scales[:, half * HALF : (half + 1) * HALF])
+                for half in range(HALVES)
+            ]
 
         nc.scalar.copy(
             off_slots[:].rearrange("p (t c i) -> p t c i", t=PACK, i=RUN),
@@ -230,60 +253,60 @@ def tile_list_mesh_block_refinement_kernel(
             nc.tensor.transpose(off_bank[:, t, :], off_slots[:, t * P : (t + 1) * P], ident[:])
         nc.scalar.copy(out=off_col[:], in_=off_bank[:, :, 0:GROUPS])
 
-        d_abs = slopes(*ws_first)
         v2_s = held("v2_s", [P, M], U8)
-        nc.vector.tensor_copy(v2_s[:], tab2_s[:].indirect(idx2[:]))
         v2_w = held("v2_w", [P, M], U32)
-        nc.vector.tensor_copy(v2_w[:], tab2_w[:].indirect(idx2[:]))
-        wv_q = quantize("wv0", round_wv(0))
-
-        def pack_wo(g):
-            return quantize("wo%d" % g, round_planes(nc.scalar.copy, "w_bf16", wo_raw[g]))
-
-        def halves(codes, scales):
-            return [
-                (codes[:, half * HALF : (half + 1) * HALF], scales[:, half * HALF : (half + 1) * HALF])
-                for half in range(HALVES)
-            ]
-
-        wo_q, z_q = [], []
+        wv_q, wo_q, z_q, wf_ordered = [], [], [], []
+        for t in range(PACK):
+            slope(0, t)
+            if t == 0:
+                nc.vector.tensor_copy(v2_s[:], tab2_s[:].indirect(idx2[:]))
+                nc.vector.tensor_copy(v2_w[:], tab2_w[:].indirect(idx2[:]))
+                wf_ordered.append(reorder_weight("wf", wf_raw, wf_s, 0, 4))
         for g in range(GROUPS):
             last = g == GROUPS - 1
-            b_abs = fine(g)
-            step = turn("step", [P, PACK, M], F32, 1)
-            for t in range(PACK):
-                nc.vector.tensor_copy(step[:, t, :], d_abs[t][:].indirect(p1[:]))
-            nc.vector.tensor_tensor(step[:], step[:], b_abs[:], ALU.min)
-            wv_now = wv_q
-            if last:
-                wo_q.append(pack_wo(g))
-            else:
-                wv_q = quantize("wv%d" % (g + 1), round_wv(g + 1))
-            h = values(*wv_now)
-            for t in range(PACK):
-                nc.vector.tensor_scalar(step[:, t, :], step[:, t, :], off_col[:, t, g : g + 1], None, ALU.mult)
-            parts = HALVES if last else 1
-            width = M // parts
-            z = []
-            for part in range(parts):
-                planes = turn("z", [P, PACK, width], F32, 2)
-                offsets = p1[:, part * width // 16 : (part + 1) * width // 16]
+            b_abs = limit(g)
+            if g == 0:
+                wv_q.append(pack_wv(0))
+                wo_raw.append(load_wo(1))
+                ws_ordered.append(reorder_weight("ws", ws_raw, ws_s, 1, 2))
+            offset(g, b_abs, nc.vector if last else nc.gpsimd)
+            if not last:
                 for t in range(PACK):
-                    nc.vector.tensor_tensor(
-                        planes[:, t, :], h[t][:].indirect(offsets), step[:, t, part * width : (part + 1) * width], ALU.add
-                    )
-                z.append(planes)
-            if last:
-                rounded = [
-                    round_planes(nc.scalar.copy, "w_bf16", z[0]),
-                    round_planes(nc.vector.tensor_copy, "z_bf16", z[1]),
-                ]
-                packed = [quantize("z%d_%d" % (g, part), rounded[part]) for part in range(parts)]
-                z_q.append([(codes[:], scales[:]) for codes, scales in packed])
+                    slope(g + 1, t)
+                wv_q.append(pack_wv(g + 1))
+                if g == 0:
+                    wo_raw.append(load_wo(2))
+                    wf_ordered.append(reorder_weight("wf", wf_raw, wf_s, 1, 4))
+                planes = turn("z", [P, PACK, M], F32, 1)
+                for t in range(PACK):
+                    if g == 1 and t == EARLY:
+                        wo_q.append(pack_wo(0))
+                    refine(g, t, value(g, t), planes, 0, 1)
+                grouped = turn("z_bf16", [P, PACK * M], BF16, 1)
+                z_q.append(halves(*quantize("z%d" % g, round_planes(nc.vector.tensor_copy, grouped, planes[:]))))
             else:
-                z_q.append(halves(*quantize("z%d" % g, round_planes(nc.vector.tensor_copy, "z_bf16", z[0]))))
-                d_abs = slopes(*reorder_ws(g + 1))
-                wo_q.append(pack_wo(g))
+                planes = turn("z", [P, PACK, HALF], F32, 1)
+                h = []
+                wo_q.append(pack_wo(1))
+                for t in range(PACK):
+                    if t == EARLY:
+                        wo_q.append(pack_wo(2))
+                    h.append(value(g, t))
+                    refine(g, t, h[t], planes[:], 0, HALVES)
+                first = round_planes(nc.scalar.copy, turn("w_bf16", [P, PACK * HALF], BF16, 3), planes[:])
+                spent = steps[g][:, :, :HALF]
+                for t in range(PACK):
+                    offsets = p1[:, HALF // 16 :]
+                    nc.vector.tensor_tensor(
+                        spent[:, PACK - 1 - t, :], h[t][:].indirect(offsets), steps[g][:, t, HALF:], ALU.add
+                    )
+                second = turn("z_bf16", [P, PACK * HALF], BF16, 1)
+                nc.vector.tensor_copy(
+                    second[:].rearrange("p (c i t) -> p c t i", i=4, t=PACK),
+                    spent[:, ::-1, :].rearrange("p t (c i) -> p c t i", i=4),
+                )
+                packed = [quantize("z%d_%d" % (g, part), r) for part, r in enumerate((first, second))]
+                z_q.append([(codes[:], scales[:]) for codes, scales in packed])
 
         acc = [[next_bank([P, HALF]) for n in range(N // P)] for half in range(HALVES)]
         for g in range(GROUPS):
@@ -298,9 +321,10 @@ def tile_list_mesh_block_refinement_kernel(
                     )
 
         for half in range(HALVES):
+            results = turn("b_abs", [P, 2, 2, HALF], F32, 2)
             for pair, copy in enumerate((nc.scalar.copy, nc.vector.tensor_copy)):
-                result = held("result%d_%d" % (half, pair), [P, 2, HALF], F32)
+                result = results[:, pair]
                 for n in range(2):
                     copy(result[:, n, :], acc[half][2 * pair + n][:])
                 rows = out[2 * pair * P : 2 * (pair + 1) * P, half * HALF : (half + 1) * HALF]
-                nc.sync.dma_start(out=rows.rearrange("(n p) m -> p n m", p=P), in_=result[:])
+                nc.sync.dma_start(out=rows.rearrange("(n p) m -> p n m", p=P), in_=result)

@@ -269,7 +269,7 @@ def tile_list_mesh_block_refinement_kernel(
                 wv_q.append(pack_wv(0))
                 wo_raw.append(load_wo(1))
                 ws_ordered.append(reorder_weight("ws", ws_raw, ws_s, 1, 2))
-            offset(g, b_abs, nc.vector if last else nc.gpsimd)
+            offset(g, b_abs, nc.vector)
             if not last:
                 for t in range(PACK):
                     slope(g + 1, t)

@@ -181,6 +181,13 @@ def tile_list_mesh_block_refinement_kernel(
             )
             return grouped
 
+        def pool_round(grouped, planes):
+            nc.gpsimd.tensor_scalar(
+                grouped[:].rearrange("p (n t) -> p n t", t=PACK), planes.rearrange("p t n -> p n t"),
+                1.0, 0.0, ALU.mult, ALU.add,
+            )
+            return grouped
+
         def pack_wo(g):
             grouped = turn("w_bf16", [P, PACK * N], BF16, 3)
             return quantize("wo%d" % g, round_planes(nc.scalar.copy, grouped, wo_raw[g][:]))
@@ -214,18 +221,18 @@ def tile_list_mesh_block_refinement_kernel(
             nc.vector.tensor_copy(steps[g][:, t, :], window[:].indirect(p1[:]))
 
         def limit(g):
-            b_abs = turn("b_abs", [P, PACK, M], F32, 2)
+            b_abs = turn("fine%d" % (g % 2), [P, PACK, M], F32, 1)
             for t in range(PACK):
                 words, scales = slot(wf_ordered, g, t, 4)
                 bank = product(words.bitcast(FP8X4), scales[WF_ROW:P, :], v2_w[:].bitcast(FP8X4), v2_s[TAB2_ROW:P, :])
                 nc.scalar.activation(out=b_abs[:, t, :], in_=bank[:], func=ACT.Abs)
             return b_abs
 
-        def offset(g, b_abs, engine):
+        def offset(g, b_abs):
             step = steps[g]
-            nc.vector.tensor_tensor(step[:], step[:], b_abs[:], ALU.min)
+            nc.vector.tensor_tensor(b_abs[:], step[:], b_abs[:], ALU.min)
             for t in range(PACK):
-                engine.tensor_scalar(step[:, t, :], step[:, t, :], off_col[:, t, g : g + 1], 0.0, ALU.mult, ALU.add)
+                nc.vector.tensor_scalar(step[:, t, :], b_abs[:, t, :], off_col[:, t, g : g + 1], None, ALU.mult)
 
         def value(g, t):
             codes, scales = wv_q[g]
@@ -269,8 +276,9 @@ def tile_list_mesh_block_refinement_kernel(
                 wv_q.append(pack_wv(0))
                 wo_raw.append(load_wo(1))
                 ws_ordered.append(reorder_weight("ws", ws_raw, ws_s, 1, 2))
-            offset(g, b_abs, nc.vector)
+            offset(g, b_abs)
             if not last:
+                wo_bf16 = pool_round(turn("fine%d" % (g % 2), [P, PACK * N], BF16, 1), wo_raw[g][:])
                 for t in range(PACK):
                     slope(g + 1, t)
                 wv_q.append(pack_wv(g + 1))
@@ -279,15 +287,14 @@ def tile_list_mesh_block_refinement_kernel(
                     wf_ordered.append(reorder_weight("wf", wf_raw, wf_s, 1, 4))
                 planes = turn("z", [P, PACK, M], F32, 1)
                 for t in range(PACK):
-                    if g == 1 and t == EARLY:
-                        wo_q.append(pack_wo(0))
+                    if t == EARLY:
+                        wo_q.append(quantize("wo%d" % g, wo_bf16))
                     refine(g, t, value(g, t), planes, 0, 1)
                 grouped = turn("z_bf16", [P, PACK * M], BF16, 1)
                 z_q.append(halves(*quantize("z%d" % g, round_planes(nc.vector.tensor_copy, grouped, planes[:]))))
             else:
                 planes = turn("z", [P, PACK, HALF], F32, 1)
                 h = []
-                wo_q.append(pack_wo(1))
                 for t in range(PACK):
                     if t == EARLY:
                         wo_q.append(pack_wo(2))
@@ -321,7 +328,7 @@ def tile_list_mesh_block_refinement_kernel(
                     )
 
         for half in range(HALVES):
-            results = turn("b_abs", [P, 2, 2, HALF], F32, 2)
+            results = turn(("fine1", "step")[half], [P, 2, 2, HALF], F32, 1 + half)
             for pair, copy in enumerate((nc.scalar.copy, nc.vector.tensor_copy)):
                 result = results[:, pair]
                 for n in range(2):

@@ -66,7 +66,7 @@ def tile_list_mesh_block_refinement_kernel(
         tab2_s = held("tab2_s", [P, T2], U8)
         ws_raw = [held("ws_raw%d" % first, [P, 2 * GROUP * count], U8) for first, count in SPANS]
         ws_s = held("ws_s", [P, H], U8)
-        wf_raw = [held("wf_raw%d" % first, [P, 4 * GROUP * count], U8) for first, count in SPANS]
+        wf_raw = [turn("wf_first", [P, 4 * GROUP], U8, 1), held("wf_rest", [P, 4 * GROUP * (GROUPS - 1)], U8)]
         wf_s = held("wf_s", [P, H], U8)
         off_rows = held("off_rows", [P, GROUP], F32)
         off_slots = held("off_slots", [P, GROUP], F32)
@@ -117,10 +117,10 @@ def tile_list_mesh_block_refinement_kernel(
             in_=tab2_words[0].rearrange("p t i -> p (t i)").bitcast(I32),
         )
         nc.sync.dma_start(idx2[:], offs2)
-        nc.sync.dma_start(p1[:], pos1)
         load_scales(tab2_s, tab2_scales, TAB2_ROW)
-        load_words(wf_raw, wf_rows, 0)
+        nc.sync.dma_start(p1[:], pos1)
         load_scales(wf_s, wf_scales, WF_ROW)
+        load_words(wf_raw, wf_rows, 0)
         wv_raw = [load_wv(0)]
         load_words(ws_raw, ws_rows, 1)
         wv_raw.append(load_wv(1))
@@ -140,8 +140,8 @@ def tile_list_mesh_block_refinement_kernel(
 
         def reorder_weight(name, raw, plane, span, bytes_per_col):
             first, count = SPANS[span]
-            words = reorder(name + "_words", raw[span][:], span, bytes_per_col)
             scales = reorder(name + "_scales", plane[:, first * GROUP : (first + count) * GROUP], span, 1)
+            words = reorder(name + "_words", raw[span][:], span, bytes_per_col)
             return words, scales
 
         def slot(ordered, g, t, bytes_per_col):
@@ -205,34 +205,43 @@ def tile_list_mesh_block_refinement_kernel(
 
         def coarse(name, bufs, lhs, lhs_s, func):
             window = turn(name, [P, S], F32, bufs)
-            for half in range(S // BANK):
-                cols = slice(half * BANK, (half + 1) * BANK)
-                bank = product(lhs, lhs_s, v_w[half][:].bitcast(FP8X4), v_s[:, cols])
-                nc.scalar.activation(out=window[:, cols], in_=bank[:], func=func)
+            cols = [slice(half * BANK, (half + 1) * BANK) for half in range(S // BANK)]
+            banks = [product(lhs, lhs_s, words[:].bitcast(FP8X4), v_s[:, c]) for words, c in zip(v_w, cols)]
+            for bank, c in reversed(list(zip(banks, cols))):
+                nc.scalar.activation(out=window[:, c], in_=bank[:], func=func)
             return window
 
         steps = {}
 
         def slope(g, t):
-            if g not in steps:
-                steps[g] = turn("step", [P, PACK, M], F32, 2)
+            if t % 2 == 0 and g == 0:
+                steps[g, t // 2] = turn(("step_first", "wf_first")[t // 2], [P, 2, M], F32, 1)[:]
+            elif t == 0:
+                whole = turn("step%d" % g, [P, PACK, M], F32, 1)
+                steps[g] = whole
+                steps[g, 0], steps[g, 1] = whole[:, :2, :], whole[:, 2:, :]
             words, scales = slot(ws_ordered, g, t, 2)
             window = coarse("d_abs", 6, words.bitcast(FP4X4), scales, ACT.Abs)
-            nc.vector.tensor_copy(steps[g][:, t, :], window[:].indirect(p1[:]))
+            nc.vector.tensor_copy(steps[g, t // 2][:, t % 2, :], window[:].indirect(p1[:]))
 
         def limit(g):
             b_abs = turn("fine%d" % (g % 2), [P, PACK, M], F32, 1)
+            banks = []
             for t in range(PACK):
                 words, scales = slot(wf_ordered, g, t, 4)
-                bank = product(words.bitcast(FP8X4), scales[WF_ROW:P, :], v2_w[:].bitcast(FP8X4), v2_s[TAB2_ROW:P, :])
-                nc.scalar.activation(out=b_abs[:, t, :], in_=bank[:], func=ACT.Abs)
+                banks.append(
+                    product(words.bitcast(FP8X4), scales[WF_ROW:P, :], v2_w[:].bitcast(FP8X4), v2_s[TAB2_ROW:P, :])
+                )
+            for t in range(PACK):
+                nc.scalar.activation(out=b_abs[:, t ^ 1, :], in_=banks[t ^ 1][:], func=ACT.Abs)
             return b_abs
 
         def offset(g, b_abs):
-            step = steps[g]
-            nc.vector.tensor_tensor(b_abs[:], step[:], b_abs[:], ALU.min)
+            for u in range(2):
+                pair = b_abs[:, 2 * u : 2 * u + 2, :]
+                nc.vector.tensor_tensor(pair, steps[g, u], pair, ALU.min)
             for t in range(PACK):
-                nc.vector.tensor_scalar(step[:, t, :], b_abs[:, t, :], off_col[:, t, g : g + 1], None, ALU.mult)
+                nc.vector.tensor_scalar(steps[g, t // 2][:, t % 2, :], b_abs[:, t, :], off_col[:, t, g : g + 1], None, ALU.mult)
 
         def value(g, t):
             codes, scales = wv_q[g]
@@ -242,7 +251,7 @@ def tile_list_mesh_block_refinement_kernel(
             width = M // parts
             offsets = p1[:, part * width // 16 : (part + 1) * width // 16]
             nc.vector.tensor_tensor(
-                planes[:, t, :], h[:].indirect(offsets), steps[g][:, t, part * width : (part + 1) * width], ALU.add
+                planes[:, t, :], h[:].indirect(offsets), steps[g, t // 2][:, t % 2, part * width : (part + 1) * width], ALU.add
             )
 
         def halves(codes, scales):
@@ -263,12 +272,11 @@ def tile_list_mesh_block_refinement_kernel(
         v2_s = held("v2_s", [P, M], U8)
         v2_w = held("v2_w", [P, M], U32)
         wv_q, wo_q, z_q, wf_ordered = [], [], [], []
+        nc.vector.tensor_copy(v2_w[:], tab2_w[:].indirect(idx2[:]))
+        nc.vector.tensor_copy(v2_s[:], tab2_s[:].indirect(idx2[:]))
+        wf_ordered.append(reorder_weight("wf", wf_raw, wf_s, 0, 4))
         for t in range(PACK):
             slope(0, t)
-            if t == 0:
-                nc.vector.tensor_copy(v2_s[:], tab2_s[:].indirect(idx2[:]))
-                nc.vector.tensor_copy(v2_w[:], tab2_w[:].indirect(idx2[:]))
-                wf_ordered.append(reorder_weight("wf", wf_raw, wf_s, 0, 4))
         for g in range(GROUPS):
             last = g == GROUPS - 1
             b_abs = limit(g)
@@ -281,6 +289,9 @@ def tile_list_mesh_block_refinement_kernel(
                 wo_bf16 = pool_round(turn("fine%d" % (g % 2), [P, PACK * N], BF16, 1), wo_raw[g][:])
                 for t in range(PACK):
                     slope(g + 1, t)
+                if g == 1:
+                    grouped = turn("z_bf16", [P, PACK * M], BF16, 1)
+                    z_q.append(halves(*quantize("z0", round_planes(nc.scalar.copy, grouped, planes[:]))))
                 wv_q.append(pack_wv(g + 1))
                 if g == 0:
                     wo_raw.append(load_wo(2))
@@ -290,8 +301,9 @@ def tile_list_mesh_block_refinement_kernel(
                     if t == EARLY:
                         wo_q.append(quantize("wo%d" % g, wo_bf16))
                     refine(g, t, value(g, t), planes, 0, 1)
-                grouped = turn("z_bf16", [P, PACK * M], BF16, 1)
-                z_q.append(halves(*quantize("z%d" % g, round_planes(nc.vector.tensor_copy, grouped, planes[:]))))
+                if g == 1:
+                    grouped = turn("z_bf16", [P, PACK * M], BF16, 1)
+                    z_q.append(halves(*quantize("z1", round_planes(nc.vector.tensor_copy, grouped, planes[:]))))
             else:
                 planes = turn("z", [P, PACK, HALF], F32, 1)
                 h = []
@@ -328,7 +340,7 @@ def tile_list_mesh_block_refinement_kernel(
                     )
 
         for half in range(HALVES):
-            results = turn(("fine1", "step")[half], [P, 2, 2, HALF], F32, 1 + half)
+            results = turn(("fine1", "step1")[half], [P, 2, 2, HALF], F32, 1)
             for pair, copy in enumerate((nc.scalar.copy, nc.vector.tensor_copy)):
                 result = results[:, pair]
                 for n in range(2):

@@ -31,7 +31,8 @@ TAB_LAST = T - T // 4
 HALF = M // HALVES
 TAB2_ROW = 4
 WF_ROW = 8
-EARLY = PACK // 2
+FRESH = 6
+SHARE = GROUPS * N // 2
 
 
 def tile_list_mesh_block_refinement_kernel(
@@ -60,9 +61,9 @@ def tile_list_mesh_block_refinement_kernel(
         idx = held("idx", [P, S // 16], U16)
         idx2 = held("idx2", [P, M // 16], U16)
         p1 = held("p1", [P, M // 16], U16)
-        tab_w = held("tab_w", [P, T], U32)
+        tab_w = turn("tab_w", [P, T], U32, 1)
         tab_s = held("tab_s", [P, T], U8)
-        tab2_w = held("tab2_w", [P, T2], U32)
+        tab2_w = turn("tab2_w", [P, T2], U32, 1)
         tab2_s = held("tab2_s", [P, T2], U8)
         ws_raw = [held("ws_raw%d" % first, [P, 2 * GROUP * count], U8) for first, count in SPANS]
         ws_s = held("ws_s", [P, H], U8)
@@ -125,8 +126,7 @@ def tile_list_mesh_block_refinement_kernel(
         load_words(ws_raw, ws_rows, 1)
         wv_raw.append(load_wv(1))
         load_words(wf_raw, wf_rows, 1)
-        wv_raw.append(load_wv(2))
-        wo_raw = [load_wo(0)]
+        wo_raw = [load_wo(0), load_wo(1)]
 
         def reorder(name, src, span, bytes_per_col):
             count = SPANS[span][1]
@@ -183,14 +183,9 @@ def tile_list_mesh_block_refinement_kernel(
 
         def pool_round(grouped, planes):
             nc.gpsimd.tensor_scalar(
-                grouped[:].rearrange("p (n t) -> p n t", t=PACK), planes.rearrange("p t n -> p n t"),
+                grouped.rearrange("p (n t) -> p n t", t=PACK), planes.rearrange("p t n -> p n t"),
                 1.0, 0.0, ALU.mult, ALU.add,
             )
-            return grouped
-
-        def pack_wo(g):
-            grouped = turn("w_bf16", [P, PACK * N], BF16, 3)
-            return quantize("wo%d" % g, round_planes(nc.scalar.copy, grouped, wo_raw[g][:]))
 
         used = []
 
@@ -203,15 +198,14 @@ def tile_list_mesh_block_refinement_kernel(
             nc.tensor.matmul_mx(out=bank[:], lhsT=lhs, lhsT_scale=lhs_s, rhs=rhs, rhs_scale=rhs_s, start=True, stop=True)
             return bank
 
-        def coarse(name, bufs, lhs, lhs_s, func):
-            window = turn(name, [P, S], F32, bufs)
+        def coarse(window, lhs, lhs_s, func):
             cols = [slice(half * BANK, (half + 1) * BANK) for half in range(S // BANK)]
             banks = [product(lhs, lhs_s, words[:].bitcast(FP8X4), v_s[:, c]) for words, c in zip(v_w, cols)]
             for bank, c in reversed(list(zip(banks, cols))):
                 nc.scalar.activation(out=window[:, c], in_=bank[:], func=func)
             return window
 
-        steps = {}
+        steps, late = {}, []
 
         def slope(g, t):
             if t % 2 == 0 and g == 0:
@@ -221,8 +215,14 @@ def tile_list_mesh_block_refinement_kernel(
                 steps[g] = whole
                 steps[g, 0], steps[g, 1] = whole[:, :2, :], whole[:, 2:, :]
             words, scales = slot(ws_ordered, g, t, 2)
-            window = coarse("d_abs", 6, words.bitcast(FP4X4), scales, ACT.Abs)
-            nc.vector.tensor_copy(steps[g, t // 2][:, t % 2, :], window[:].indirect(p1[:]))
+            tile = PACK * g + t
+            if tile == FRESH:
+                late.extend(two[:, k, :] for two in [turn("tab2_w", [P, 2, S], F32, 1)] for k in range(2))
+            elif tile == FRESH + 2:
+                late.extend(four[:, k, :] for four in [turn("tab_w", [P, PACK, S], F32, 1)] for k in range(PACK))
+            room = turn("window", [P, S], F32, 9)[:] if tile < FRESH else late[tile - FRESH]
+            window = coarse(room, words.bitcast(FP4X4), scales, ACT.Abs)
+            nc.vector.tensor_copy(steps[g, t // 2][:, t % 2, :], window.indirect(p1[:]))
 
         def limit(g):
             b_abs = turn("fine%d" % (g % 2), [P, PACK, M], F32, 1)
@@ -245,7 +245,9 @@ def tile_list_mesh_block_refinement_kernel(
 
         def value(g, t):
             codes, scales = wv_q[g]
-            return coarse("h", 5, codes[:, P * t : P * (t + 1)].bitcast(FP8X4), scales[:, P * t : P * (t + 1)], ACT.Copy)
+            first = t == 0 and g < GROUPS - 1
+            window = turn("first%d" % g if first else "window", [P, S], F32, 1 if first else 9)
+            return coarse(window, codes[:, P * t : P * (t + 1)].bitcast(FP8X4), scales[:, P * t : P * (t + 1)], ACT.Copy)
 
         def refine(g, t, h, planes, part, parts):
             width = M // parts
@@ -282,11 +284,16 @@ def tile_list_mesh_block_refinement_kernel(
             b_abs = limit(g)
             if g == 0:
                 wv_q.append(pack_wv(0))
-                wo_raw.append(load_wo(1))
+                wv_raw.append(load_wv(2))
                 ws_ordered.append(reorder_weight("ws", ws_raw, ws_s, 1, 2))
             offset(g, b_abs)
             if not last:
-                wo_bf16 = pool_round(turn("fine%d" % (g % 2), [P, PACK * N], BF16, 1), wo_raw[g][:])
+                wo_bf16 = turn("fine%d" % (g % 2), [P, PACK * SHARE], BF16, 1)
+                pieces = [wo_raw[0][:], wo_raw[1][:, :, : N // 2]] if g == 0 else [wo_raw[1][:, :, N // 2 :], wo_raw[2][:]]
+                cut = pieces[0].shape[2]
+                spans = (slice(0, cut), slice(cut, SHARE))
+                for piece, span in zip(pieces, spans):
+                    pool_round(wo_bf16[:, PACK * span.start : PACK * span.stop], piece)
                 for t in range(PACK):
                     slope(g + 1, t)
                 if g == 1:
@@ -298,9 +305,16 @@ def tile_list_mesh_block_refinement_kernel(
                     wf_ordered.append(reorder_weight("wf", wf_raw, wf_s, 1, 4))
                 planes = turn("z", [P, PACK, M], F32, 1)
                 for t in range(PACK):
-                    if t == EARLY:
-                        wo_q.append(quantize("wo%d" % g, wo_bf16))
                     refine(g, t, value(g, t), planes, 0, 1)
+                    if t == 0:
+                        codes = turn("first%d" % g, [P, SHARE], U32, 1)
+                        scales = held("wo_scales%d" % g, [P, SHARE], U8)
+                        for span in spans:
+                            nc.vector.quantize_mx(
+                                out=codes[:, span].bitcast(FP8X4), scales=scales[:, span],
+                                in_=wo_bf16[:, PACK * span.start : PACK * span.stop],
+                            )
+                        wo_q.append((codes, scales))
                 if g == 1:
                     grouped = turn("z_bf16", [P, PACK * M], BF16, 1)
                     z_q.append(halves(*quantize("z1", round_planes(nc.vector.tensor_copy, grouped, planes[:]))))
@@ -308,8 +322,6 @@ def tile_list_mesh_block_refinement_kernel(
                 planes = turn("z", [P, PACK, HALF], F32, 1)
                 h = []
                 for t in range(PACK):
-                    if t == EARLY:
-                        wo_q.append(pack_wo(2))
                     h.append(value(g, t))
                     refine(g, t, h[t], planes[:], 0, HALVES)
                 first = round_planes(nc.scalar.copy, turn("w_bf16", [P, PACK * HALF], BF16, 3), planes[:])
@@ -329,11 +341,12 @@ def tile_list_mesh_block_refinement_kernel(
 
         acc = [[next_bank([P, HALF]) for n in range(N // P)] for half in range(HALVES)]
         for g in range(GROUPS):
-            wo_codes, wo_scales = wo_q[g]
             for half in range(HALVES):
                 z_codes, z_scales = z_q[g][half]
                 for n in range(N // P):
-                    cols = slice(n * P, (n + 1) * P)
+                    share, start = divmod(g * N + n * P, SHARE)
+                    wo_codes, wo_scales = wo_q[share]
+                    cols = slice(start, start + P)
                     nc.tensor.matmul_mx(
                         out=acc[half][n][:], lhsT=wo_codes[:, cols].bitcast(FP8X4), lhsT_scale=wo_scales[:, cols],
                         rhs=z_codes.bitcast(FP8X4), rhs_scale=z_scales, start=(g == 0), stop=(g == GROUPS - 1),

@@ -32,7 +32,6 @@ HALF = M // HALVES
 TAB2_ROW = 4
 WF_ROW = 8
 FRESH = 6
-SHARE = GROUPS * N // 2
 
 
 def tile_list_mesh_block_refinement_kernel(
@@ -126,7 +125,8 @@ def tile_list_mesh_block_refinement_kernel(
         load_words(ws_raw, ws_rows, 1)
         wv_raw.append(load_wv(1))
         load_words(wf_raw, wf_rows, 1)
-        wo_raw = [load_wo(0), load_wo(1)]
+        wo_raw = [load_wo(0)]
+        wv_raw.append(load_wv(2))
 
         def reorder(name, src, span, bytes_per_col):
             count = SPANS[span][1]
@@ -155,13 +155,14 @@ def tile_list_mesh_block_refinement_kernel(
         v_w = []
         for half in range(S // BANK):
             words = held("v_w%d" % half, [P, BANK], U32)
-            cols = slice(half * BANK // 16, (half + 1) * BANK // 16)
-            nc.vector.tensor_copy(words[:], tab_w[:].indirect(idx[:, cols]))
+            part = slice(half * BANK // 16, (half + 1) * BANK // 16)
+            nc.vector.tensor_copy(words[:], tab_w[:].indirect(idx[:, part]))
             v_w.append(words)
 
-        def quantize(name, grouped):
+        def quantize(name, grouped, codes=None):
             width = grouped.shape[1] // PACK
-            codes = held(name + "_codes", [P, width], U32)
+            if codes is None:
+                codes = held(name + "_codes", [P, width], U32)
             scales = held(name + "_scales", [P, width], U8)
             nc.vector.quantize_mx(out=codes[:].bitcast(FP8X4), scales=scales[:], in_=grouped[:])
             return codes, scales
@@ -198,29 +199,41 @@ def tile_list_mesh_block_refinement_kernel(
             nc.tensor.matmul_mx(out=bank[:], lhsT=lhs, lhsT_scale=lhs_s, rhs=rhs, rhs_scale=rhs_s, start=True, stop=True)
             return bank
 
+        cols = [slice(half * BANK, (half + 1) * BANK) for half in range(S // BANK)]
+
         def coarse(window, lhs, lhs_s, func):
-            cols = [slice(half * BANK, (half + 1) * BANK) for half in range(S // BANK)]
             banks = [product(lhs, lhs_s, words[:].bitcast(FP8X4), v_s[:, c]) for words, c in zip(v_w, cols)]
             for bank, c in reversed(list(zip(banks, cols))):
                 nc.scalar.activation(out=window[:, c], in_=bank[:], func=func)
             return window
 
+        def first_slopes():
+            windows = [turn("window", [P, S], F32, 11) for t in range(2)]
+            steps[0, 0] = turn("step_first", [P, 2, M], F32, 1)[:]
+            for words, c in zip(v_w, cols):
+                for t in range(2):
+                    lhs, lhs_s = slot(ws_ordered, 0, t, 2)
+                    bank = product(lhs.bitcast(FP4X4), lhs_s, words[:].bitcast(FP8X4), v_s[:, c])
+                    nc.scalar.activation(out=windows[t][:, c], in_=bank[:], func=ACT.Abs)
+            for t in range(2):
+                nc.vector.tensor_copy(steps[0, 0][:, t, :], windows[t][:].indirect(p1[:]))
+
         steps, late = {}, []
 
         def slope(g, t):
-            if t % 2 == 0 and g == 0:
-                steps[g, t // 2] = turn(("step_first", "wf_first")[t // 2], [P, 2, M], F32, 1)[:]
+            if (g, t) == (0, 2):
+                steps[0, 1] = turn("wf_first", [P, 2, M], F32, 1)[:]
             elif t == 0:
                 whole = turn("step%d" % g, [P, PACK, M], F32, 1)
                 steps[g] = whole
-                steps[g, 0], steps[g, 1] = whole[:, :2, :], whole[:, 2:, :]
+                steps[g, 0], steps[g, 1] = whole[:, :2, :], whole[:, 2:PACK, :]
             words, scales = slot(ws_ordered, g, t, 2)
             tile = PACK * g + t
             if tile == FRESH:
                 late.extend(two[:, k, :] for two in [turn("tab2_w", [P, 2, S], F32, 1)] for k in range(2))
             elif tile == FRESH + 2:
                 late.extend(four[:, k, :] for four in [turn("tab_w", [P, PACK, S], F32, 1)] for k in range(PACK))
-            room = turn("window", [P, S], F32, 9)[:] if tile < FRESH else late[tile - FRESH]
+            room = turn("window", [P, S], F32, 11)[:] if tile < FRESH else late[tile - FRESH]
             window = coarse(room, words.bitcast(FP4X4), scales, ACT.Abs)
             nc.vector.tensor_copy(steps[g, t // 2][:, t % 2, :], window.indirect(p1[:]))
 
@@ -245,8 +258,7 @@ def tile_list_mesh_block_refinement_kernel(
 
         def value(g, t):
             codes, scales = wv_q[g]
-            first = t == 0 and g < GROUPS - 1
-            window = turn("first%d" % g if first else "window", [P, S], F32, 1 if first else 9)
+            window = turn("window", [P, S], F32, 11)
             return coarse(window, codes[:, P * t : P * (t + 1)].bitcast(FP8X4), scales[:, P * t : P * (t + 1)], ACT.Copy)
 
         def refine(g, t, h, planes, part, parts):
@@ -277,23 +289,20 @@ def tile_list_mesh_block_refinement_kernel(
         nc.vector.tensor_copy(v2_w[:], tab2_w[:].indirect(idx2[:]))
         nc.vector.tensor_copy(v2_s[:], tab2_s[:].indirect(idx2[:]))
         wf_ordered.append(reorder_weight("wf", wf_raw, wf_s, 0, 4))
-        for t in range(PACK):
+        first_slopes()
+        for t in range(2, PACK):
             slope(0, t)
         for g in range(GROUPS):
             last = g == GROUPS - 1
             b_abs = limit(g)
             if g == 0:
                 wv_q.append(pack_wv(0))
-                wv_raw.append(load_wv(2))
+                wo_raw.append(load_wo(1))
                 ws_ordered.append(reorder_weight("ws", ws_raw, ws_s, 1, 2))
             offset(g, b_abs)
             if not last:
-                wo_bf16 = turn("fine%d" % (g % 2), [P, PACK * SHARE], BF16, 1)
-                pieces = [wo_raw[0][:], wo_raw[1][:, :, : N // 2]] if g == 0 else [wo_raw[1][:, :, N // 2 :], wo_raw[2][:]]
-                cut = pieces[0].shape[2]
-                spans = (slice(0, cut), slice(cut, SHARE))
-                for piece, span in zip(pieces, spans):
-                    pool_round(wo_bf16[:, PACK * span.start : PACK * span.stop], piece)
+                wo_bf16 = turn("fine%d" % (g % 2), [P, PACK * N], BF16, 1)
+                pool_round(wo_bf16[:], wo_raw[g][:])
                 for t in range(PACK):
                     slope(g + 1, t)
                 if g == 1:
@@ -303,40 +312,32 @@ def tile_list_mesh_block_refinement_kernel(
                 if g == 0:
                     wo_raw.append(load_wo(2))
                     wf_ordered.append(reorder_weight("wf", wf_raw, wf_s, 1, 4))
-                planes = turn("z", [P, PACK, M], F32, 1)
-                for t in range(PACK):
-                    refine(g, t, value(g, t), planes, 0, 1)
-                    if t == 0:
-                        codes = turn("first%d" % g, [P, SHARE], U32, 1)
-                        scales = held("wo_scales%d" % g, [P, SHARE], U8)
-                        for span in spans:
-                            nc.vector.quantize_mx(
-                                out=codes[:, span].bitcast(FP8X4), scales=scales[:, span],
-                                in_=wo_bf16[:, PACK * span.start : PACK * span.stop],
-                            )
-                        wo_q.append((codes, scales))
-                if g == 1:
-                    grouped = turn("z_bf16", [P, PACK * M], BF16, 1)
-                    z_q.append(halves(*quantize("z1", round_planes(nc.vector.tensor_copy, grouped, planes[:]))))
-            else:
-                planes = turn("z", [P, PACK, HALF], F32, 1)
-                h = []
-                for t in range(PACK):
-                    h.append(value(g, t))
-                    refine(g, t, h[t], planes[:], 0, HALVES)
-                first = round_planes(nc.scalar.copy, turn("w_bf16", [P, PACK * HALF], BF16, 3), planes[:])
-                spent = steps[g][:, :, :HALF]
-                for t in range(PACK):
-                    offsets = p1[:, HALF // 16 :]
-                    nc.vector.tensor_tensor(
-                        spent[:, PACK - 1 - t, :], h[t][:].indirect(offsets), steps[g][:, t, HALF:], ALU.add
+            planes = turn("z", [P, PACK, M], F32, 1)
+            for t in range(PACK):
+                if last and t == PACK // 2:
+                    grouped = turn("w_bf16", [P, PACK * N], BF16, 3)
+                    wo_q.append(quantize("wo%d" % g, round_planes(nc.scalar.copy, grouped, wo_raw[g][:])))
+                h = value(g, t)
+                parts = HALVES if g and t == PACK - 1 else 1
+                for part in range(parts):
+                    refine(g, t, h, planes[:, :, part * M // parts : (part + 1) * M // parts], part, parts)
+                if not last and t == 1:
+                    wo_q.append(quantize("wo%d" % g, wo_bf16))
+            sides = [planes[:, :, half * HALF : (half + 1) * HALF] for half in range(HALVES)]
+            if g == 1:
+                grouped = turn("z_bf16", [P, PACK * M], BF16, 1)
+                for half in range(HALVES):
+                    round_planes(
+                        nc.vector.tensor_copy, grouped[:, half * PACK * HALF : (half + 1) * PACK * HALF], sides[half]
                     )
-                second = turn("z_bf16", [P, PACK * HALF], BF16, 1)
-                nc.vector.tensor_copy(
-                    second[:].rearrange("p (c i t) -> p c t i", i=4, t=PACK),
-                    spent[:, ::-1, :].rearrange("p t (c i) -> p c t i", i=4),
-                )
-                packed = [quantize("z%d_%d" % (g, part), r) for part, r in enumerate((first, second))]
+                z_q.append(halves(*quantize("z1", grouped)))
+            elif last:
+                packed = []
+                for half, (copy, name, bufs) in enumerate(
+                    ((nc.vector.tensor_copy, "z_bf16", 1), (nc.scalar.copy, "w_bf16", 3))
+                ):
+                    grouped = turn(name, [P, PACK * HALF], BF16, bufs)
+                    packed.append(quantize("z2_%d" % half, round_planes(copy, grouped, sides[half])))
                 z_q.append([(codes[:], scales[:]) for codes, scales in packed])
 
         acc = [[next_bank([P, HALF]) for n in range(N // P)] for half in range(HALVES)]
@@ -344,19 +345,16 @@ def tile_list_mesh_block_refinement_kernel(
             for half in range(HALVES):
                 z_codes, z_scales = z_q[g][half]
                 for n in range(N // P):
-                    share, start = divmod(g * N + n * P, SHARE)
-                    wo_codes, wo_scales = wo_q[share]
-                    cols = slice(start, start + P)
+                    wo_codes, wo_scales = wo_q[g]
+                    rows = slice(n * P, (n + 1) * P)
                     nc.tensor.matmul_mx(
-                        out=acc[half][n][:], lhsT=wo_codes[:, cols].bitcast(FP8X4), lhsT_scale=wo_scales[:, cols],
+                        out=acc[half][n][:], lhsT=wo_codes[:, rows].bitcast(FP8X4), lhsT_scale=wo_scales[:, rows],
                         rhs=z_codes.bitcast(FP8X4), rhs_scale=z_scales, start=(g == 0), stop=(g == GROUPS - 1),
                     )
 
         for half in range(HALVES):
-            results = turn(("fine1", "step1")[half], [P, 2, 2, HALF], F32, 1)
-            for pair, copy in enumerate((nc.scalar.copy, nc.vector.tensor_copy)):
-                result = results[:, pair]
-                for n in range(2):
-                    copy(result[:, n, :], acc[half][2 * pair + n][:])
-                rows = out[2 * pair * P : 2 * (pair + 1) * P, half * HALF : (half + 1) * HALF]
-                nc.sync.dma_start(out=rows.rearrange("(n p) m -> p n m", p=P), in_=result)
+            results = turn(("fine1", "step1")[half], [P, N // P, HALF], F32, 1)
+            for n in range(N // P):
+                copy = nc.vector.tensor_copy if n % 2 else nc.scalar.copy
+                copy(results[:, n, :], acc[half][n][:])
+                nc.sync.dma_start(out=out[n * P : (n + 1) * P, half * HALF : (half + 1) * HALF], in_=results[:, n, :])

@@ -32,6 +32,7 @@ HALF = M // HALVES
 TAB2_ROW = 4
 WF_ROW = 8
 FRESH = 6
+PAIR_BYTES = 4 * 2 * M
 
 
 def tile_list_mesh_block_refinement_kernel(
@@ -42,6 +43,7 @@ def tile_list_mesh_block_refinement_kernel(
     with ExitStack() as ctx:
         keep = ctx.enter_context(tc.tile_pool(name="keep", bufs=1))
         ring = ctx.enter_context(tc.tile_pool(name="ring", bufs=2))
+        laid = ctx.enter_context(tc.tile_pool(name="laid", bufs=1))
         psum = ctx.enter_context(tc.psum_pool(name="psum", bufs=1))
 
         def held(name, shape, dtype):
@@ -66,7 +68,10 @@ def tile_list_mesh_block_refinement_kernel(
         tab2_s = held("tab2_s", [P, T2], U8)
         ws_raw = [held("ws_raw%d" % first, [P, 2 * GROUP * count], U8) for first, count in SPANS]
         ws_s = held("ws_s", [P, H], U8)
-        wf_raw = [turn("wf_first", [P, 4 * GROUP], U8, 1), held("wf_rest", [P, 4 * GROUP * (GROUPS - 1)], U8)]
+        wf_raw = [
+            laid.tile([P, 4 * GROUP], U8, name="wf_first", align_bytes=64, offset=PAIR_BYTES - 2 * GROUP),
+            held("wf_rest", [P, 4 * GROUP * (GROUPS - 1)], U8),
+        ]
         wf_s = held("wf_s", [P, H], U8)
         off_rows = held("off_rows", [P, GROUP], F32)
         off_slots = held("off_slots", [P, GROUP], F32)
@@ -89,15 +94,15 @@ def tile_list_mesh_block_refinement_kernel(
             nc.sync.dma_start(out=tiles[span][:].bitcast(I32), in_=rows[:, first * n : (first + count) * n])
 
         def load_wv(g):
-            raw = turn("raw", [P, PACK, GROUP], F32, 4)
+            raw = turn("wv_raw%d" % g, [P, PACK, GROUP], F32, 1)
             nc.sync.dma_start(
                 out=raw[:],
                 in_=wv[:, g * GROUP : (g + 1) * GROUP].rearrange("(p j) r -> p j r", j=PACK),
             )
             return raw
 
-        def load_wo(g):
-            raw = turn("raw", [P, PACK, N], F32, 4)
+        def load_wo(g, name):
+            raw = turn(name, [P, PACK, N], F32, 1)
             rows = wo[g * GROUP : (g + 1) * GROUP, :].rearrange("(c t i) n -> t c i n", t=PACK, i=RUN)
             for t in range(PACK):
                 nc.sync.dma_start(out=raw[:, t, :], in_=rows[t])
@@ -120,38 +125,32 @@ def tile_list_mesh_block_refinement_kernel(
         load_scales(tab2_s, tab2_scales, TAB2_ROW)
         nc.sync.dma_start(p1[:], pos1)
         load_scales(wf_s, wf_scales, WF_ROW)
-        load_words(wf_raw, wf_rows, 0)
-        wv_raw = [load_wv(0)]
         load_words(ws_raw, ws_rows, 1)
-        wv_raw.append(load_wv(1))
+        load_words(wf_raw, wf_rows, 0)
+        wv_raw = [load_wv(g) for g in range(GROUPS)]
+        wo_raw = [load_wo(0, "wo_raw0")]
         load_words(wf_raw, wf_rows, 1)
-        wo_raw = [load_wo(0)]
-        wv_raw.append(load_wv(2))
+        wo_raw.append(load_wo(1, "wo_raw1"))
 
-        def reorder(name, src, span, bytes_per_col):
-            count = SPANS[span][1]
+        def reorder(dst, src, count, bytes_per_col):
             w = RUN * bytes_per_col // 4
-            dst = held("%s%d" % (name, span), [P, count * GROUP * bytes_per_col], U8)
             nc.vector.tensor_copy(
-                out=dst[:].bitcast(I32).rearrange("p (g t c w) -> p g t c w", g=count, t=PACK, w=w),
+                out=dst.bitcast(I32).rearrange("p (g t c w) -> p g t c w", g=count, t=PACK, w=w),
                 in_=src.bitcast(I32).rearrange("p (g c t w) -> p g t c w", g=count, t=PACK, w=w),
             )
             return dst
 
-        def reorder_weight(name, raw, plane, span, bytes_per_col):
-            first, count = SPANS[span]
-            scales = reorder(name + "_scales", plane[:, first * GROUP : (first + count) * GROUP], span, 1)
-            words = reorder(name + "_words", raw[span][:], span, bytes_per_col)
-            return words, scales
-
-        def slot(ordered, g, t, bytes_per_col):
-            words, scales = ordered[min(g, 1)]
-            c = (g - SPANS[min(g, 1)][0]) * GROUP + t * P
-            return words[:, bytes_per_col * c : bytes_per_col * (c + P)], scales[:, c : c + P]
+        def reorder_weight(room, raw, plane, first, count, bytes_per_col):
+            n = count * GROUP
+            scales = reorder(room[:, :n], plane[:, first * GROUP : first * GROUP + n], count, 1)
+            words = reorder(room[:, n:], raw[:], count, bytes_per_col)
+            return [
+                (words[:, bytes_per_col * c : bytes_per_col * (c + P)], scales[:, c : c + P]) for c in range(0, n, P)
+            ]
 
         v_s = held("v_s", [P, S], U8)
         nc.vector.tensor_copy(v_s[:], tab_s[:].indirect(idx[:]))
-        ws_ordered = [reorder_weight("ws", ws_raw, ws_s, 0, 2)]
+        ws_slots = reorder_weight(held("ws_first", [P, 3 * GROUP], U8), ws_raw[0], ws_s, 0, 1, 2)
         v_w = []
         for half in range(S // BANK):
             words = held("v_w%d" % half, [P, BANK], U32)
@@ -167,13 +166,16 @@ def tile_list_mesh_block_refinement_kernel(
             nc.vector.quantize_mx(out=codes[:].bitcast(FP8X4), scales=scales[:], in_=grouped[:])
             return codes, scales
 
-        def pack_wv(g):
-            grouped = turn("w_bf16", [P, PACK * GROUP], BF16, 3)
-            nc.scalar.copy(
-                grouped[:].rearrange("p (t c i j) -> p t c j i", t=PACK, i=RUN, j=PACK),
-                wv_raw[g][:].rearrange("p j (c t i) -> p t c j i", t=PACK, i=RUN),
-            )
-            return quantize("wv%d" % g, grouped)
+        def round_wv(g, grouped, slots, on_pool):
+            dst = grouped[:].rearrange("p (t c i j) -> p t c i j", t=PACK, i=RUN, j=PACK)[:, slots]
+            src = wv_raw[g][:].rearrange("p j (c t i) -> p t c i j", t=PACK, i=RUN)[:, slots]
+            if on_pool:
+                order = "p t c i j -> p c t i j"
+                nc.gpsimd.tensor_scalar(dst.rearrange(order), src.rearrange(order), 1.0, 0.0, ALU.mult, ALU.add)
+            else:
+                order = "p t c i j -> p t c j i"
+                nc.scalar.copy(dst.rearrange(order), src.rearrange(order))
+            return grouped
 
         def round_planes(copy, grouped, planes):
             copy(
@@ -212,7 +214,7 @@ def tile_list_mesh_block_refinement_kernel(
             steps[0, 0] = turn("step_first", [P, 2, M], F32, 1)[:]
             for words, c in zip(v_w, cols):
                 for t in range(2):
-                    lhs, lhs_s = slot(ws_ordered, 0, t, 2)
+                    lhs, lhs_s = ws_slots[t]
                     bank = product(lhs.bitcast(FP4X4), lhs_s, words[:].bitcast(FP8X4), v_s[:, c])
                     nc.scalar.activation(out=windows[t][:, c], in_=bank[:], func=ACT.Abs)
             for t in range(2):
@@ -222,12 +224,12 @@ def tile_list_mesh_block_refinement_kernel(
 
         def slope(g, t):
             if (g, t) == (0, 2):
-                steps[0, 1] = turn("wf_first", [P, 2, M], F32, 1)[:]
+                steps[0, 1] = laid.tile([P, 2, M], F32, name="step_second", align_bytes=64, offset=0)[:]
             elif t == 0:
                 whole = turn("step%d" % g, [P, PACK, M], F32, 1)
                 steps[g] = whole
                 steps[g, 0], steps[g, 1] = whole[:, :2, :], whole[:, 2:PACK, :]
-            words, scales = slot(ws_ordered, g, t, 2)
+            words, scales = ws_slots[PACK * g + t]
             tile = PACK * g + t
             if tile == FRESH:
                 late.extend(two[:, k, :] for two in [turn("tab2_w", [P, 2, S], F32, 1)] for k in range(2))
@@ -241,7 +243,7 @@ def tile_list_mesh_block_refinement_kernel(
             b_abs = turn("fine%d" % (g % 2), [P, PACK, M], F32, 1)
             banks = []
             for t in range(PACK):
-                words, scales = slot(wf_ordered, g, t, 4)
+                words, scales = wf_slots[PACK * g + t]
                 banks.append(
                     product(words.bitcast(FP8X4), scales[WF_ROW:P, :], v2_w[:].bitcast(FP8X4), v2_s[TAB2_ROW:P, :])
                 )
@@ -285,44 +287,61 @@ def tile_list_mesh_block_refinement_kernel(
 
         v2_s = held("v2_s", [P, M], U8)
         v2_w = held("v2_w", [P, M], U32)
-        wv_q, wo_q, z_q, wf_ordered = [], [], [], []
+        wv_q, wo_q, z_q = [], [], []
         nc.vector.tensor_copy(v2_w[:], tab2_w[:].indirect(idx2[:]))
         nc.vector.tensor_copy(v2_s[:], tab2_s[:].indirect(idx2[:]))
-        wf_ordered.append(reorder_weight("wf", wf_raw, wf_s, 0, 4))
+        ws_slots.extend(reorder_weight(held("ws_rest", [P, 6 * GROUP], U8), ws_raw[1], ws_s, 1, GROUPS - 1, 2))
+        wf_slots = reorder_weight(held("wf_ordered", [P, 5 * GROUP], U8), wf_raw[0], wf_s, 0, 1, 4)
+
+        def wo_half(k):
+            return wo_raw[k // 2][:, :, (k % 2) * N // 2 : (k % 2 + 1) * N // 2]
+
+        def keep_wo(codes, scales):
+            wo_q.extend((codes[:, c : c + P], scales[:, c : c + P]) for c in range(0, codes.shape[1], P))
+
+        wv_first = laid.tile([P, PACK * GROUP], BF16, name="wv_first", align_bytes=64, offset=PAIR_BYTES)
+        round_wv(0, wv_first, slice(0, PACK), True)
+        wv_second = round_wv(1, turn("w_bf16", [P, PACK * GROUP], BF16, 3), slice(0, PACK // 2), True)
+        wo_raw.append(load_wo(2, "wv_raw0"))
         first_slopes()
         for t in range(2, PACK):
             slope(0, t)
+        for t in range(PACK):
+            slope(1, t)
+        wv_q.append(quantize("wv0", wv_first, turn("tab2_w", [P, GROUP], U32, 1)))
         for g in range(GROUPS):
             last = g == GROUPS - 1
             b_abs = limit(g)
-            if g == 0:
-                wv_q.append(pack_wv(0))
-                wo_raw.append(load_wo(1))
-                ws_ordered.append(reorder_weight("ws", ws_raw, ws_s, 1, 2))
             offset(g, b_abs)
-            if not last:
-                wo_bf16 = turn("fine%d" % (g % 2), [P, PACK * N], BF16, 1)
-                pool_round(wo_bf16[:], wo_raw[g][:])
+            if g == 0:
+                wv_q.append(quantize("wv1", round_wv(1, wv_second, slice(PACK // 2, PACK), False)))
+                wv_last = turn("w_bf16", [P, PACK * GROUP], BF16, 3)
+                wv_q.append(quantize("wv2", round_wv(2, wv_last, slice(0, PACK), False)))
+                wo_first = round_planes(nc.scalar.copy, turn("z_bf16", [P, PACK * N // 2], BF16, 1), wo_half(0))
+                room = turn("wv_raw2", [P, 10 * GROUP], U8, 1)
+                wf_slots.extend(reorder_weight(room, wf_raw[1], wf_s, 1, GROUPS - 1, 4))
+                keep_wo(*quantize("wo_first", wo_first))
+            elif g == 1:
+                wo_middle = turn("fine1", [P, PACK * N], BF16, 1)
+                for k in range(2):
+                    pool_round(wo_middle[:, k * PACK * N // 2 : (k + 1) * PACK * N // 2], wo_half(1 + k))
                 for t in range(PACK):
-                    slope(g + 1, t)
-                if g == 1:
-                    grouped = turn("z_bf16", [P, PACK * M], BF16, 1)
-                    z_q.append(halves(*quantize("z0", round_planes(nc.scalar.copy, grouped, planes[:]))))
-                wv_q.append(pack_wv(g + 1))
-                if g == 0:
-                    wo_raw.append(load_wo(2))
-                    wf_ordered.append(reorder_weight("wf", wf_raw, wf_s, 1, 4))
+                    slope(2, t)
+                grouped = turn("z_bf16", [P, PACK * M], BF16, 1)
+                z_q.append(halves(*quantize("z0", round_planes(nc.scalar.copy, grouped, planes[:]))))
             planes = turn("z", [P, PACK, M], F32, 1)
             for t in range(PACK):
                 if last and t == PACK // 2:
                     grouped = turn("w_bf16", [P, PACK * N], BF16, 3)
-                    wo_q.append(quantize("wo%d" % g, round_planes(nc.scalar.copy, grouped, wo_raw[g][:])))
+                    keep_wo(*quantize("wo_last", round_planes(nc.scalar.copy, grouped, wo_raw[g][:])))
                 h = value(g, t)
                 parts = HALVES if g and t == PACK - 1 else 1
                 for part in range(parts):
                     refine(g, t, h, planes[:, :, part * M // parts : (part + 1) * M // parts], part, parts)
-                if not last and t == 1:
-                    wo_q.append(quantize("wo%d" % g, wo_bf16))
+            if g == 1:
+                grouped = round_planes(nc.scalar.copy, turn("w_bf16", [P, PACK * N // 2], BF16, 3), wo_half(3))
+                keep_wo(*quantize("wo_middle", wo_middle, turn("wo_raw1", [P, N], U32, 1)))
+                keep_wo(*quantize("wo_half", grouped))
             sides = [planes[:, :, half * HALF : (half + 1) * HALF] for half in range(HALVES)]
             if g == 1:
                 grouped = turn("z_bf16", [P, PACK * M], BF16, 1)
@@ -345,10 +364,9 @@ def tile_list_mesh_block_refinement_kernel(
             for half in range(HALVES):
                 z_codes, z_scales = z_q[g][half]
                 for n in range(N // P):
-                    wo_codes, wo_scales = wo_q[g]
-                    rows = slice(n * P, (n + 1) * P)
+                    wo_codes, wo_scales = wo_q[g * N // P + n]
                     nc.tensor.matmul_mx(
-                        out=acc[half][n][:], lhsT=wo_codes[:, rows].bitcast(FP8X4), lhsT_scale=wo_scales[:, rows],
+                        out=acc[half][n][:], lhsT=wo_codes.bitcast(FP8X4), lhsT_scale=wo_scales,
                         rhs=z_codes.bitcast(FP8X4), rhs_scale=z_scales, start=(g == 0), stop=(g == GROUPS - 1),
                     )
 

@@ -327,23 +327,26 @@ def tile_list_mesh_block_refinement_kernel(
                     pool_round(wo_middle[:, k * PACK * N // 2 : (k + 1) * PACK * N // 2], wo_half(1 + k))
                 for t in range(PACK):
                     slope(2, t)
-                grouped = turn("z_bf16", [P, PACK * M], BF16, 1)
-                z_q.append(halves(*quantize("z0", round_planes(nc.scalar.copy, grouped, planes[:]))))
-            planes = turn("z", [P, PACK, M], F32, 1)
+            planes = turn("z", [P, PACK, M], F32, 2)
             for t in range(PACK):
                 if last and t == PACK // 2:
                     grouped = turn("w_bf16", [P, PACK * N], BF16, 3)
                     keep_wo(*quantize("wo_last", round_planes(nc.scalar.copy, grouped, wo_raw[g][:])))
                 h = value(g, t)
-                parts = HALVES if g and t == PACK - 1 else 1
+                parts = HALVES if t == PACK - 1 else 1
                 for part in range(parts):
                     refine(g, t, h, planes[:, :, part * M // parts : (part + 1) * M // parts], part, parts)
             if g == 1:
+                round_planes(nc.scalar.copy, z_first[:, PACK * HALF :], sides[1])
+                z_q.append(halves(*quantize("z0", z_first)))
                 grouped = round_planes(nc.scalar.copy, turn("w_bf16", [P, PACK * N // 2], BF16, 3), wo_half(3))
                 keep_wo(*quantize("wo_middle", wo_middle, turn("wo_raw1", [P, N], U32, 1)))
                 keep_wo(*quantize("wo_half", grouped))
             sides = [planes[:, :, half * HALF : (half + 1) * HALF] for half in range(HALVES)]
-            if g == 1:
+            if g == 0:
+                z_first = turn("w_bf16", [P, PACK * M], BF16, 3)
+                round_planes(nc.vector.tensor_copy, z_first[:, : PACK * HALF], sides[0])
+            elif g == 1:
                 grouped = turn("z_bf16", [P, PACK * M], BF16, 1)
                 for half in range(HALVES):
                     round_planes(

@@ -210,7 +210,7 @@ def tile_list_mesh_block_refinement_kernel(
             return window
 
         def first_slopes():
-            windows = [turn("window", [P, S], F32, 11) for t in range(2)]
+            windows = [turn("window", [P, S], F32, 10) for t in range(2)]
             steps[0, 0] = turn("step_first", [P, 2, M], F32, 1)[:]
             for words, c in zip(v_w, cols):
                 for t in range(2):
@@ -235,7 +235,7 @@ def tile_list_mesh_block_refinement_kernel(
                 late.extend(two[:, k, :] for two in [turn("tab2_w", [P, 2, S], F32, 1)] for k in range(2))
             elif tile == FRESH + 2:
                 late.extend(four[:, k, :] for four in [turn("tab_w", [P, PACK, S], F32, 1)] for k in range(PACK))
-            room = turn("window", [P, S], F32, 11)[:] if tile < FRESH else late[tile - FRESH]
+            room = turn("window", [P, S], F32, 10)[:] if tile < FRESH else late[tile - FRESH]
             window = coarse(room, words.bitcast(FP4X4), scales, ACT.Abs)
             nc.vector.tensor_copy(steps[g, t // 2][:, t % 2, :], window.indirect(p1[:]))
 
@@ -256,11 +256,14 @@ def tile_list_mesh_block_refinement_kernel(
                 pair = b_abs[:, 2 * u : 2 * u + 2, :]
                 nc.vector.tensor_tensor(pair, steps[g, u], pair, ALU.min)
             for t in range(PACK):
-                nc.vector.tensor_scalar(steps[g, t // 2][:, t % 2, :], b_abs[:, t, :], off_col[:, t, g : g + 1], None, ALU.mult)
+                engine = nc.gpsimd if g == 1 else nc.vector
+                engine.tensor_scalar(
+                    steps[g, t // 2][:, t % 2, :], b_abs[:, t, :], off_col[:, t, g : g + 1], 0.0, ALU.mult, ALU.add
+                )
 
         def value(g, t):
             codes, scales = wv_q[g]
-            window = turn("window", [P, S], F32, 11)
+            window = turn("window", [P, S], F32, 10)
             return coarse(window, codes[:, P * t : P * (t + 1)].bitcast(FP8X4), scales[:, P * t : P * (t + 1)], ACT.Copy)
 
         def refine(g, t, h, planes, part, parts):
@@ -322,9 +325,8 @@ def tile_list_mesh_block_refinement_kernel(
                 wf_slots.extend(reorder_weight(room, wf_raw[1], wf_s, 1, GROUPS - 1, 4))
                 keep_wo(*quantize("wo_first", wo_first))
             elif g == 1:
-                wo_middle = turn("fine1", [P, PACK * N], BF16, 1)
-                for k in range(2):
-                    pool_round(wo_middle[:, k * PACK * N // 2 : (k + 1) * PACK * N // 2], wo_half(1 + k))
+                wo_second = turn("fine1", [P, PACK * N // 2], BF16, 1)
+                pool_round(wo_second[:], wo_half(1))
                 for t in range(PACK):
                     slope(2, t)
             planes = turn("z", [P, PACK, M], F32, 2)
@@ -333,20 +335,18 @@ def tile_list_mesh_block_refinement_kernel(
                     grouped = turn("w_bf16", [P, PACK * N], BF16, 3)
                     keep_wo(*quantize("wo_last", round_planes(nc.scalar.copy, grouped, wo_raw[g][:])))
                 h = value(g, t)
-                parts = HALVES if t == PACK - 1 else 1
+                parts = HALVES if g and t == PACK - 1 else 1
                 for part in range(parts):
                     refine(g, t, h, planes[:, :, part * M // parts : (part + 1) * M // parts], part, parts)
             if g == 1:
-                round_planes(nc.scalar.copy, z_first[:, PACK * HALF :], sides[1])
-                z_q.append(halves(*quantize("z0", z_first)))
-                grouped = round_planes(nc.scalar.copy, turn("w_bf16", [P, PACK * N // 2], BF16, 3), wo_half(3))
-                keep_wo(*quantize("wo_middle", wo_middle, turn("wo_raw1", [P, N], U32, 1)))
-                keep_wo(*quantize("wo_half", grouped))
-            sides = [planes[:, :, half * HALF : (half + 1) * HALF] for half in range(HALVES)]
-            if g == 0:
                 z_first = turn("w_bf16", [P, PACK * M], BF16, 3)
-                round_planes(nc.vector.tensor_copy, z_first[:, : PACK * HALF], sides[0])
-            elif g == 1:
+                z_q.append(halves(*quantize("z0", round_planes(nc.scalar.copy, z_first, earlier[:]))))
+                grouped = round_planes(nc.scalar.copy, turn("w_bf16", [P, PACK * N], BF16, 3), wo_raw[1][:])
+                keep_wo(*quantize("wo_second", wo_second, turn("wo_raw1", [P, N // 2], U32, 1)))
+                keep_wo(*quantize("wo_middle", grouped))
+            sides = [planes[:, :, half * HALF : (half + 1) * HALF] for half in range(HALVES)]
+            earlier = planes
+            if g == 1:
                 grouped = turn("z_bf16", [P, PACK * M], BF16, 1)
                 for half in range(HALVES):
                     round_planes(

@@ -335,18 +335,20 @@ def tile_list_mesh_block_refinement_kernel(
                     grouped = turn("w_bf16", [P, PACK * N], BF16, 3)
                     keep_wo(*quantize("wo_last", round_planes(nc.scalar.copy, grouped, wo_raw[g][:])))
                 h = value(g, t)
-                parts = HALVES if g and t == PACK - 1 else 1
+                parts = HALVES if t == PACK - 1 else 1
                 for part in range(parts):
                     refine(g, t, h, planes[:, :, part * M // parts : (part + 1) * M // parts], part, parts)
             if g == 1:
-                z_first = turn("w_bf16", [P, PACK * M], BF16, 3)
-                z_q.append(halves(*quantize("z0", round_planes(nc.scalar.copy, z_first, earlier[:]))))
+                round_planes(nc.scalar.copy, z_first[:, PACK * HALF :], sides[1])
+                z_q.append(halves(*quantize("z0", z_first)))
                 grouped = round_planes(nc.scalar.copy, turn("w_bf16", [P, PACK * N], BF16, 3), wo_raw[1][:])
                 keep_wo(*quantize("wo_second", wo_second, turn("wo_raw1", [P, N // 2], U32, 1)))
                 keep_wo(*quantize("wo_middle", grouped))
             sides = [planes[:, :, half * HALF : (half + 1) * HALF] for half in range(HALVES)]
-            earlier = planes
-            if g == 1:
+            if g == 0:
+                z_first = turn("w_bf16", [P, PACK * M], BF16, 3)
+                round_planes(nc.vector.tensor_copy, z_first[:, : PACK * HALF], sides[0])
+            elif g == 1:
                 grouped = turn("z_bf16", [P, PACK * M], BF16, 1)
                 for half in range(HALVES):
                     round_planes(

@@ -23,16 +23,25 @@ RUN = 4
 GROUP = P * PACK
 GROUPS = H // GROUP
 BANK = 512
-BANKS = 8
-HALVES = 2
-SPANS = ((0, 1), (1, GROUPS - 1))
+SET = 4
+HALF = M // 2
+PARTS = (slice(0, HALF), slice(HALF, HALF + P), slice(HALF + P, M))
 TAB_FIRST = T // 4
 TAB_LAST = T - T // 4
-HALF = M // HALVES
 TAB2_ROW = 4
 WF_ROW = 8
-FRESH = 6
-PAIR_BYTES = 4 * 2 * M
+
+KIB = 1024
+WINDOW = 4 * KIB
+PLANES = 8 * KIB
+AT_WINDOWS = 0
+AT_TAB = AT_WINDOWS + 12 * WINDOW
+AT_TAB2 = AT_TAB + 4 * WINDOW
+AT_RAW = AT_TAB2 + PLANES + T2
+AT_PICKS = AT_RAW + 5 * PLANES
+AT_FINE = AT_PICKS + PLANES
+AT_WO_STAGE = AT_FINE + 2 * PLANES
+AT_STAGE = AT_WO_STAGE + PLANES
 
 
 def tile_list_mesh_block_refinement_kernel(
@@ -42,19 +51,18 @@ def tile_list_mesh_block_refinement_kernel(
     nc = tc.nc
     with ExitStack() as ctx:
         keep = ctx.enter_context(tc.tile_pool(name="keep", bufs=1))
-        ring = ctx.enter_context(tc.tile_pool(name="ring", bufs=2))
         laid = ctx.enter_context(tc.tile_pool(name="laid", bufs=1))
         psum = ctx.enter_context(tc.psum_pool(name="psum", bufs=1))
 
         def held(name, shape, dtype):
             return keep.tile(shape, dtype, name=name, align_bytes=64)
 
-        def turn(name, shape, dtype, bufs):
-            return ring.tile(shape, dtype, name=name, bufs=bufs, align_bytes=64)
+        def place(name, shape, dtype, at):
+            return laid.tile(shape, dtype, name=name, align_bytes=64, offset=at)
 
-        def load_scales(plane, scales, row):
+        def load_scales(plane, scales, row, queue):
             for r in range(4):
-                nc.sync.dma_start(
+                queue.dma_start(
                     out=plane[row + r : P : 32, :].bitcast(I32),
                     in_=scales[0, r : 16 : 4, :].bitcast(I32),
                 )
@@ -62,47 +70,48 @@ def tile_list_mesh_block_refinement_kernel(
         idx = held("idx", [P, S // 16], U16)
         idx2 = held("idx2", [P, M // 16], U16)
         p1 = held("p1", [P, M // 16], U16)
-        tab_w = turn("tab_w", [P, T], U32, 1)
+        tab_w = place("tab_w", [P, T], U32, AT_TAB)
         tab_s = held("tab_s", [P, T], U8)
-        tab2_w = turn("tab2_w", [P, T2], U32, 1)
-        tab2_s = held("tab2_s", [P, T2], U8)
-        ws_raw = [held("ws_raw%d" % first, [P, 2 * GROUP * count], U8) for first, count in SPANS]
+        tab2_w = place("tab2_w", [P, T2], U32, AT_TAB2)
+        tab2_s = place("tab2_s", [P, T2], U8, AT_TAB2 + PLANES)
         ws_s = held("ws_s", [P, H], U8)
-        wf_raw = [
-            laid.tile([P, 4 * GROUP], U8, name="wf_first", align_bytes=64, offset=PAIR_BYTES - 2 * GROUP),
-            held("wf_rest", [P, 4 * GROUP * (GROUPS - 1)], U8),
-        ]
         wf_s = held("wf_s", [P, H], U8)
         off_rows = held("off_rows", [P, GROUP], F32)
         off_slots = held("off_slots", [P, GROUP], F32)
-        off_col = held("off_col", [P, PACK, GROUPS], F32)
+        off_col = held("off_col", [P, GROUPS, PACK], F32)
+        off_size = held("off_size", [P, GROUPS, PACK], F32)
+        off_twice = held("off_twice", [P, GROUPS, PACK], F32)
+        off_sign = held("off_sign", [P, GROUPS, PACK], F32)
         ident = held("ident", [P, P], F32)
 
         nc.vector.memset(tab_s[:].bitcast(I32), 0)
         nc.gpsimd.memset(off_rows[:], 0.0)
         nc.vector.memset(ws_s[:].bitcast(I32), 0)
-        nc.gpsimd.memset(tab2_s[:].bitcast(I32), 0)
         nc.vector.memset(wf_s[:].bitcast(I32), 0)
+        make_identity(nc, ident[:])
+        nc.gpsimd.memset(tab2_s[:].bitcast(I32), 0)
+        load_scales(tab2_s, tab2_scales, TAB2_ROW, nc.gpsimd)
 
         tab_rows = tab_words[0].rearrange("p t i -> p (t i)").bitcast(I32)
         ws_rows = ws_words[0].bitcast(I32)
         wf_rows = wf_words[0].rearrange("p t i -> p (t i)").bitcast(I32)
 
-        def load_words(tiles, rows, span):
-            first, count = SPANS[span]
+        def load_words(name, rows, first, count, at=None):
             n = rows.shape[1] // GROUPS
-            nc.sync.dma_start(out=tiles[span][:].bitcast(I32), in_=rows[:, first * n : (first + count) * n])
+            shape = [P, 4 * n * count]
+            raw = held(name, shape, U8) if at is None else place(name, shape, U8, at)
+            nc.sync.dma_start(out=raw[:].bitcast(I32), in_=rows[:, first * n : (first + count) * n])
+            return raw
 
-        def load_wv(g):
-            raw = turn("wv_raw%d" % g, [P, PACK, GROUP], F32, 1)
+        def load_wv(g, raw):
             nc.sync.dma_start(
-                out=raw[:],
+                out=raw,
                 in_=wv[:, g * GROUP : (g + 1) * GROUP].rearrange("(p j) r -> p j r", j=PACK),
             )
             return raw
 
-        def load_wo(g, name):
-            raw = turn(name, [P, PACK, N], F32, 1)
+        def load_wo(g, at):
+            raw = place("wo_raw%d" % g, [P, PACK, N], F32, at)
             rows = wo[g * GROUP : (g + 1) * GROUP, :].rearrange("(c t i) n -> t c i n", t=PACK, i=RUN)
             for t in range(PACK):
                 nc.sync.dma_start(out=raw[:, t, :], in_=rows[t])
@@ -110,27 +119,27 @@ def tile_list_mesh_block_refinement_kernel(
 
         nc.sync.dma_start(idx[:], offs)
         nc.sync.dma_start(out=tab_w[:, :TAB_FIRST].bitcast(I32), in_=tab_rows[:, :TAB_FIRST])
-        load_scales(tab_s, tab_scales, 0)
-        load_words(ws_raw, ws_rows, 0)
+        load_scales(tab_s, tab_scales, 0, nc.sync)
+        ws_first = load_words("ws_first", ws_rows, 0, 1)
         nc.sync.dma_start(out=tab_w[:, TAB_FIRST:TAB_LAST].bitcast(I32), in_=tab_rows[:, TAB_FIRST:TAB_LAST])
-        load_scales(ws_s, ws_scales, 0)
+        load_scales(ws_s, ws_scales, 0, nc.sync)
         nc.sync.dma_start(out=tab_w[:, TAB_LAST:].bitcast(I32), in_=tab_rows[:, TAB_LAST:])
         nc.scalar.dma_start(out=off_rows[0:GROUPS, :], in_=off.rearrange("(g r) -> g r", g=GROUPS))
-        make_identity(nc, ident[:])
+        wf_first = load_words("wf_first", wf_rows, 0, GROUPS - 1, AT_WO_STAGE)
+        load_scales(wf_s, wf_scales, WF_ROW, nc.sync)
+        ws_rest = load_words("ws_rest", ws_rows, 1, GROUPS - 1, AT_WO_STAGE + WINDOW)
+        nc.sync.dma_start(p1[:], pos1)
+        wo_raw = [load_wo(0, AT_RAW)]
         nc.sync.dma_start(
             out=tab2_w[:].bitcast(I32),
             in_=tab2_words[0].rearrange("p t i -> p (t i)").bitcast(I32),
         )
         nc.sync.dma_start(idx2[:], offs2)
-        load_scales(tab2_s, tab2_scales, TAB2_ROW)
-        nc.sync.dma_start(p1[:], pos1)
-        load_scales(wf_s, wf_scales, WF_ROW)
-        load_words(ws_raw, ws_rows, 1)
-        load_words(wf_raw, wf_rows, 0)
-        wv_raw = [load_wv(g) for g in range(GROUPS)]
-        wo_raw = [load_wo(0, "wo_raw0")]
-        load_words(wf_raw, wf_rows, 1)
-        wo_raw.append(load_wo(1, "wo_raw1"))
+        wo_raw.append(load_wo(1, AT_RAW + 2 * PLANES))
+        wf_last = load_words("wf_last", wf_rows, GROUPS - 1, 1)
+        wv_raw = [load_wv(0, place("wv_raw0", [P, PACK, GROUP], F32, AT_RAW + PLANES)[:])]
+        both = place("wv_raw12", [P, 2, PACK, GROUP], F32, AT_RAW + 3 * PLANES)
+        wv_raw.extend(load_wv(g, both[:, g - 1]) for g in (1, 2))
 
         def reorder(dst, src, count, bytes_per_col):
             w = RUN * bytes_per_col // 4
@@ -148,236 +157,219 @@ def tile_list_mesh_block_refinement_kernel(
                 (words[:, bytes_per_col * c : bytes_per_col * (c + P)], scales[:, c : c + P]) for c in range(0, n, P)
             ]
 
+        def quantize(name, grouped, at=None):
+            width = grouped.shape[1] // PACK
+            codes = held(name + "_codes", [P, width], U32)
+            shape = [P, width]
+            scales = held(name + "_scales", shape, U8) if at is None else place(name + "_scales", shape, U8, at)
+            nc.vector.quantize_mx(out=codes[:].bitcast(FP8X4), scales=scales[:], in_=grouped)
+            return codes, scales
+
+        def columns(quantized, width):
+            codes, scales = quantized
+            return [(codes[:, c : c + width], scales[:, c : c + width]) for c in range(0, codes.shape[1], width)]
+
+        def woven(grouped):
+            return grouped.rearrange("p (c i t) -> p c t i", i=4, t=PACK)
+
+        def plain(planes):
+            return planes.rearrange("p t (c i) -> p c t i", i=4)
+
+        def round_wv(copy, grouped, g):
+            copy(
+                grouped.rearrange("p (t c i j) -> p t c j i", t=PACK, i=RUN, j=PACK),
+                wv_raw[g].rearrange("p j (c t i) -> p t c j i", t=PACK, i=RUN),
+            )
+            return grouped
+
+        def round_wo(grouped, raw, g):
+            planes = raw[:].rearrange("p t n -> p n t")
+            nc.gpsimd.tensor_tensor(
+                grouped.rearrange("p (n t) -> p n t", t=PACK), planes,
+                off_sign[:, g : g + 1, :].to_broadcast(list(planes.shape)), ALU.mult,
+            )
+
+        freed = [list(range(SET)), list(range(SET, 2 * SET))]
+        sets = []
+
+        def through_banks(jobs, backwards=True):
+            side = len(sets) % 2
+            sets.append(side)
+            order = list(reversed(jobs)) if backwards else jobs
+            banks = []
+            for number, (dst, func, factor, lhs, lhs_s, rhs, rhs_s) in zip(freed[side], order):
+                bank = psum.tile([P, BANK], F32, name="bank%d" % number)
+                nc.tensor.matmul_mx(
+                    out=bank[:], lhsT=lhs, lhsT_scale=lhs_s, rhs=rhs, rhs_scale=rhs_s, start=True, stop=True
+                )
+                banks.append(bank)
+            if backwards:
+                banks.reverse()
+                freed[side].reverse()
+            for bank, job in zip(banks, jobs):
+                nc.scalar.activation(out=job[0], in_=bank[:], func=job[1], scale=job[2])
+
+        cols = [slice(half * BANK, (half + 1) * BANK) for half in range(S // BANK)]
+
+        def coarse_jobs(window, func, factor, lhs, lhs_s):
+            return [
+                (window[:, c], func, factor, lhs, lhs_s, words[:].bitcast(FP8X4), v_s[:, c])
+                for words, c in zip(v_w, cols)
+            ]
+
+        def slope_jobs(window, g, t):
+            words, scales = ws_slots[PACK * g + t]
+            return coarse_jobs(window, ACT.Abs, off_size[:, g, t : t + 1], words.bitcast(FP4X4), scales)
+
+        def value_jobs(window, g, t):
+            codes, scales = wv_slots[PACK * g + t]
+            return coarse_jobs(window, ACT.Copy, off_sign[:, g, t : t + 1], codes.bitcast(FP8X4), scales)
+
+        def coarse(name, at, jobs, g):
+            windows = [place("%s%d_%d" % (name, g, t), [P, S], F32, at + t * WINDOW) for t in range(PACK)]
+            for t in range(0, PACK, 2):
+                through_banks(jobs(windows[t], g, t) + jobs(windows[t + 1], g, t + 1))
+            return windows
+
+        def pick(planes, windows):
+            for t, window in enumerate(windows):
+                nc.vector.tensor_copy(planes[:, t, :], window[:].indirect(p1[:]))
+
+        def fine(planes, g):
+            through_banks([
+                (planes[:, t, :], ACT.Abs, off_size[:, g, t : t + 1], words.bitcast(FP8X4), scales[WF_ROW:P, :],
+                 v2_w[:].bitcast(FP8X4), v2_s[TAB2_ROW:P, :])
+                for t, (words, scales) in enumerate(wf_slots[PACK * g : PACK * (g + 1)])
+            ])
+
+        nc.scalar.copy(
+            off_slots[:].rearrange("p (t c i) -> p t c i", t=PACK, i=RUN),
+            off_rows[:].rearrange("p (c t i) -> p t c i", t=PACK, i=RUN),
+        )
+        off_bank = psum.tile([P, PACK, P], F32, name="bank%d" % (2 * SET - 1))
+        for t in range(PACK):
+            nc.tensor.transpose(off_bank[:, t, :], off_slots[:, t * P : (t + 1) * P], ident[:])
+        nc.scalar.copy(out=off_col[:].rearrange("p g t -> p t g"), in_=off_bank[:, :, 0:GROUPS])
+        nc.scalar.activation(out=off_size[:], in_=off_col[:], func=ACT.Abs)
+        nc.vector.tensor_scalar(off_twice[:], off_col[:], 0.0, 2.0, ALU.is_ge, ALU.mult)
+        nc.gpsimd.tensor_scalar(off_sign[:], off_twice[:], 1.0, -1.0, ALU.mult, ALU.add)
+
         v_s = held("v_s", [P, S], U8)
         nc.vector.tensor_copy(v_s[:], tab_s[:].indirect(idx[:]))
-        ws_slots = reorder_weight(held("ws_first", [P, 3 * GROUP], U8), ws_raw[0], ws_s, 0, 1, 2)
+        ws_slots = reorder_weight(held("ws_head", [P, 3 * GROUP], U8), ws_first, ws_s, 0, 1, 2)
         v_w = []
         for half in range(S // BANK):
             words = held("v_w%d" % half, [P, BANK], U32)
             part = slice(half * BANK // 16, (half + 1) * BANK // 16)
             nc.vector.tensor_copy(words[:], tab_w[:].indirect(idx[:, part]))
             v_w.append(words)
+        wf_slots = reorder_weight(held("wf_head", [P, 10 * GROUP], U8), wf_first, wf_s, 0, GROUPS - 1, 4)
+        ws_slots.extend(reorder_weight(held("ws_tail", [P, 6 * GROUP], U8), ws_rest, ws_s, 1, GROUPS - 1, 2))
 
-        def quantize(name, grouped, codes=None):
-            width = grouped.shape[1] // PACK
-            if codes is None:
-                codes = held(name + "_codes", [P, width], U32)
-            scales = held(name + "_scales", [P, width], U8)
-            nc.vector.quantize_mx(out=codes[:].bitcast(FP8X4), scales=scales[:], in_=grouped[:])
-            return codes, scales
+        unit = PACK * M
+        wo_bf16 = place("wo_bf16", [P, 2 * unit], BF16, AT_WO_STAGE)
+        for g in range(2):
+            round_wo(wo_bf16[:, g * unit : (g + 1) * unit], wo_raw[g], g)
 
-        def round_wv(g, grouped, slots, on_pool):
-            dst = grouped[:].rearrange("p (t c i j) -> p t c i j", t=PACK, i=RUN, j=PACK)[:, slots]
-            src = wv_raw[g][:].rearrange("p j (c t i) -> p t c i j", t=PACK, i=RUN)[:, slots]
-            if on_pool:
-                order = "p t c i j -> p c t i j"
-                nc.gpsimd.tensor_scalar(dst.rearrange(order), src.rearrange(order), 1.0, 0.0, ALU.mult, ALU.add)
-            else:
-                order = "p t c i j -> p t c j i"
-                nc.scalar.copy(dst.rearrange(order), src.rearrange(order))
-            return grouped
-
-        def round_planes(copy, grouped, planes):
-            copy(
-                grouped[:].rearrange("p (c i t) -> p c t i", i=4, t=PACK),
-                planes.rearrange("p t (c i) -> p c t i", i=4),
-            )
-            return grouped
-
-        def pool_round(grouped, planes):
-            nc.gpsimd.tensor_scalar(
-                grouped.rearrange("p (n t) -> p n t", t=PACK), planes.rearrange("p t n -> p n t"),
-                1.0, 0.0, ALU.mult, ALU.add,
-            )
-
-        used = []
-
-        def next_bank(shape):
-            used.append(len(used))
-            return psum.tile(shape, F32, name="bank%d" % (used[-1] % BANKS))
-
-        def product(lhs, lhs_s, rhs, rhs_s):
-            bank = next_bank([P, BANK])
-            nc.tensor.matmul_mx(out=bank[:], lhsT=lhs, lhsT_scale=lhs_s, rhs=rhs, rhs_scale=rhs_s, start=True, stop=True)
-            return bank
-
-        cols = [slice(half * BANK, (half + 1) * BANK) for half in range(S // BANK)]
-
-        def coarse(window, lhs, lhs_s, func):
-            banks = [product(lhs, lhs_s, words[:].bitcast(FP8X4), v_s[:, c]) for words, c in zip(v_w, cols)]
-            for bank, c in reversed(list(zip(banks, cols))):
-                nc.scalar.activation(out=window[:, c], in_=bank[:], func=func)
-            return window
-
-        def first_slopes():
-            windows = [turn("window", [P, S], F32, 10) for t in range(2)]
-            steps[0, 0] = turn("step_first", [P, 2, M], F32, 1)[:]
-            for words, c in zip(v_w, cols):
-                for t in range(2):
-                    lhs, lhs_s = ws_slots[t]
-                    bank = product(lhs.bitcast(FP4X4), lhs_s, words[:].bitcast(FP8X4), v_s[:, c])
-                    nc.scalar.activation(out=windows[t][:, c], in_=bank[:], func=ACT.Abs)
-            for t in range(2):
-                nc.vector.tensor_copy(steps[0, 0][:, t, :], windows[t][:].indirect(p1[:]))
-
-        steps, late = {}, []
-
-        def slope(g, t):
-            if (g, t) == (0, 2):
-                steps[0, 1] = laid.tile([P, 2, M], F32, name="step_second", align_bytes=64, offset=0)[:]
-            elif t == 0:
-                whole = turn("step%d" % g, [P, PACK, M], F32, 1)
-                steps[g] = whole
-                steps[g, 0], steps[g, 1] = whole[:, :2, :], whole[:, 2:PACK, :]
-            words, scales = ws_slots[PACK * g + t]
-            tile = PACK * g + t
-            if tile == FRESH:
-                late.extend(two[:, k, :] for two in [turn("tab2_w", [P, 2, S], F32, 1)] for k in range(2))
-            elif tile == FRESH + 2:
-                late.extend(four[:, k, :] for four in [turn("tab_w", [P, PACK, S], F32, 1)] for k in range(PACK))
-            room = turn("window", [P, S], F32, 10)[:] if tile < FRESH else late[tile - FRESH]
-            window = coarse(room, words.bitcast(FP4X4), scales, ACT.Abs)
-            nc.vector.tensor_copy(steps[g, t // 2][:, t % 2, :], window.indirect(p1[:]))
-
-        def limit(g):
-            b_abs = turn("fine%d" % (g % 2), [P, PACK, M], F32, 1)
-            banks = []
-            for t in range(PACK):
-                words, scales = wf_slots[PACK * g + t]
-                banks.append(
-                    product(words.bitcast(FP8X4), scales[WF_ROW:P, :], v2_w[:].bitcast(FP8X4), v2_s[TAB2_ROW:P, :])
-                )
-            for t in range(PACK):
-                nc.scalar.activation(out=b_abs[:, t ^ 1, :], in_=banks[t ^ 1][:], func=ACT.Abs)
-            return b_abs
-
-        def offset(g, b_abs):
-            for u in range(2):
-                pair = b_abs[:, 2 * u : 2 * u + 2, :]
-                nc.vector.tensor_tensor(pair, steps[g, u], pair, ALU.min)
-            for t in range(PACK):
-                engine = nc.gpsimd if g == 1 else nc.vector
-                engine.tensor_scalar(
-                    steps[g, t // 2][:, t % 2, :], b_abs[:, t, :], off_col[:, t, g : g + 1], 0.0, ALU.mult, ALU.add
-                )
-
-        def value(g, t):
-            codes, scales = wv_q[g]
-            window = turn("window", [P, S], F32, 10)
-            return coarse(window, codes[:, P * t : P * (t + 1)].bitcast(FP8X4), scales[:, P * t : P * (t + 1)], ACT.Copy)
-
-        def refine(g, t, h, planes, part, parts):
-            width = M // parts
-            offsets = p1[:, part * width // 16 : (part + 1) * width // 16]
-            nc.vector.tensor_tensor(
-                planes[:, t, :], h[:].indirect(offsets), steps[g, t // 2][:, t % 2, part * width : (part + 1) * width], ALU.add
-            )
-
-        def halves(codes, scales):
-            return [
-                (codes[:, half * HALF : (half + 1) * HALF], scales[:, half * HALF : (half + 1) * HALF])
-                for half in range(HALVES)
-            ]
-
-        nc.scalar.copy(
-            off_slots[:].rearrange("p (t c i) -> p t c i", t=PACK, i=RUN),
-            off_rows[:].rearrange("p (c t i) -> p t c i", t=PACK, i=RUN),
-        )
-        off_bank = next_bank([P, PACK, P])
-        for t in range(PACK):
-            nc.tensor.transpose(off_bank[:, t, :], off_slots[:, t * P : (t + 1) * P], ident[:])
-        nc.scalar.copy(out=off_col[:], in_=off_bank[:, :, 0:GROUPS])
-
+        picks = [place("picks%d" % g, [P, PACK, M], F32, at) for g, at in enumerate((AT_PICKS, AT_TAB2 + T2))]
+        limits = [place("limits%d" % g, [P, PACK, M], F32, AT_FINE + g * PLANES) for g in range(2)]
+        windows = [place("d0_%d" % t, [P, S], F32, AT_WINDOWS + t * WINDOW) for t in range(PACK)]
+        jobs = [slope_jobs(windows[t], 0, t) for t in range(PACK)]
+        through_banks([jobs[0][0], jobs[1][0], jobs[0][1], jobs[1][1]], backwards=False)
+        through_banks(jobs[2] + jobs[3])
+        pick(picks[0][:], windows)
         v2_s = held("v2_s", [P, M], U8)
         v2_w = held("v2_w", [P, M], U32)
-        wv_q, wo_q, z_q = [], [], []
+        windows = coarse("d", AT_WINDOWS + 4 * WINDOW, slope_jobs, 1)
         nc.vector.tensor_copy(v2_w[:], tab2_w[:].indirect(idx2[:]))
         nc.vector.tensor_copy(v2_s[:], tab2_s[:].indirect(idx2[:]))
-        ws_slots.extend(reorder_weight(held("ws_rest", [P, 6 * GROUP], U8), ws_raw[1], ws_s, 1, GROUPS - 1, 2))
-        wf_slots = reorder_weight(held("wf_ordered", [P, 5 * GROUP], U8), wf_raw[0], wf_s, 0, 1, 4)
+        pick(picks[1][:], windows)
+        for g in range(2):
+            fine(limits[g][:], g)
 
-        def wo_half(k):
-            return wo_raw[k // 2][:, :, (k % 2) * N // 2 : (k % 2 + 1) * N // 2]
+        wv_first = place("wv_first", [P, PACK * GROUP], BF16, AT_WINDOWS + 6 * WINDOW)
+        round_wv(nc.vector.tensor_copy, wv_first[:], 0)
+        wo_raw.append(load_wo(2, AT_RAW + PLANES))
+        wo_q = columns(quantize("wo01", wo_bf16[:], AT_WINDOWS + 7 * WINDOW), P)
+        wv_slots = columns(quantize("wv0", wv_first[:]), P)
+        least = [
+            place("least%d" % g, [P, PACK * M], F32, at) for g, at in enumerate((AT_WINDOWS + 5 * WINDOW, AT_WO_STAGE))
+        ]
+        for g in (1, 0):
+            nc.vector.tensor_tensor(woven(least[g][:]), plain(picks[g][:]), plain(limits[g][:]), ALU.min)
+        room = place("wf_tail", [P, 5 * GROUP], U8, AT_RAW + 2 * PLANES)
+        wf_slots.extend(reorder_weight(room, wf_last, wf_s, GROUPS - 1, 1, 4))
+        wv_rest = place("wv_rest", [P, 2 * PACK * GROUP], BF16, AT_STAGE)
+        for g in (1, 2):
+            round_wv(nc.scalar.copy, wv_rest[:, (g - 1) * PACK * GROUP : g * PACK * GROUP], g)
+        wv_slots.extend(columns(quantize("wv12", wv_rest[:]), P))
 
-        def keep_wo(codes, scales):
-            wo_q.extend((codes[:, c : c + P], scales[:, c : c + P]) for c in range(0, codes.shape[1], P))
+        last = GROUPS - 1
+        stage = place("stage", [P, GROUPS * unit], BF16, AT_STAGE)
+        round_wo(stage[:, :unit], wo_raw[last], last)
+        for g in range(2):
+            windows = coarse("h", (AT_RAW + 3 * PLANES, AT_WINDOWS)[g], value_jobs, g)
+            values = place("values%d" % g, [P, PACK, M], F32, (AT_PICKS, AT_TAB2 + T2)[g])
+            pick(values[:], windows)
+            nc.gpsimd.tensor_tensor(
+                stage[:, (g + 1) * unit : (g + 2) * unit].rearrange("p (m t) -> p m t", t=PACK),
+                values[:].rearrange("p t m -> p m t"), least[g][:].rearrange("p (m t) -> p m t", t=PACK), ALU.add,
+            )
 
-        wv_first = laid.tile([P, PACK * GROUP], BF16, name="wv_first", align_bytes=64, offset=PAIR_BYTES)
-        round_wv(0, wv_first, slice(0, PACK), True)
-        wv_second = round_wv(1, turn("w_bf16", [P, PACK * GROUP], BF16, 3), slice(0, PACK // 2), True)
-        wo_raw.append(load_wo(2, "wv_raw0"))
-        first_slopes()
-        for t in range(2, PACK):
-            slope(0, t)
-        for t in range(PACK):
-            slope(1, t)
-        wv_q.append(quantize("wv0", wv_first, turn("tab2_w", [P, GROUP], U32, 1)))
-        for g in range(GROUPS):
-            last = g == GROUPS - 1
-            b_abs = limit(g)
-            offset(g, b_abs)
-            if g == 0:
-                wv_q.append(quantize("wv1", round_wv(1, wv_second, slice(PACK // 2, PACK), False)))
-                wv_last = turn("w_bf16", [P, PACK * GROUP], BF16, 3)
-                wv_q.append(quantize("wv2", round_wv(2, wv_last, slice(0, PACK), False)))
-                wo_first = round_planes(nc.scalar.copy, turn("z_bf16", [P, PACK * N // 2], BF16, 1), wo_half(0))
-                room = turn("wv_raw2", [P, 10 * GROUP], U8, 1)
-                wf_slots.extend(reorder_weight(room, wf_raw[1], wf_s, 1, GROUPS - 1, 4))
-                keep_wo(*quantize("wo_first", wo_first))
-            elif g == 1:
-                wo_second = turn("fine1", [P, PACK * N // 2], BF16, 1)
-                pool_round(wo_second[:], wo_half(1))
-                for t in range(PACK):
-                    slope(2, t)
-            planes = turn("z", [P, PACK, M], F32, 2)
+        windows = coarse("d", AT_WINDOWS + 8 * WINDOW, slope_jobs, last)
+        picks = place("picks2", [P, PACK, M], F32, AT_FINE)
+        pick(picks[:], windows)
+        windows = coarse("h", AT_TAB, value_jobs, last)
+        limits = place("limits2", [P, PACK, M], F32, AT_FINE + PLANES)
+        fine(limits[:], last)
+        both = columns(quantize("stage_a", stage[:, : 2 * unit], AT_WINDOWS + 10 * WINDOW), M)
+        wo_q.extend(columns(both[0], P))
+        steps = place("steps2", [P, PACK, M], F32, AT_WINDOWS + 5 * WINDOW)
+        for side in (slice(0, HALF), slice(HALF, M)):
+            nc.vector.tensor_tensor(steps[:, :, side], picks[:, :, side], limits[:, :, side], ALU.min)
+
+        z_last, waiting = [], []
+        for k, part in enumerate(PARTS):
+            width = part.stop - part.start
+            planes = place("z2_%d" % k, [P, PACK, width], F32, AT_WINDOWS + k * WINDOW)
+            offsets = p1[:, part.start // 16 : part.stop // 16]
             for t in range(PACK):
-                if last and t == PACK // 2:
-                    grouped = turn("w_bf16", [P, PACK * N], BF16, 3)
-                    keep_wo(*quantize("wo_last", round_planes(nc.scalar.copy, grouped, wo_raw[g][:])))
-                h = value(g, t)
-                parts = HALVES if t == PACK - 1 else 1
-                for part in range(parts):
-                    refine(g, t, h, planes[:, :, part * M // parts : (part + 1) * M // parts], part, parts)
-            if g == 1:
-                round_planes(nc.scalar.copy, z_first[:, PACK * HALF :], sides[1])
-                z_q.append(halves(*quantize("z0", z_first)))
-                grouped = round_planes(nc.scalar.copy, turn("w_bf16", [P, PACK * N], BF16, 3), wo_raw[1][:])
-                keep_wo(*quantize("wo_second", wo_second, turn("wo_raw1", [P, N // 2], U32, 1)))
-                keep_wo(*quantize("wo_middle", grouped))
-            sides = [planes[:, :, half * HALF : (half + 1) * HALF] for half in range(HALVES)]
-            if g == 0:
-                z_first = turn("w_bf16", [P, PACK * M], BF16, 3)
-                round_planes(nc.vector.tensor_copy, z_first[:, : PACK * HALF], sides[0])
-            elif g == 1:
-                grouped = turn("z_bf16", [P, PACK * M], BF16, 1)
-                for half in range(HALVES):
-                    round_planes(
-                        nc.vector.tensor_copy, grouped[:, half * PACK * HALF : (half + 1) * PACK * HALF], sides[half]
-                    )
-                z_q.append(halves(*quantize("z1", grouped)))
-            elif last:
-                packed = []
-                for half, (copy, name, bufs) in enumerate(
-                    ((nc.vector.tensor_copy, "z_bf16", 1), (nc.scalar.copy, "w_bf16", 3))
-                ):
-                    grouped = turn(name, [P, PACK * HALF], BF16, bufs)
-                    packed.append(quantize("z2_%d" % half, round_planes(copy, grouped, sides[half])))
-                z_q.append([(codes[:], scales[:]) for codes, scales in packed])
+                nc.vector.tensor_tensor(planes[:, t, :], windows[t][:].indirect(offsets), steps[:, t, part], ALU.add)
+            if k == 0:
+                z_early = [both[1], quantize("stage_b", stage[:, 2 * unit :], AT_WINDOWS + 11 * WINDOW)]
+            else:
+                z_last.append(quantize("z2_%d" % (k - 1), waiting[-1]))
+            rounded = held("z2_bf16_%d" % k, [P, PACK * width], BF16)
+            copy = nc.vector.tensor_copy if k == len(PARTS) - 1 else nc.scalar.copy
+            copy(woven(rounded[:]), plain(planes[:]))
+            waiting.append(rounded[:])
+        z_last.append(quantize("z2_%d" % k, waiting[-1]))
 
-        acc = [[next_bank([P, HALF]) for n in range(N // P)] for half in range(HALVES)]
-        for g in range(GROUPS):
-            for half in range(HALVES):
-                z_codes, z_scales = z_q[g][half]
+        numbers = freed[len(sets) % 2] + freed[(len(sets) + 1) % 2]
+        acc = [
+            [psum.tile([P, 2, part.stop - part.start], F32, name="bank%d" % numbers[2 * k + pair]) for pair in range(2)]
+            for k, part in enumerate(PARTS)
+        ]
+        for early, g in enumerate((1, 0, last)):
+            for k, part in enumerate(PARTS):
+                if g == last:
+                    z_codes, z_scales = z_last[k][0][:], z_last[k][1][:]
+                else:
+                    z_codes, z_scales = z_early[g][0][:, part], z_early[g][1][:, part]
                 for n in range(N // P):
                     wo_codes, wo_scales = wo_q[g * N // P + n]
                     nc.tensor.matmul_mx(
-                        out=acc[half][n][:], lhsT=wo_codes.bitcast(FP8X4), lhsT_scale=wo_scales,
-                        rhs=z_codes.bitcast(FP8X4), rhs_scale=z_scales, start=(g == 0), stop=(g == GROUPS - 1),
+                        out=acc[k][n // 2][:, n % 2, :], lhsT=wo_codes.bitcast(FP8X4), lhsT_scale=wo_scales,
+                        rhs=z_codes.bitcast(FP8X4), rhs_scale=z_scales,
+                        start=(early == 0 and n % 2 == 0), stop=(g == last and n % 2 == 1),
                     )
 
-        for half in range(HALVES):
-            results = turn(("fine1", "step1")[half], [P, N // P, HALF], F32, 1)
-            for n in range(N // P):
-                copy = nc.vector.tensor_copy if n % 2 else nc.scalar.copy
-                copy(results[:, n, :], acc[half][n][:])
-                nc.sync.dma_start(out=out[n * P : (n + 1) * P, half * HALF : (half + 1) * HALF], in_=results[:, n, :])
+        for k, part in enumerate(PARTS):
+            for pair in range(2):
+                results = place(
+                    "results%d_%d" % (k, pair), [P, 2, part.stop - part.start], F32, AT_FINE + (2 * k + pair) * 2 * KIB
+                )
+                copy = nc.vector.tensor_copy if k == len(PARTS) - 1 and pair else nc.scalar.copy
+                copy(results[:], acc[k][pair][:])
+                rows = out[2 * pair * P : 2 * (pair + 1) * P, part].rearrange("(u p) m -> p u m", u=2)
+                nc.sync.dma_start(out=rows, in_=results[:])

@@ -20,6 +20,7 @@ ACT = mybir.ActivationFunctionType
 P = 128
 PACK = 4
 RUN = 4
+POOL_RUN = 8
 GROUP = P * PACK
 GROUPS = H // GROUP
 BANK = 512
@@ -169,11 +170,11 @@ def tile_list_mesh_block_refinement_kernel(
             codes, scales = quantized
             return [(codes[:, c : c + width], scales[:, c : c + width]) for c in range(0, codes.shape[1], width)]
 
-        def woven(grouped):
-            return grouped.rearrange("p (c i t) -> p c t i", i=4, t=PACK)
+        def woven(grouped, run=4):
+            return grouped.rearrange("p (c i t) -> p c t i", i=run, t=PACK)
 
-        def plain(planes):
-            return planes.rearrange("p t (c i) -> p c t i", i=4)
+        def plain(planes, run=4):
+            return planes.rearrange("p t (c i) -> p c t i", i=run)
 
         def round_wv(copy, grouped, g):
             copy(
@@ -183,11 +184,9 @@ def tile_list_mesh_block_refinement_kernel(
             return grouped
 
         def round_wo(grouped, raw, g):
-            planes = raw[:].rearrange("p t n -> p n t")
-            nc.gpsimd.tensor_tensor(
-                grouped.rearrange("p (n t) -> p n t", t=PACK), planes,
-                off_sign[:, g : g + 1, :].to_broadcast(list(planes.shape)), ALU.mult,
-            )
+            planes = plain(raw[:], POOL_RUN)
+            signs = off_sign[:, g : g + 1, :].unsqueeze(3).to_broadcast(list(planes.shape))
+            nc.gpsimd.tensor_tensor(woven(grouped, POOL_RUN), planes, signs, ALU.mult)
 
         freed = [list(range(SET)), list(range(SET, 2 * SET))]
         sets = []
@@ -293,10 +292,10 @@ def tile_list_mesh_block_refinement_kernel(
         wo_q = columns(quantize("wo01", wo_bf16[:], AT_WINDOWS + 7 * WINDOW), P)
         wv_slots = columns(quantize("wv0", wv_first[:]), P)
         least = [
-            place("least%d" % g, [P, PACK * M], F32, at) for g, at in enumerate((AT_WINDOWS + 5 * WINDOW, AT_WO_STAGE))
+            place("least%d" % g, [P, PACK, M], F32, at) for g, at in enumerate((AT_WINDOWS + 5 * WINDOW, AT_WO_STAGE))
         ]
         for g in (1, 0):
-            nc.vector.tensor_tensor(woven(least[g][:]), plain(picks[g][:]), plain(limits[g][:]), ALU.min)
+            nc.vector.tensor_tensor(least[g][:], picks[g][:], limits[g][:], ALU.min)
         room = place("wf_tail", [P, 5 * GROUP], U8, AT_RAW + 2 * PLANES)
         wf_slots.extend(reorder_weight(room, wf_last, wf_s, GROUPS - 1, 1, 4))
         wv_rest = place("wv_rest", [P, 2 * PACK * GROUP], BF16, AT_STAGE)
@@ -312,8 +311,8 @@ def tile_list_mesh_block_refinement_kernel(
             values = place("values%d" % g, [P, PACK, M], F32, (AT_PICKS, AT_TAB2 + T2)[g])
             pick(values[:], windows)
             nc.gpsimd.tensor_tensor(
-                stage[:, (g + 1) * unit : (g + 2) * unit].rearrange("p (m t) -> p m t", t=PACK),
-                values[:].rearrange("p t m -> p m t"), least[g][:].rearrange("p (m t) -> p m t", t=PACK), ALU.add,
+                woven(stage[:, (g + 1) * unit : (g + 2) * unit], POOL_RUN),
+                plain(values[:], POOL_RUN), plain(least[g][:], POOL_RUN), ALU.add,
             )
 
         windows = coarse("d", AT_WINDOWS + 8 * WINDOW, slope_jobs, last)

@@ -20,7 +20,6 @@ ACT = mybir.ActivationFunctionType
 P = 128
 PACK = 4
 RUN = 4
-POOL_RUN = 8
 GROUP = P * PACK
 GROUPS = H // GROUP
 BANK = 512
@@ -35,14 +34,17 @@ WF_ROW = 8
 KIB = 1024
 WINDOW = 4 * KIB
 PLANES = 8 * KIB
+EDGE = 64
 AT_WINDOWS = 0
 AT_TAB = AT_WINDOWS + 12 * WINDOW
 AT_TAB2 = AT_TAB + 4 * WINDOW
 AT_RAW = AT_TAB2 + PLANES + T2
-AT_PICKS = AT_RAW + 5 * PLANES
+AT_VALUES = AT_RAW + 4 * PLANES
+AT_PICKS = AT_VALUES + 4 * WINDOW
 AT_FINE = AT_PICKS + PLANES
 AT_WO_STAGE = AT_FINE + 2 * PLANES
 AT_STAGE = AT_WO_STAGE + PLANES
+AT_WOVEN = AT_STAGE + 3 * WINDOW
 
 
 def tile_list_mesh_block_refinement_kernel(
@@ -77,8 +79,8 @@ def tile_list_mesh_block_refinement_kernel(
         tab2_s = place("tab2_s", [P, T2], U8, AT_TAB2 + PLANES)
         ws_s = held("ws_s", [P, H], U8)
         wf_s = held("wf_s", [P, H], U8)
-        off_rows = held("off_rows", [P, GROUP], F32)
-        off_slots = held("off_slots", [P, GROUP], F32)
+        off_rows = place("off_rows", [P, GROUP], F32, AT_FINE)
+        off_slots = place("off_slots", [P, GROUP], F32, AT_FINE + 2 * KIB)
         off_col = held("off_col", [P, GROUPS, PACK], F32)
         off_size = held("off_size", [P, GROUPS, PACK], F32)
         off_twice = held("off_twice", [P, GROUPS, PACK], F32)
@@ -104,11 +106,8 @@ def tile_list_mesh_block_refinement_kernel(
             nc.sync.dma_start(out=raw[:].bitcast(I32), in_=rows[:, first * n : (first + count) * n])
             return raw
 
-        def load_wv(g, raw):
-            nc.sync.dma_start(
-                out=raw,
-                in_=wv[:, g * GROUP : (g + 1) * GROUP].rearrange("(p j) r -> p j r", j=PACK),
-            )
+        def load_wv(first, width, raw):
+            nc.sync.dma_start(out=raw, in_=wv[:, first : first + width].rearrange("(p j) r -> p j r", j=PACK))
             return raw
 
         def load_wo(g, at):
@@ -136,11 +135,13 @@ def tile_list_mesh_block_refinement_kernel(
             in_=tab2_words[0].rearrange("p t i -> p (t i)").bitcast(I32),
         )
         nc.sync.dma_start(idx2[:], offs2)
-        wo_raw.append(load_wo(1, AT_RAW + 2 * PLANES))
+        wo_raw.append(load_wo(1, AT_RAW + PLANES))
+        wv_head = load_wv(0, GROUP, place("wv_head", [P, PACK, GROUP], F32, AT_STAGE + WINDOW)[:])
         wf_last = load_words("wf_last", wf_rows, GROUPS - 1, 1)
-        wv_raw = [load_wv(0, place("wv_raw0", [P, PACK, GROUP], F32, AT_RAW + PLANES)[:])]
-        both = place("wv_raw12", [P, 2, PACK, GROUP], F32, AT_RAW + 3 * PLANES)
-        wv_raw.extend(load_wv(g, both[:, g - 1]) for g in (1, 2))
+        wide = place("wv_end", [P, PACK * GROUP + 2 * EDGE // 4], F32, AT_VALUES + WINDOW - EDGE)
+        wv_end = load_wv(H - GROUP // 2, GROUP // 2, wide[:, : PACK * GROUP // 2].rearrange("p (j r) -> p j r", j=PACK))
+        both = place("wv_middle", [P, 2, PACK, GROUP], F32, AT_RAW + 2 * PLANES)
+        wv_middle = [load_wv(GROUP, GROUP, both[:, 0]), load_wv(2 * GROUP, GROUP // 2, both[:, 1, :, : GROUP // 2])]
 
         def reorder(dst, src, count, bytes_per_col):
             w = RUN * bytes_per_col // 4
@@ -158,11 +159,10 @@ def tile_list_mesh_block_refinement_kernel(
                 (words[:, bytes_per_col * c : bytes_per_col * (c + P)], scales[:, c : c + P]) for c in range(0, n, P)
             ]
 
-        def quantize(name, grouped, at=None):
+        def quantize(name, grouped):
             width = grouped.shape[1] // PACK
             codes = held(name + "_codes", [P, width], U32)
-            shape = [P, width]
-            scales = held(name + "_scales", shape, U8) if at is None else place(name + "_scales", shape, U8, at)
+            scales = held(name + "_scales", [P, width], U8)
             nc.vector.quantize_mx(out=codes[:].bitcast(FP8X4), scales=scales[:], in_=grouped)
             return codes, scales
 
@@ -170,23 +170,36 @@ def tile_list_mesh_block_refinement_kernel(
             codes, scales = quantized
             return [(codes[:, c : c + width], scales[:, c : c + width]) for c in range(0, codes.shape[1], width)]
 
-        def woven(grouped, run=4):
-            return grouped.rearrange("p (c i t) -> p c t i", i=run, t=PACK)
+        def woven(grouped):
+            return grouped.rearrange("p (c i t) -> p c t i", i=4, t=PACK)
 
-        def plain(planes, run=4):
-            return planes.rearrange("p t (c i) -> p c t i", i=run)
+        def plain(planes):
+            return planes.rearrange("p t (c i) -> p c t i", i=4)
 
-        def round_wv(copy, grouped, g):
-            copy(
-                grouped.rearrange("p (t c i j) -> p t c j i", t=PACK, i=RUN, j=PACK),
-                wv_raw[g].rearrange("p j (c t i) -> p t c j i", t=PACK, i=RUN),
+        def paired(pairs):
+            return pairs.rearrange("p (u n e) -> p u e n", u=2, e=2)
+
+        def by_pairs(planes):
+            return planes.rearrange("p (u e) n -> p u e n", u=2)
+
+        def weave(grouped, pairs):
+            nc.scalar.copy(
+                grouped.bitcast(U32).rearrange("p (n u) -> p n u", u=2),
+                pairs.bitcast(U32).rearrange("p (u n) -> p n u", u=2),
             )
-            return grouped
 
-        def round_wo(grouped, raw, g):
-            planes = plain(raw[:], POOL_RUN)
-            signs = off_sign[:, g : g + 1, :].unsqueeze(3).to_broadcast(list(planes.shape))
-            nc.gpsimd.tensor_tensor(woven(grouped, POOL_RUN), planes, signs, ALU.mult)
+        def wv_views(grouped, raw, slots, runs):
+            dst = grouped.rearrange("p (t c i j) -> p t c i j", t=PACK, i=RUN, j=PACK)[:, slots, runs]
+            src = raw.rearrange("p j (c t i) -> p t c i j", t=PACK, i=RUN)[:, slots]
+            return dst, src
+
+        def round_wv(copy, grouped, raw, slots=slice(0, PACK), runs=slice(0, P // RUN)):
+            copy(*[view.rearrange("p t c i j -> p t c j i") for view in wv_views(grouped, raw, slots, runs)])
+
+        def round_wo(pairs, g):
+            planes = by_pairs(wo_raw[g][:])
+            signs = off_sign[:, g, :].rearrange("p (u e) -> p u e", u=2).unsqueeze(3).to_broadcast(list(planes.shape))
+            nc.gpsimd.tensor_tensor(paired(pairs), planes, signs, ALU.mult)
 
         freed = [list(range(SET)), list(range(SET, 2 * SET))]
         sets = []
@@ -253,12 +266,12 @@ def tile_list_mesh_block_refinement_kernel(
         nc.vector.tensor_scalar(off_twice[:], off_col[:], 0.0, 2.0, ALU.is_ge, ALU.mult)
         nc.gpsimd.tensor_scalar(off_sign[:], off_twice[:], 1.0, -1.0, ALU.mult, ALU.add)
 
-        v_s = held("v_s", [P, S], U8)
+        v_s = place("v_s", [P, S], U8, AT_WOVEN + 2 * PLANES)
         nc.vector.tensor_copy(v_s[:], tab_s[:].indirect(idx[:]))
         ws_slots = reorder_weight(held("ws_head", [P, 3 * GROUP], U8), ws_first, ws_s, 0, 1, 2)
         v_w = []
         for half in range(S // BANK):
-            words = held("v_w%d" % half, [P, BANK], U32)
+            words = place("v_w%d" % half, [P, BANK], U32, AT_WOVEN + half * PLANES)
             part = slice(half * BANK // 16, (half + 1) * BANK // 16)
             nc.vector.tensor_copy(words[:], tab_w[:].indirect(idx[:, part]))
             v_w.append(words)
@@ -266,9 +279,13 @@ def tile_list_mesh_block_refinement_kernel(
         ws_slots.extend(reorder_weight(held("ws_tail", [P, 6 * GROUP], U8), ws_rest, ws_s, 1, GROUPS - 1, 2))
 
         unit = PACK * M
-        wo_bf16 = place("wo_bf16", [P, 2 * unit], BF16, AT_WO_STAGE)
+        wo_pairs = place("wo_pairs", [P, 2 * unit], BF16, AT_WO_STAGE)
         for g in range(2):
-            round_wo(wo_bf16[:, g * unit : (g + 1) * unit], wo_raw[g], g)
+            round_wo(wo_pairs[:, g * unit : (g + 1) * unit], g)
+        wv_first = place("wv_first", [P, unit], BF16, AT_RAW)
+        views = wv_views(wv_first[:], wv_head, slice(0, PACK - 1), slice(0, P // RUN))
+        dst, src = [view.rearrange("p t c i j -> p c t i j") for view in views]
+        nc.gpsimd.tensor_scalar(dst, src, 1.0, 0.0, ALU.mult, ALU.add)
 
         picks = [place("picks%d" % g, [P, PACK, M], F32, at) for g, at in enumerate((AT_PICKS, AT_TAB2 + T2))]
         limits = [place("limits%d" % g, [P, PACK, M], F32, AT_FINE + g * PLANES) for g in range(2)]
@@ -286,43 +303,45 @@ def tile_list_mesh_block_refinement_kernel(
         for g in range(2):
             fine(limits[g][:], g)
 
-        wv_first = place("wv_first", [P, PACK * GROUP], BF16, AT_WINDOWS + 6 * WINDOW)
-        round_wv(nc.vector.tensor_copy, wv_first[:], 0)
-        wo_raw.append(load_wo(2, AT_RAW + PLANES))
-        wo_q = columns(quantize("wo01", wo_bf16[:], AT_WINDOWS + 7 * WINDOW), P)
-        wv_slots = columns(quantize("wv0", wv_first[:]), P)
-        least = [
-            place("least%d" % g, [P, PACK, M], F32, at) for g, at in enumerate((AT_WINDOWS + 5 * WINDOW, AT_WO_STAGE))
-        ]
-        for g in (1, 0):
-            nc.vector.tensor_tensor(least[g][:], picks[g][:], limits[g][:], ALU.min)
-        room = place("wf_tail", [P, 5 * GROUP], U8, AT_RAW + 2 * PLANES)
+        wo_raw.append(load_wo(2, AT_WINDOWS + 4 * WINDOW))
+        wv_rest = place("wv_rest", [P, 2 * unit], BF16, AT_WINDOWS + 6 * WINDOW)
+        middle = P // RUN // 2
+        round_wv(nc.scalar.copy, wv_rest[:, unit:], wv_end, runs=slice(middle, 2 * middle))
+        round_wv(nc.vector.tensor_copy, wv_first[:], wv_head, slots=slice(PACK - 1, PACK))
+        room = place("wf_tail", [P, 5 * GROUP], U8, AT_RAW + PLANES)
         wf_slots.extend(reorder_weight(room, wf_last, wf_s, GROUPS - 1, 1, 4))
-        wv_rest = place("wv_rest", [P, 2 * PACK * GROUP], BF16, AT_STAGE)
-        for g in (1, 2):
-            round_wv(nc.scalar.copy, wv_rest[:, (g - 1) * PACK * GROUP : g * PACK * GROUP], g)
-        wv_slots.extend(columns(quantize("wv12", wv_rest[:]), P))
+        wv_slots = columns(quantize("wv0", wv_first[:]), P)
+        round_wv(nc.vector.tensor_copy, wv_rest[:, :unit], wv_middle[0])
+        round_wv(nc.vector.tensor_copy, wv_rest[:, unit:], wv_middle[1], runs=slice(0, middle))
+        least = {}
+        for g in (1, 0):
+            wv_slots.extend(columns(quantize("wv%d" % (2 - g), wv_rest[:, (1 - g) * unit : (2 - g) * unit]), P))
+            least[g] = place("least%d" % g, [P, PACK, M], F32, AT_RAW + (2 + g) * PLANES)
+            nc.vector.tensor_tensor(least[g][:], picks[g][:], limits[g][:], ALU.min)
 
         last = GROUPS - 1
-        stage = place("stage", [P, GROUPS * unit], BF16, AT_STAGE)
-        round_wo(stage[:, :unit], wo_raw[last], last)
+        stage = place("stage", [P, GROUPS * unit], BF16, AT_FINE)
+        round_wo(stage[:, :unit], last)
         for g in range(2):
-            windows = coarse("h", (AT_RAW + 3 * PLANES, AT_WINDOWS)[g], value_jobs, g)
+            windows = coarse("h", (AT_VALUES, AT_WINDOWS)[g], value_jobs, g)
             values = place("values%d" % g, [P, PACK, M], F32, (AT_PICKS, AT_TAB2 + T2)[g])
             pick(values[:], windows)
             nc.gpsimd.tensor_tensor(
-                woven(stage[:, (g + 1) * unit : (g + 2) * unit], POOL_RUN),
-                plain(values[:], POOL_RUN), plain(least[g][:], POOL_RUN), ALU.add,
+                paired(stage[:, (g + 1) * unit : (g + 2) * unit]), by_pairs(values[:]), by_pairs(least[g][:]), ALU.add
             )
 
         windows = coarse("d", AT_WINDOWS + 8 * WINDOW, slope_jobs, last)
-        picks = place("picks2", [P, PACK, M], F32, AT_FINE)
+        picks = place("picks2", [P, PACK, M], F32, AT_STAGE + WINDOW)
         pick(picks[:], windows)
         windows = coarse("h", AT_TAB, value_jobs, last)
-        limits = place("limits2", [P, PACK, M], F32, AT_FINE + PLANES)
+        limits = place("limits2", [P, PACK, M], F32, AT_RAW)
         fine(limits[:], last)
-        both = columns(quantize("stage_a", stage[:, : 2 * unit], AT_WINDOWS + 10 * WINDOW), M)
-        wo_q.extend(columns(both[0], P))
+        ready = []
+        for k, pairs in enumerate((wo_pairs[:], stage[:, : 2 * unit], stage[:, 2 * unit :])):
+            grouped = place("woven%d" % k, list(pairs.shape), BF16, AT_WOVEN + k * PLANES)
+            for c in range(0, pairs.shape[1], unit):
+                weave(grouped[:, c : c + unit], pairs[:, c : c + unit])
+            ready.append(grouped[:])
         steps = place("steps2", [P, PACK, M], F32, AT_WINDOWS + 5 * WINDOW)
         for side in (slice(0, HALF), slice(HALF, M)):
             nc.vector.tensor_tensor(steps[:, :, side], picks[:, :, side], limits[:, :, side], ALU.min)
@@ -335,8 +354,12 @@ def tile_list_mesh_block_refinement_kernel(
             for t in range(PACK):
                 nc.vector.tensor_tensor(planes[:, t, :], windows[t][:].indirect(offsets), steps[:, t, part], ALU.add)
             if k == 0:
-                z_early = [both[1], quantize("stage_b", stage[:, 2 * unit :], AT_WINDOWS + 11 * WINDOW)]
+                wo_q = columns(quantize("wo01", ready[0]), P)
+                both = columns(quantize("wo2_z0", ready[1]), M)
+                wo_q.extend(columns(both[0], P))
             else:
+                if k == 1:
+                    z_early = [both[1], quantize("z1", ready[2])]
                 z_last.append(quantize("z2_%d" % (k - 1), waiting[-1]))
             rounded = held("z2_bf16_%d" % k, [P, PACK * width], BF16)
             copy = nc.vector.tensor_copy if k == len(PARTS) - 1 else nc.scalar.copy
@@ -349,7 +372,7 @@ def tile_list_mesh_block_refinement_kernel(
             [psum.tile([P, 2, part.stop - part.start], F32, name="bank%d" % numbers[2 * k + pair]) for pair in range(2)]
             for k, part in enumerate(PARTS)
         ]
-        for early, g in enumerate((1, 0, last)):
+        for g in range(GROUPS):
             for k, part in enumerate(PARTS):
                 if g == last:
                     z_codes, z_scales = z_last[k][0][:], z_last[k][1][:]
@@ -360,13 +383,13 @@ def tile_list_mesh_block_refinement_kernel(
                     nc.tensor.matmul_mx(
                         out=acc[k][n // 2][:, n % 2, :], lhsT=wo_codes.bitcast(FP8X4), lhsT_scale=wo_scales,
                         rhs=z_codes.bitcast(FP8X4), rhs_scale=z_scales,
-                        start=(early == 0 and n % 2 == 0), stop=(g == last and n % 2 == 1),
+                        start=(g == 0 and n % 2 == 0), stop=(g == last and n % 2 == 1),
                     )
 
         for k, part in enumerate(PARTS):
             for pair in range(2):
                 results = place(
-                    "results%d_%d" % (k, pair), [P, 2, part.stop - part.start], F32, AT_FINE + (2 * k + pair) * 2 * KIB
+                    "results%d_%d" % (k, pair), [P, 2, part.stop - part.start], F32, AT_STAGE + (2 * k + pair) * 2 * KIB
                 )
                 copy = nc.vector.tensor_copy if k == len(PARTS) - 1 and pair else nc.scalar.copy
                 copy(results[:], acc[k][pair][:])

@@ -35,6 +35,7 @@ KIB = 1024
 WINDOW = 4 * KIB
 PLANES = 8 * KIB
 EDGE = 64
+SHARE = 128
 AT_WINDOWS = 0
 AT_TAB = AT_WINDOWS + 12 * WINDOW
 AT_TAB2 = AT_TAB + 4 * WINDOW
@@ -197,9 +198,10 @@ def tile_list_mesh_block_refinement_kernel(
             copy(*[view.rearrange("p t c i j -> p t c j i") for view in wv_views(grouped, raw, slots, runs)])
 
         def round_wo(pairs, g):
-            planes = by_pairs(wo_raw[g][:])
-            signs = off_sign[:, g, :].rearrange("p (u e) -> p u e", u=2).unsqueeze(3).to_broadcast(list(planes.shape))
-            nc.gpsimd.tensor_tensor(paired(pairs), planes, signs, ALU.mult)
+            for t in range(PACK):
+                nc.gpsimd.tensor_scalar(
+                    paired(pairs)[:, t // 2, t % 2], wo_raw[g][:, t, :], off_sign[:, g, t : t + 1], 0.0, ALU.mult, ALU.add
+                )
 
         freed = [list(range(SET)), list(range(SET, 2 * SET))]
         sets = []
@@ -326,8 +328,10 @@ def tile_list_mesh_block_refinement_kernel(
             windows = coarse("h", (AT_VALUES, AT_WINDOWS)[g], value_jobs, g)
             values = place("values%d" % g, [P, PACK, M], F32, (AT_PICKS, AT_TAB2 + T2)[g])
             pick(values[:], windows)
+            width = M - g * SHARE
             nc.gpsimd.tensor_tensor(
-                paired(stage[:, (g + 1) * unit : (g + 2) * unit]), by_pairs(values[:]), by_pairs(least[g][:]), ALU.add
+                paired(stage[:, (g + 1) * unit : (g + 1) * unit + PACK * width]),
+                by_pairs(values[:, :, :width]), by_pairs(least[g][:, :, :width]), ALU.add,
             )
 
         windows = coarse("d", AT_WINDOWS + 8 * WINDOW, slope_jobs, last)
@@ -337,14 +341,22 @@ def tile_list_mesh_block_refinement_kernel(
         limits = place("limits2", [P, PACK, M], F32, AT_RAW)
         fine(limits[:], last)
         ready = []
-        for k, pairs in enumerate((wo_pairs[:], stage[:, : 2 * unit], stage[:, 2 * unit :])):
+        for k, pairs in enumerate((wo_pairs[:], stage[:, : 2 * unit])):
             grouped = place("woven%d" % k, list(pairs.shape), BF16, AT_WOVEN + k * PLANES)
             for c in range(0, pairs.shape[1], unit):
                 weave(grouped[:, c : c + unit], pairs[:, c : c + unit])
             ready.append(grouped[:])
+        grouped = place("woven2", [P, unit], BF16, AT_WOVEN + 2 * PLANES)
+        width = M - SHARE
+        weave(grouped[:, : PACK * width], stage[:, 2 * unit : 2 * unit + PACK * width])
+        ready.append(grouped[:])
         steps = place("steps2", [P, PACK, M], F32, AT_WINDOWS + 5 * WINDOW)
         for side in (slice(0, HALF), slice(HALF, M)):
             nc.vector.tensor_tensor(steps[:, :, side], picks[:, :, side], limits[:, :, side], ALU.min)
+
+        nc.vector.tensor_tensor(
+            woven(grouped[:, PACK * width :]), plain(values[:, :, width:]), plain(least[1][:, :, width:]), ALU.add
+        )
 
         z_last, waiting = [], []
         for k, part in enumerate(PARTS):

@@ -34,8 +34,7 @@ WF_ROW = 8
 KIB = 1024
 WINDOW = 4 * KIB
 PLANES = 8 * KIB
-EDGE = 64
-SHARE = 128
+LENT = 2
 AT_WINDOWS = 0
 AT_TAB = AT_WINDOWS + 12 * WINDOW
 AT_TAB2 = AT_TAB + 4 * WINDOW
@@ -126,6 +125,7 @@ def tile_list_mesh_block_refinement_kernel(
         load_scales(ws_s, ws_scales, 0, nc.sync)
         nc.sync.dma_start(out=tab_w[:, TAB_LAST:].bitcast(I32), in_=tab_rows[:, TAB_LAST:])
         nc.scalar.dma_start(out=off_rows[0:GROUPS, :], in_=off.rearrange("(g r) -> g r", g=GROUPS))
+        nc.sync.dma_start(idx2[:], offs2)
         wf_first = load_words("wf_first", wf_rows, 0, GROUPS - 1, AT_WO_STAGE)
         load_scales(wf_s, wf_scales, WF_ROW, nc.sync)
         ws_rest = load_words("ws_rest", ws_rows, 1, GROUPS - 1, AT_WO_STAGE + WINDOW)
@@ -135,14 +135,11 @@ def tile_list_mesh_block_refinement_kernel(
             out=tab2_w[:].bitcast(I32),
             in_=tab2_words[0].rearrange("p t i -> p (t i)").bitcast(I32),
         )
-        nc.sync.dma_start(idx2[:], offs2)
         wo_raw.append(load_wo(1, AT_RAW + PLANES))
         wv_head = load_wv(0, GROUP, place("wv_head", [P, PACK, GROUP], F32, AT_STAGE + WINDOW)[:])
         wf_last = load_words("wf_last", wf_rows, GROUPS - 1, 1)
-        wide = place("wv_end", [P, PACK * GROUP + 2 * EDGE // 4], F32, AT_VALUES + WINDOW - EDGE)
-        wv_end = load_wv(H - GROUP // 2, GROUP // 2, wide[:, : PACK * GROUP // 2].rearrange("p (j r) -> p j r", j=PACK))
         both = place("wv_middle", [P, 2, PACK, GROUP], F32, AT_RAW + 2 * PLANES)
-        wv_middle = [load_wv(GROUP, GROUP, both[:, 0]), load_wv(2 * GROUP, GROUP // 2, both[:, 1, :, : GROUP // 2])]
+        wv_middle = [load_wv(g * GROUP, GROUP, both[:, g - 1]) for g in (1, 2)]
 
         def reorder(dst, src, count, bytes_per_col):
             w = RUN * bytes_per_col // 4
@@ -189,13 +186,13 @@ def tile_list_mesh_block_refinement_kernel(
                 pairs.bitcast(U32).rearrange("p (u n) -> p n u", u=2),
             )
 
-        def wv_views(grouped, raw, slots, runs):
-            dst = grouped.rearrange("p (t c i j) -> p t c i j", t=PACK, i=RUN, j=PACK)[:, slots, runs]
+        def wv_views(grouped, raw, slots):
+            dst = grouped.rearrange("p (t c i j) -> p t c i j", t=PACK, i=RUN, j=PACK)[:, slots]
             src = raw.rearrange("p j (c t i) -> p t c i j", t=PACK, i=RUN)[:, slots]
             return dst, src
 
-        def round_wv(copy, grouped, raw, slots=slice(0, PACK), runs=slice(0, P // RUN)):
-            copy(*[view.rearrange("p t c i j -> p t c j i") for view in wv_views(grouped, raw, slots, runs)])
+        def round_wv(copy, grouped, raw, slots=slice(0, PACK)):
+            copy(*[view.rearrange("p t c i j -> p t c j i") for view in wv_views(grouped, raw, slots)])
 
         def round_wo(pairs, g):
             for t in range(PACK):
@@ -206,7 +203,7 @@ def tile_list_mesh_block_refinement_kernel(
         freed = [list(range(SET)), list(range(SET, 2 * SET))]
         sets = []
 
-        def through_banks(jobs, backwards=True):
+        def through_banks(jobs, backwards=True, lent=0):
             side = len(sets) % 2
             sets.append(side)
             order = list(reversed(jobs)) if backwards else jobs
@@ -220,8 +217,11 @@ def tile_list_mesh_block_refinement_kernel(
             if backwards:
                 banks.reverse()
                 freed[side].reverse()
-            for bank, job in zip(banks, jobs):
-                nc.scalar.activation(out=job[0], in_=bank[:], func=job[1], scale=job[2])
+            for k, (bank, job) in enumerate(zip(banks, jobs)):
+                if k < len(jobs) - lent:
+                    nc.scalar.activation(out=job[0], in_=bank[:], func=job[1], scale=job[2])
+                else:
+                    nc.vector.tensor_scalar(job[0], bank[:], job[2], 0.0, ALU.mult, ALU.add)
 
         cols = [slice(half * BANK, (half + 1) * BANK) for half in range(S // BANK)]
 
@@ -239,10 +239,10 @@ def tile_list_mesh_block_refinement_kernel(
             codes, scales = wv_slots[PACK * g + t]
             return coarse_jobs(window, ACT.Copy, off_sign[:, g, t : t + 1], codes.bitcast(FP8X4), scales)
 
-        def coarse(name, at, jobs, g):
+        def coarse(name, at, jobs, g, lent=0):
             windows = [place("%s%d_%d" % (name, g, t), [P, S], F32, at + t * WINDOW) for t in range(PACK)]
             for t in range(0, PACK, 2):
-                through_banks(jobs(windows[t], g, t) + jobs(windows[t + 1], g, t + 1))
+                through_banks(jobs(windows[t], g, t) + jobs(windows[t + 1], g, t + 1), lent=lent if t else 0)
             return windows
 
         def pick(planes, windows):
@@ -271,6 +271,8 @@ def tile_list_mesh_block_refinement_kernel(
         v_s = place("v_s", [P, S], U8, AT_WOVEN + 2 * PLANES)
         nc.vector.tensor_copy(v_s[:], tab_s[:].indirect(idx[:]))
         ws_slots = reorder_weight(held("ws_head", [P, 3 * GROUP], U8), ws_first, ws_s, 0, 1, 2)
+        v2_s = held("v2_s", [P, M], U8)
+        nc.vector.tensor_copy(v2_s[:], tab2_s[:].indirect(idx2[:]))
         v_w = []
         for half in range(S // BANK):
             words = place("v_w%d" % half, [P, BANK], U32, AT_WOVEN + half * PLANES)
@@ -285,7 +287,7 @@ def tile_list_mesh_block_refinement_kernel(
         for g in range(2):
             round_wo(wo_pairs[:, g * unit : (g + 1) * unit], g)
         wv_first = place("wv_first", [P, unit], BF16, AT_RAW)
-        views = wv_views(wv_first[:], wv_head, slice(0, PACK - 1), slice(0, P // RUN))
+        views = wv_views(wv_first[:], wv_head, slice(0, PACK))
         dst, src = [view.rearrange("p t c i j -> p c t i j") for view in views]
         nc.gpsimd.tensor_scalar(dst, src, 1.0, 0.0, ALU.mult, ALU.add)
 
@@ -296,25 +298,20 @@ def tile_list_mesh_block_refinement_kernel(
         through_banks([jobs[0][0], jobs[1][0], jobs[0][1], jobs[1][1]], backwards=False)
         through_banks(jobs[2] + jobs[3])
         pick(picks[0][:], windows)
-        v2_s = held("v2_s", [P, M], U8)
         v2_w = held("v2_w", [P, M], U32)
         windows = coarse("d", AT_WINDOWS + 4 * WINDOW, slope_jobs, 1)
         nc.vector.tensor_copy(v2_w[:], tab2_w[:].indirect(idx2[:]))
-        nc.vector.tensor_copy(v2_s[:], tab2_s[:].indirect(idx2[:]))
         pick(picks[1][:], windows)
         for g in range(2):
             fine(limits[g][:], g)
 
         wo_raw.append(load_wo(2, AT_WINDOWS + 4 * WINDOW))
         wv_rest = place("wv_rest", [P, 2 * unit], BF16, AT_WINDOWS + 6 * WINDOW)
-        middle = P // RUN // 2
-        round_wv(nc.scalar.copy, wv_rest[:, unit:], wv_end, runs=slice(middle, 2 * middle))
-        round_wv(nc.vector.tensor_copy, wv_first[:], wv_head, slots=slice(PACK - 1, PACK))
         room = place("wf_tail", [P, 5 * GROUP], U8, AT_RAW + PLANES)
         wf_slots.extend(reorder_weight(room, wf_last, wf_s, GROUPS - 1, 1, 4))
         wv_slots = columns(quantize("wv0", wv_first[:]), P)
         round_wv(nc.vector.tensor_copy, wv_rest[:, :unit], wv_middle[0])
-        round_wv(nc.vector.tensor_copy, wv_rest[:, unit:], wv_middle[1], runs=slice(0, middle))
+        round_wv(nc.vector.tensor_copy, wv_rest[:, unit:], wv_middle[1])
         least = {}
         for g in (1, 0):
             wv_slots.extend(columns(quantize("wv%d" % (2 - g), wv_rest[:, (1 - g) * unit : (2 - g) * unit]), P))
@@ -328,36 +325,33 @@ def tile_list_mesh_block_refinement_kernel(
             windows = coarse("h", (AT_VALUES, AT_WINDOWS)[g], value_jobs, g)
             values = place("values%d" % g, [P, PACK, M], F32, (AT_PICKS, AT_TAB2 + T2)[g])
             pick(values[:], windows)
-            width = M - g * SHARE
             nc.gpsimd.tensor_tensor(
-                paired(stage[:, (g + 1) * unit : (g + 1) * unit + PACK * width]),
-                by_pairs(values[:, :, :width]), by_pairs(least[g][:, :, :width]), ALU.add,
+                paired(stage[:, (g + 1) * unit : (g + 2) * unit]), by_pairs(values[:]), by_pairs(least[g][:]), ALU.add
             )
 
         windows = coarse("d", AT_WINDOWS + 8 * WINDOW, slope_jobs, last)
         picks = place("picks2", [P, PACK, M], F32, AT_STAGE + WINDOW)
         pick(picks[:], windows)
-        windows = coarse("h", AT_TAB, value_jobs, last)
+        windows = coarse("h", AT_TAB, value_jobs, last, LENT)
         limits = place("limits2", [P, PACK, M], F32, AT_RAW)
         fine(limits[:], last)
+        sources = (
+            (wo_pairs[:, :unit], stage[:, unit : 2 * unit]),
+            (wo_pairs[:, unit:], stage[:, 2 * unit :]),
+            (stage[:, :unit],),
+        )
         ready = []
-        for k, pairs in enumerate((wo_pairs[:], stage[:, : 2 * unit])):
-            grouped = place("woven%d" % k, list(pairs.shape), BF16, AT_WOVEN + k * PLANES)
-            for c in range(0, pairs.shape[1], unit):
-                weave(grouped[:, c : c + unit], pairs[:, c : c + unit])
+        for k, pieces in enumerate(sources):
+            grouped = place("woven%d" % k, [P, len(pieces) * unit], BF16, AT_WOVEN + k * PLANES)
+            for c, pairs in enumerate(pieces):
+                weave(grouped[:, c * unit : (c + 1) * unit], pairs)
             ready.append(grouped[:])
-        grouped = place("woven2", [P, unit], BF16, AT_WOVEN + 2 * PLANES)
-        width = M - SHARE
-        weave(grouped[:, : PACK * width], stage[:, 2 * unit : 2 * unit + PACK * width])
-        ready.append(grouped[:])
         steps = place("steps2", [P, PACK, M], F32, AT_WINDOWS + 5 * WINDOW)
         for side in (slice(0, HALF), slice(HALF, M)):
             nc.vector.tensor_tensor(steps[:, :, side], picks[:, :, side], limits[:, :, side], ALU.min)
 
-        nc.vector.tensor_tensor(
-            woven(grouped[:, PACK * width :]), plain(values[:, :, width:]), plain(least[1][:, :, width:]), ALU.add
-        )
 
+        early = [columns(quantize("wo0_z0", ready[0]), M)]
         z_last, waiting = [], []
         for k, part in enumerate(PARTS):
             width = part.stop - part.start
@@ -365,13 +359,9 @@ def tile_list_mesh_block_refinement_kernel(
             offsets = p1[:, part.start // 16 : part.stop // 16]
             for t in range(PACK):
                 nc.vector.tensor_tensor(planes[:, t, :], windows[t][:].indirect(offsets), steps[:, t, part], ALU.add)
-            if k == 0:
-                wo_q = columns(quantize("wo01", ready[0]), P)
-                both = columns(quantize("wo2_z0", ready[1]), M)
-                wo_q.extend(columns(both[0], P))
-            else:
-                if k == 1:
-                    z_early = [both[1], quantize("z1", ready[2])]
+            if k < last:
+                early.append(columns(quantize("early%d" % k, ready[k + 1]), M))
+            if k > 0:
                 z_last.append(quantize("z2_%d" % (k - 1), waiting[-1]))
             rounded = held("z2_bf16_%d" % k, [P, PACK * width], BF16)
             copy = nc.vector.tensor_copy if k == len(PARTS) - 1 else nc.scalar.copy
@@ -389,9 +379,9 @@ def tile_list_mesh_block_refinement_kernel(
                 if g == last:
                     z_codes, z_scales = z_last[k][0][:], z_last[k][1][:]
                 else:
-                    z_codes, z_scales = z_early[g][0][:, part], z_early[g][1][:, part]
+                    z_codes, z_scales = early[g][1][0][:, part], early[g][1][1][:, part]
                 for n in range(N // P):
-                    wo_codes, wo_scales = wo_q[g * N // P + n]
+                    wo_codes, wo_scales = columns(early[g][0], P)[n]
                     nc.tensor.matmul_mx(
                         out=acc[k][n // 2][:, n % 2, :], lhsT=wo_codes.bitcast(FP8X4), lhsT_scale=wo_scales,
                         rhs=z_codes.bitcast(FP8X4), rhs_scale=z_scales,

@@ -22,29 +22,34 @@ PACK = 4
 RUN = 4
 GROUP = P * PACK
 GROUPS = H // GROUP
+LAST = GROUPS - 1
 BANK = 512
 SET = 4
-HALF = M // 2
-PARTS = (slice(0, HALF), slice(HALF, HALF + P), slice(HALF + P, M))
+UNIT = PACK * M
+PARTS = (slice(0, M // 2), slice(M // 2, M // 2 + P), slice(M // 2 + P, M))
 TAB_FIRST = T // 4
 TAB_LAST = T - T // 4
 TAB2_ROW = 4
 WF_ROW = 8
+RING = 11
 
 KIB = 1024
 WINDOW = 4 * KIB
 PLANES = 8 * KIB
-LENT = 2
-AT_WINDOWS = 0
-AT_TAB = AT_WINDOWS + 12 * WINDOW
-AT_TAB2 = AT_TAB + 4 * WINDOW
-AT_RAW = AT_TAB2 + PLANES + T2
-AT_VALUES = AT_RAW + 4 * PLANES
-AT_PICKS = AT_VALUES + 4 * WINDOW
-AT_FINE = AT_PICKS + PLANES
-AT_WO_STAGE = AT_FINE + 2 * PLANES
-AT_STAGE = AT_WO_STAGE + PLANES
-AT_WOVEN = AT_STAGE + 3 * WINDOW
+LAP = KIB // 2
+AT_TAB = 0
+AT_WO = AT_TAB + 2 * PLANES
+AT_TAB2 = AT_WO + GROUPS * PLANES
+AT_WF = AT_TAB2 + PLANES
+AT_FIRST = AT_WF + 5 * LAST * GROUP - LAP
+AT_WV = AT_FIRST + WINDOW - LAP
+AT_RING = AT_WV + 2 * LAST * UNIT
+AT_PAIRS = AT_RING + (RING - 1) * WINDOW
+AT_LIMITS = AT_PAIRS + LAST * WINDOW
+AT_WOVEN = AT_LIMITS + LAST * PLANES
+AT_WV_LAST = AT_WOVEN + 5 * WINDOW
+AT_WV_RAW = AT_WV_LAST + WINDOW
+AT_PICKS = AT_WV_RAW + PLANES
 
 
 def tile_list_mesh_block_refinement_kernel(
@@ -63,12 +68,7 @@ def tile_list_mesh_block_refinement_kernel(
         def place(name, shape, dtype, at):
             return laid.tile(shape, dtype, name=name, align_bytes=64, offset=at)
 
-        def load_scales(plane, scales, row, queue):
-            for r in range(4):
-                queue.dma_start(
-                    out=plane[row + r : P : 32, :].bitcast(I32),
-                    in_=scales[0, r : 16 : 4, :].bitcast(I32),
-                )
+        banks = [psum.tile([P, BANK], F32, name="bank%d" % b) for b in range(2 * SET)]
 
         idx = held("idx", [P, S // 16], U16)
         idx2 = held("idx2", [P, M // 16], U16)
@@ -76,70 +76,70 @@ def tile_list_mesh_block_refinement_kernel(
         tab_w = place("tab_w", [P, T], U32, AT_TAB)
         tab_s = held("tab_s", [P, T], U8)
         tab2_w = place("tab2_w", [P, T2], U32, AT_TAB2)
-        tab2_s = place("tab2_s", [P, T2], U8, AT_TAB2 + PLANES)
+        tab2_s = held("tab2_s", [P, T2], U8)
         ws_s = held("ws_s", [P, H], U8)
         wf_s = held("wf_s", [P, H], U8)
-        off_rows = place("off_rows", [P, GROUP], F32, AT_FINE)
-        off_slots = place("off_slots", [P, GROUP], F32, AT_FINE + 2 * KIB)
-        off_col = held("off_col", [P, GROUPS, PACK], F32)
-        off_size = held("off_size", [P, GROUPS, PACK], F32)
-        off_twice = held("off_twice", [P, GROUPS, PACK], F32)
-        off_sign = held("off_sign", [P, GROUPS, PACK], F32)
+        off_rows = held("off_rows", [P, GROUP], F32)
         ident = held("ident", [P, P], F32)
 
-        nc.vector.memset(tab_s[:].bitcast(I32), 0)
         nc.gpsimd.memset(off_rows[:], 0.0)
-        nc.vector.memset(ws_s[:].bitcast(I32), 0)
-        nc.vector.memset(wf_s[:].bitcast(I32), 0)
+        for plane in (tab_s, ws_s, wf_s):
+            nc.vector.memset(plane[:].bitcast(I32), 0)
         make_identity(nc, ident[:])
         nc.gpsimd.memset(tab2_s[:].bitcast(I32), 0)
-        load_scales(tab2_s, tab2_scales, TAB2_ROW, nc.gpsimd)
 
-        tab_rows = tab_words[0].rearrange("p t i -> p (t i)").bitcast(I32)
-        ws_rows = ws_words[0].bitcast(I32)
-        wf_rows = wf_words[0].rearrange("p t i -> p (t i)").bitcast(I32)
+        def load_scales(plane, scales, row, queue):
+            for r in range(4):
+                queue.dma_start(
+                    out=plane[row + r : P : 32, :].bitcast(I32),
+                    in_=scales[0, r : 16 : 4, :].bitcast(I32),
+                )
 
-        def load_words(name, rows, first, count, at=None):
-            n = rows.shape[1] // GROUPS
-            shape = [P, 4 * n * count]
-            raw = held(name, shape, U8) if at is None else place(name, shape, U8, at)
-            nc.sync.dma_start(out=raw[:].bitcast(I32), in_=rows[:, first * n : (first + count) * n])
+        def load_words(raw, rows):
+            nc.sync.dma_start(out=raw[:].bitcast(I32), in_=rows)
             return raw
 
-        def load_wv(first, width, raw):
-            nc.sync.dma_start(out=raw, in_=wv[:, first : first + width].rearrange("(p j) r -> p j r", j=PACK))
-            return raw
-
-        def load_wo(g, at):
-            raw = place("wo_raw%d" % g, [P, PACK, N], F32, at)
-            rows = wo[g * GROUP : (g + 1) * GROUP, :].rearrange("(c t i) n -> t c i n", t=PACK, i=RUN)
+        def load_wo(name, g, cols, at):
+            raw = place(name, [P, PACK, cols.stop - cols.start], F32, at)
+            rows = wo[g * GROUP : (g + 1) * GROUP, cols].rearrange("(c t i) n -> t c i n", t=PACK, i=RUN)
             for t in range(PACK):
                 nc.sync.dma_start(out=raw[:, t, :], in_=rows[t])
             return raw
 
+        def load_wv(g):
+            raw = place("wv_raw%d" % g, [P, PACK, GROUP], F32, (AT_WO + LAST * PLANES, AT_TAB, AT_LIMITS + PLANES)[g])
+            rows = wv[:, g * GROUP : (g + 1) * GROUP].rearrange("(p j) r -> p j r", j=PACK)
+            nc.sync.dma_start(out=raw[:], in_=rows)
+            return raw
+
+        tab_rows = tab_words[0].rearrange("p t i -> p (t i)").bitcast(I32)
+        ws_rows = ws_words[0].bitcast(I32)
+        ws_cut = 2 * GROUP // 4
+
+        load_scales(tab2_s, tab2_scales, TAB2_ROW, nc.gpsimd)
         nc.sync.dma_start(idx[:], offs)
         nc.sync.dma_start(out=tab_w[:, :TAB_FIRST].bitcast(I32), in_=tab_rows[:, :TAB_FIRST])
         load_scales(tab_s, tab_scales, 0, nc.sync)
-        ws_first = load_words("ws_first", ws_rows, 0, 1)
+        ws_first = load_words(held("ws_first", [P, 2 * GROUP], U8), ws_rows[:, :ws_cut])
         nc.sync.dma_start(out=tab_w[:, TAB_FIRST:TAB_LAST].bitcast(I32), in_=tab_rows[:, TAB_FIRST:TAB_LAST])
         load_scales(ws_s, ws_scales, 0, nc.sync)
         nc.sync.dma_start(out=tab_w[:, TAB_LAST:].bitcast(I32), in_=tab_rows[:, TAB_LAST:])
         nc.scalar.dma_start(out=off_rows[0:GROUPS, :], in_=off.rearrange("(g r) -> g r", g=GROUPS))
         nc.sync.dma_start(idx2[:], offs2)
-        wf_first = load_words("wf_first", wf_rows, 0, GROUPS - 1, AT_WO_STAGE)
+        wf_rows = wf_words[0].rearrange("p t i -> p (t i)").bitcast(I32)
+        wf_first = load_words(place("wf_first", [P, 4 * GROUP], U8, AT_PAIRS), wf_rows[:, :GROUP])
         load_scales(wf_s, wf_scales, WF_ROW, nc.sync)
-        ws_rest = load_words("ws_rest", ws_rows, 1, GROUPS - 1, AT_WO_STAGE + WINDOW)
+        ws_rest = load_words(place("ws_rest", [P, 2 * LAST * GROUP], U8, AT_PAIRS + WINDOW), ws_rows[:, ws_cut:])
         nc.sync.dma_start(p1[:], pos1)
-        wo_raw = [load_wo(0, AT_RAW)]
+        wo_raw = [load_wo("wo_raw0", 0, slice(0, N), AT_WO)]
         nc.sync.dma_start(
-            out=tab2_w[:].bitcast(I32),
-            in_=tab2_words[0].rearrange("p t i -> p (t i)").bitcast(I32),
+            out=tab2_w[:].bitcast(I32), in_=tab2_words[0].rearrange("p t i -> p (t i)").bitcast(I32)
         )
-        wo_raw.append(load_wo(1, AT_RAW + PLANES))
-        wv_head = load_wv(0, GROUP, place("wv_head", [P, PACK, GROUP], F32, AT_STAGE + WINDOW)[:])
-        wf_last = load_words("wf_last", wf_rows, GROUPS - 1, 1)
-        both = place("wv_middle", [P, 2, PACK, GROUP], F32, AT_RAW + 2 * PLANES)
-        wv_middle = [load_wv(g * GROUP, GROUP, both[:, g - 1]) for g in (1, 2)]
+        wo_raw.append(load_wo("wo_raw1", 1, slice(0, N), AT_WO + PLANES))
+        wo_left = load_wo("wo_left", LAST, slice(0, N // 2), AT_WV_RAW)
+        wf_rest = load_words(held("wf_rest", [P, 4 * LAST * GROUP], U8), wf_rows[:, GROUP:])
+        wv_raw = {g: load_wv(g) for g in (LAST, 0, 1)}
+        wo_right = load_wo("wo_right", LAST, slice(N // 2, N), AT_TAB + PLANES + WINDOW)
 
         def reorder(dst, src, count, bytes_per_col):
             w = RUN * bytes_per_col // 4
@@ -149,17 +149,18 @@ def tile_list_mesh_block_refinement_kernel(
             )
             return dst
 
-        def reorder_weight(room, raw, plane, first, count, bytes_per_col):
-            n = count * GROUP
-            scales = reorder(room[:, :n], plane[:, first * GROUP : first * GROUP + n], count, 1)
-            words = reorder(room[:, n:], raw[:], count, bytes_per_col)
+        def reorder_weight(words, scales, raw, plane, count, bytes_per_col):
+            reorder(scales, plane, count, 1)
+            reorder(words, raw, count, bytes_per_col)
             return [
-                (words[:, bytes_per_col * c : bytes_per_col * (c + P)], scales[:, c : c + P]) for c in range(0, n, P)
+                (words[:, bytes_per_col * c : bytes_per_col * (c + P)], scales[:, c : c + P])
+                for c in range(0, count * GROUP, P)
             ]
 
-        def quantize(name, grouped):
+        def quantize(name, grouped, at=None):
             width = grouped.shape[1] // PACK
-            codes = held(name + "_codes", [P, width], U32)
+            shape = [P, width]
+            codes = held(name + "_codes", shape, U32) if at is None else place(name + "_codes", shape, U32, at)
             scales = held(name + "_scales", [P, width], U8)
             nc.vector.quantize_mx(out=codes[:].bitcast(FP8X4), scales=scales[:], in_=grouped)
             return codes, scales
@@ -168,17 +169,77 @@ def tile_list_mesh_block_refinement_kernel(
             codes, scales = quantized
             return [(codes[:, c : c + width], scales[:, c : c + width]) for c in range(0, codes.shape[1], width)]
 
-        def woven(grouped):
-            return grouped.rearrange("p (c i t) -> p c t i", i=4, t=PACK)
+        def round_planes(copy, grouped, planes):
+            copy(
+                grouped.rearrange("p (c i t) -> p c t i", i=4, t=PACK),
+                planes.rearrange("p t (c i) -> p c t i", i=4),
+            )
 
-        def plain(planes):
-            return planes.rearrange("p t (c i) -> p c t i", i=4)
+        freed = [list(range(SET)), list(range(SET, 2 * SET))]
+        sets = []
+
+        def through_banks(jobs, backwards=True):
+            side = len(sets) % 2
+            sets.append(side)
+            order = list(reversed(jobs)) if backwards else jobs
+            for number, (dst, func, factor, lhs, lhs_s, rhs, rhs_s) in zip(freed[side], order):
+                nc.tensor.matmul_mx(
+                    out=banks[number][:], lhsT=lhs, lhsT_scale=lhs_s, rhs=rhs, rhs_scale=rhs_s, start=True, stop=True
+                )
+            if backwards:
+                freed[side].reverse()
+            for number, job in zip(freed[side], jobs):
+                nc.scalar.activation(out=job[0], in_=banks[number][:], func=job[1], scale=job[2])
+
+        off_slots = held("off_slots", [P, GROUP], F32)
+        off_col = held("off_col", [P, GROUPS, PACK], F32)
+        off_size = held("off_size", [P, GROUPS, PACK], F32)
+        off_twice = held("off_twice", [P, GROUPS, PACK], F32)
+        off_sign = held("off_sign", [P, GROUPS, PACK], F32)
+        nc.scalar.copy(
+            off_slots[:].rearrange("p (t c i) -> p t c i", t=PACK, i=RUN),
+            off_rows[:].rearrange("p (c t i) -> p t c i", t=PACK, i=RUN),
+        )
+        off_bank = banks[2 * SET - 1][:].rearrange("p (t c) -> p t c", t=PACK)
+        for t in range(PACK):
+            nc.tensor.transpose(off_bank[:, t, :], off_slots[:, t * P : (t + 1) * P], ident[:])
+        nc.scalar.copy(out=off_col[:].rearrange("p g t -> p t g"), in_=off_bank[:, :, 0:GROUPS])
+        nc.scalar.activation(out=off_size[:], in_=off_col[:], func=ACT.Abs)
+        nc.gpsimd.tensor_scalar(off_twice[:], off_col[:], 0.0, 2.0, ALU.is_ge, ALU.mult)
+        nc.gpsimd.tensor_scalar(off_sign[:], off_twice[:], 1.0, -1.0, ALU.mult, ALU.add)
+
+        v_s = place("v_s", [P, S], U8, AT_WOVEN + 2 * PLANES)
+        nc.vector.tensor_copy(v_s[:], tab_s[:].indirect(idx[:]))
+        room = held("ws_head", [P, 3 * GROUP], U8)
+        ws_slots = reorder_weight(room[:, GROUP:], room[:, :GROUP], ws_first[:], ws_s[:, :GROUP], 1, 2)
+        v2_s = held("v2_s", [P, M], U8)
+        nc.vector.tensor_copy(v2_s[:], tab2_s[:].indirect(idx2[:]))
+        v_w = []
+        for half in range(S // BANK):
+            words = place("v_w%d" % half, [P, BANK], U32, AT_WOVEN + half * PLANES)
+            nc.vector.tensor_copy(words[:], tab_w[:].indirect(idx[:, half * BANK // 16 : (half + 1) * BANK // 16]))
+            v_w.append(words)
+        room = place("wf_head", [P, 5 * GROUP], U8, AT_WV_LAST)
+        wf_slots = reorder_weight(room[:, GROUP:], room[:, :GROUP], wf_first[:], wf_s[:, :GROUP], 1, 4)
+        room = held("ws_tail", [P, 3 * LAST * GROUP], U8)
+        ws_slots.extend(
+            reorder_weight(room[:, LAST * GROUP :], room[:, : LAST * GROUP], ws_rest[:], ws_s[:, GROUP:], LAST, 2)
+        )
 
         def paired(pairs):
             return pairs.rearrange("p (u n e) -> p u e n", u=2, e=2)
 
-        def by_pairs(planes):
-            return planes.rearrange("p (u e) n -> p u e n", u=2)
+        def round_wo(engine, pairs, raw, g):
+            for t in range(PACK):
+                engine.tensor_scalar(
+                    paired(pairs)[:, t // 2, t % 2], raw[:, t, :], off_sign[:, g, t : t + 1], 0.0, ALU.mult, ALU.add
+                )
+
+        def round_wv(copy, grouped, raw):
+            copy(
+                grouped.rearrange("p (t c i j) -> p t c j i", t=PACK, i=RUN, j=PACK),
+                raw.rearrange("p j (c t i) -> p t c j i", t=PACK, i=RUN),
+            )
 
         def weave(grouped, pairs):
             nc.scalar.copy(
@@ -186,214 +247,137 @@ def tile_list_mesh_block_refinement_kernel(
                 pairs.bitcast(U32).rearrange("p (u n) -> p n u", u=2),
             )
 
-        def wv_views(grouped, raw, slots):
-            dst = grouped.rearrange("p (t c i j) -> p t c i j", t=PACK, i=RUN, j=PACK)[:, slots]
-            src = raw.rearrange("p j (c t i) -> p t c i j", t=PACK, i=RUN)[:, slots]
-            return dst, src
+        wo_pairs = place("wo_pairs", [P, LAST * UNIT], BF16, AT_PAIRS)
+        for g in range(LAST):
+            round_wo(nc.gpsimd, wo_pairs[:, g * UNIT : (g + 1) * UNIT], wo_raw[g], g)
+        left_pairs = held("left_pairs", [P, UNIT // 2], BF16)
+        round_wo(nc.gpsimd, left_pairs[:], wo_left, LAST)
 
-        def round_wv(copy, grouped, raw, slots=slice(0, PACK)):
-            copy(*[view.rearrange("p t c i j -> p t c j i") for view in wv_views(grouped, raw, slots)])
+        ring = [place("window0", [P, S], F32, AT_FIRST)]
+        ring.extend(place("window%d" % k, [P, S], F32, AT_RING + (k - 1) * WINDOW) for k in range(1, RING))
+        turns = [0, 1, 2, 3, 4, 5, 6, 0]
+        turns.extend(1 + k % (RING - 1) for k in range(6, 6 + 4 * PACK))
 
-        def round_wo(pairs, g):
-            for t in range(PACK):
-                nc.gpsimd.tensor_scalar(
-                    paired(pairs)[:, t // 2, t % 2], wo_raw[g][:, t, :], off_sign[:, g, t : t + 1], 0.0, ALU.mult, ALU.add
-                )
-
-        freed = [list(range(SET)), list(range(SET, 2 * SET))]
-        sets = []
-
-        def through_banks(jobs, backwards=True, lent=0):
-            side = len(sets) % 2
-            sets.append(side)
-            order = list(reversed(jobs)) if backwards else jobs
-            banks = []
-            for number, (dst, func, factor, lhs, lhs_s, rhs, rhs_s) in zip(freed[side], order):
-                bank = psum.tile([P, BANK], F32, name="bank%d" % number)
-                nc.tensor.matmul_mx(
-                    out=bank[:], lhsT=lhs, lhsT_scale=lhs_s, rhs=rhs, rhs_scale=rhs_s, start=True, stop=True
-                )
-                banks.append(bank)
-            if backwards:
-                banks.reverse()
-                freed[side].reverse()
-            for k, (bank, job) in enumerate(zip(banks, jobs)):
-                if k < len(jobs) - lent:
-                    nc.scalar.activation(out=job[0], in_=bank[:], func=job[1], scale=job[2])
-                else:
-                    nc.vector.tensor_scalar(job[0], bank[:], job[2], 0.0, ALU.mult, ALU.add)
-
-        cols = [slice(half * BANK, (half + 1) * BANK) for half in range(S // BANK)]
-
-        def coarse_jobs(window, func, factor, lhs, lhs_s):
-            return [
-                (window[:, c], func, factor, lhs, lhs_s, words[:].bitcast(FP8X4), v_s[:, c])
-                for words, c in zip(v_w, cols)
+        def coarse(func, factors, slots, dtype, g):
+            windows = [ring[turns.pop(0)] for t in range(PACK)]
+            jobs = [
+                [
+                    (windows[t][:, c : c + BANK], func, factors[:, g, t : t + 1], lhs.bitcast(dtype), lhs_s,
+                     words[:].bitcast(FP8X4), v_s[:, c : c + BANK])
+                    for words, c in zip(v_w, range(0, S, BANK))
+                ]
+                for t, (lhs, lhs_s) in enumerate(slots[PACK * g : PACK * (g + 1)])
             ]
-
-        def slope_jobs(window, g, t):
-            words, scales = ws_slots[PACK * g + t]
-            return coarse_jobs(window, ACT.Abs, off_size[:, g, t : t + 1], words.bitcast(FP4X4), scales)
-
-        def value_jobs(window, g, t):
-            codes, scales = wv_slots[PACK * g + t]
-            return coarse_jobs(window, ACT.Copy, off_sign[:, g, t : t + 1], codes.bitcast(FP8X4), scales)
-
-        def coarse(name, at, jobs, g, lent=0):
-            windows = [place("%s%d_%d" % (name, g, t), [P, S], F32, at + t * WINDOW) for t in range(PACK)]
-            for t in range(0, PACK, 2):
-                through_banks(jobs(windows[t], g, t) + jobs(windows[t + 1], g, t + 1), lent=lent if t else 0)
+            if not sets:
+                through_banks([jobs[0][0], jobs[1][0], jobs[0][1], jobs[1][1]], backwards=False)
+            else:
+                through_banks(jobs[0] + jobs[1])
+            through_banks(jobs[2] + jobs[3])
             return windows
 
         def pick(planes, windows):
-            for t, window in enumerate(windows):
-                nc.vector.tensor_copy(planes[:, t, :], window[:].indirect(p1[:]))
+            for t in range(PACK):
+                nc.vector.tensor_copy(planes[:, t, :], windows[t][:].indirect(p1[:]))
 
-        def fine(planes, g):
+        def fine(planes, g, backwards=True):
             through_banks([
                 (planes[:, t, :], ACT.Abs, off_size[:, g, t : t + 1], words.bitcast(FP8X4), scales[WF_ROW:P, :],
                  v2_w[:].bitcast(FP8X4), v2_s[TAB2_ROW:P, :])
                 for t, (words, scales) in enumerate(wf_slots[PACK * g : PACK * (g + 1)])
-            ])
+            ], backwards)
 
-        nc.scalar.copy(
-            off_slots[:].rearrange("p (t c i) -> p t c i", t=PACK, i=RUN),
-            off_rows[:].rearrange("p (c t i) -> p t c i", t=PACK, i=RUN),
-        )
-        off_bank = psum.tile([P, PACK, P], F32, name="bank%d" % (2 * SET - 1))
-        for t in range(PACK):
-            nc.tensor.transpose(off_bank[:, t, :], off_slots[:, t * P : (t + 1) * P], ident[:])
-        nc.scalar.copy(out=off_col[:].rearrange("p g t -> p t g"), in_=off_bank[:, :, 0:GROUPS])
-        nc.scalar.activation(out=off_size[:], in_=off_col[:], func=ACT.Abs)
-        nc.vector.tensor_scalar(off_twice[:], off_col[:], 0.0, 2.0, ALU.is_ge, ALU.mult)
-        nc.gpsimd.tensor_scalar(off_sign[:], off_twice[:], 1.0, -1.0, ALU.mult, ALU.add)
-
-        v_s = place("v_s", [P, S], U8, AT_WOVEN + 2 * PLANES)
-        nc.vector.tensor_copy(v_s[:], tab_s[:].indirect(idx[:]))
-        ws_slots = reorder_weight(held("ws_head", [P, 3 * GROUP], U8), ws_first, ws_s, 0, 1, 2)
-        v2_s = held("v2_s", [P, M], U8)
-        nc.vector.tensor_copy(v2_s[:], tab2_s[:].indirect(idx2[:]))
-        v_w = []
-        for half in range(S // BANK):
-            words = place("v_w%d" % half, [P, BANK], U32, AT_WOVEN + half * PLANES)
-            part = slice(half * BANK // 16, (half + 1) * BANK // 16)
-            nc.vector.tensor_copy(words[:], tab_w[:].indirect(idx[:, part]))
-            v_w.append(words)
-        wf_slots = reorder_weight(held("wf_head", [P, 10 * GROUP], U8), wf_first, wf_s, 0, GROUPS - 1, 4)
-        ws_slots.extend(reorder_weight(held("ws_tail", [P, 6 * GROUP], U8), ws_rest, ws_s, 1, GROUPS - 1, 2))
-
-        unit = PACK * M
-        wo_pairs = place("wo_pairs", [P, 2 * unit], BF16, AT_WO_STAGE)
-        for g in range(2):
-            round_wo(wo_pairs[:, g * unit : (g + 1) * unit], g)
-        wv_first = place("wv_first", [P, unit], BF16, AT_RAW)
-        views = wv_views(wv_first[:], wv_head, slice(0, PACK))
-        dst, src = [view.rearrange("p t c i j -> p c t i j") for view in views]
-        nc.gpsimd.tensor_scalar(dst, src, 1.0, 0.0, ALU.mult, ALU.add)
-
-        picks = [place("picks%d" % g, [P, PACK, M], F32, at) for g, at in enumerate((AT_PICKS, AT_TAB2 + T2))]
-        limits = [place("limits%d" % g, [P, PACK, M], F32, AT_FINE + g * PLANES) for g in range(2)]
-        windows = [place("d0_%d" % t, [P, S], F32, AT_WINDOWS + t * WINDOW) for t in range(PACK)]
-        jobs = [slope_jobs(windows[t], 0, t) for t in range(PACK)]
-        through_banks([jobs[0][0], jobs[1][0], jobs[0][1], jobs[1][1]], backwards=False)
-        through_banks(jobs[2] + jobs[3])
-        pick(picks[0][:], windows)
+        picks = [place("picks%d" % g, [P, PACK, M], F32, at) for g, at in enumerate((AT_PICKS, AT_TAB2, AT_WO + PLANES))]
         v2_w = held("v2_w", [P, M], U32)
-        windows = coarse("d", AT_WINDOWS + 4 * WINDOW, slope_jobs, 1)
-        nc.vector.tensor_copy(v2_w[:], tab2_w[:].indirect(idx2[:]))
-        pick(picks[1][:], windows)
-        for g in range(2):
-            fine(limits[g][:], g)
+        for g in range(LAST):
+            windows = coarse(ACT.Abs, off_size, ws_slots, FP4X4, g)
+            if g > 0:
+                nc.vector.tensor_copy(v2_w[:], tab2_w[:].indirect(idx2[:]))
+            pick(picks[g], windows)
+        limits = [place("limits%d" % g, [P, PACK, M], F32, AT_LIMITS + g * PLANES) for g in range(LAST)]
+        fine(limits[0], 0)
+        wv_last = place("wv_last", [P, UNIT], BF16, AT_WV_LAST)
+        round_wv(nc.scalar.copy, wv_last[:], wv_raw[LAST][:])
 
-        wo_raw.append(load_wo(2, AT_WINDOWS + 4 * WINDOW))
-        wv_rest = place("wv_rest", [P, 2 * unit], BF16, AT_WINDOWS + 6 * WINDOW)
-        room = place("wf_tail", [P, 5 * GROUP], U8, AT_RAW + PLANES)
-        wf_slots.extend(reorder_weight(room, wf_last, wf_s, GROUPS - 1, 1, 4))
-        wv_slots = columns(quantize("wv0", wv_first[:]), P)
-        round_wv(nc.vector.tensor_copy, wv_rest[:, :unit], wv_middle[0])
-        round_wv(nc.vector.tensor_copy, wv_rest[:, unit:], wv_middle[1])
-        least = {}
-        for g in (1, 0):
-            wv_slots.extend(columns(quantize("wv%d" % (2 - g), wv_rest[:, (1 - g) * unit : (2 - g) * unit]), P))
-            least[g] = place("least%d" % g, [P, PACK, M], F32, AT_RAW + (2 + g) * PLANES)
-            nc.vector.tensor_tensor(least[g][:], picks[g][:], limits[g][:], ALU.min)
-
-        last = GROUPS - 1
-        stage = place("stage", [P, GROUPS * unit], BF16, AT_FINE)
-        round_wo(stage[:, :unit], last)
-        for g in range(2):
-            windows = coarse("h", (AT_VALUES, AT_WINDOWS)[g], value_jobs, g)
-            values = place("values%d" % g, [P, PACK, M], F32, (AT_PICKS, AT_TAB2 + T2)[g])
-            pick(values[:], windows)
-            nc.gpsimd.tensor_tensor(
-                paired(stage[:, (g + 1) * unit : (g + 2) * unit]), by_pairs(values[:]), by_pairs(least[g][:]), ALU.add
-            )
-
-        windows = coarse("d", AT_WINDOWS + 8 * WINDOW, slope_jobs, last)
-        picks = place("picks2", [P, PACK, M], F32, AT_STAGE + WINDOW)
-        pick(picks[:], windows)
-        windows = coarse("h", AT_TAB, value_jobs, last, LENT)
-        limits = place("limits2", [P, PACK, M], F32, AT_RAW)
-        fine(limits[:], last)
-        sources = (
-            (wo_pairs[:, :unit], stage[:, unit : 2 * unit]),
-            (wo_pairs[:, unit:], stage[:, 2 * unit :]),
-            (stage[:, :unit],),
+        room = place("wf_tail", [P, 5 * LAST * GROUP], U8, AT_WF)
+        wf_slots.extend(
+            reorder_weight(room[:, LAST * GROUP :], room[:, : LAST * GROUP], wf_rest[:], wf_s[:, GROUP:], LAST, 4)
         )
-        ready = []
-        for k, pieces in enumerate(sources):
-            grouped = place("woven%d" % k, [P, len(pieces) * unit], BF16, AT_WOVEN + k * PLANES)
-            for c, pairs in enumerate(pieces):
-                weave(grouped[:, c * unit : (c + 1) * unit], pairs)
-            ready.append(grouped[:])
-        steps = place("steps2", [P, PACK, M], F32, AT_WINDOWS + 5 * WINDOW)
-        for side in (slice(0, HALF), slice(HALF, M)):
-            nc.vector.tensor_tensor(steps[:, :, side], picks[:, :, side], limits[:, :, side], ALU.min)
+        fine(limits[1], 1, backwards=False)
+        wv_grouped = place("wv_grouped", [P, LAST * UNIT], BF16, AT_WV)
+        for g in range(LAST):
+            round_wv(nc.vector.tensor_copy, wv_grouped[:, g * UNIT : (g + 1) * UNIT], wv_raw[g][:])
+        wv_slots = []
+        for g in range(LAST):
+            wv_slots.extend(columns(quantize("wv%d" % g, wv_grouped[:, g * UNIT : (g + 1) * UNIT]), P))
+        steps = [place("steps%d" % g, [P, PACK, M], F32, at) for g, at in enumerate((AT_WO + LAST * PLANES, AT_TAB + WINDOW))]
+        nc.vector.tensor_tensor(steps[0][:], picks[0][:], limits[0][:], ALU.min)
+        wv_slots.extend(columns(quantize("wv2", wv_last[:], AT_LIMITS), P))
+        nc.vector.tensor_tensor(steps[1][:], picks[1][:], limits[1][:], ALU.min)
 
+        stage = place("stage", [P, LAST * UNIT + UNIT // 2], BF16, AT_LIMITS + WINDOW)
+        right_pairs = stage[:, LAST * UNIT :]
+        round_wo(nc.gpsimd, right_pairs, wo_right, LAST)
+        for g in range(LAST):
+            values = picks[1 - g]
+            pick(values, coarse(ACT.Copy, off_sign, wv_slots, FP8X4, g))
+            for u in range(2):
+                two = slice(2 * u, 2 * u + 2)
+                nc.gpsimd.tensor_tensor(
+                    paired(stage[:, g * UNIT : (g + 1) * UNIT])[:, u], values[:, two, :], steps[g][:, two, :], ALU.add
+                )
 
-        early = [columns(quantize("wo0_z0", ready[0]), M)]
-        z_last, waiting = [], []
+        pick(picks[LAST], coarse(ACT.Abs, off_size, ws_slots, FP4X4, LAST))
+        windows = coarse(ACT.Copy, off_sign, wv_slots, FP8X4, LAST)
+        limits.append(place("limits2", [P, PACK, M], F32, AT_WV_RAW))
+        fine(limits[LAST], LAST)
+        woven = []
+        for g in range(LAST):
+            woven.append(place("woven%d" % g, [P, 2 * UNIT], BF16, AT_WOVEN + g * PLANES))
+            weave(woven[g][:, :UNIT], wo_pairs[:, g * UNIT : (g + 1) * UNIT])
+            weave(woven[g][:, UNIT:], stage[:, g * UNIT : (g + 1) * UNIT])
+        woven.append(place("woven2", [P, UNIT], BF16, AT_WOVEN + LAST * PLANES))
+        weave(woven[LAST][:, : UNIT // 2], left_pairs[:])
+        weave(woven[LAST][:, UNIT // 2 :], right_pairs)
+        steps.append(place("steps2", [P, PACK, M], F32, AT_WO))
+        for side in (slice(0, M // 2), slice(M // 2, M)):
+            nc.vector.tensor_tensor(steps[LAST][:, :, side], picks[LAST][:, :, side], limits[LAST][:, :, side], ALU.min)
+
+        early = [columns(quantize("wo0_z0", woven[0][:]), M)]
+        z_parts, rounded = [], []
         for k, part in enumerate(PARTS):
             width = part.stop - part.start
-            planes = place("z2_%d" % k, [P, PACK, width], F32, AT_WINDOWS + k * WINDOW)
+            sums = place("z_part%d" % k, [P, PACK, width], F32, AT_PICKS + 4 * PACK * part.start)
             offsets = p1[:, part.start // 16 : part.stop // 16]
             for t in range(PACK):
-                nc.vector.tensor_tensor(planes[:, t, :], windows[t][:].indirect(offsets), steps[:, t, part], ALU.add)
-            if k < last:
-                early.append(columns(quantize("early%d" % k, ready[k + 1]), M))
+                nc.vector.tensor_tensor(sums[:, t, :], windows[t][:].indirect(offsets), steps[LAST][:, t, part], ALU.add)
+            if k < LAST:
+                early.append(columns(quantize("early%d" % k, woven[k + 1][:]), M))
             if k > 0:
-                z_last.append(quantize("z2_%d" % (k - 1), waiting[-1]))
-            rounded = held("z2_bf16_%d" % k, [P, PACK * width], BF16)
-            copy = nc.vector.tensor_copy if k == len(PARTS) - 1 else nc.scalar.copy
-            copy(woven(rounded[:]), plain(planes[:]))
-            waiting.append(rounded[:])
-        z_last.append(quantize("z2_%d" % k, waiting[-1]))
+                z_parts.append(quantize("z_part%d" % (k - 1), rounded[k - 1][:]))
+            rounded.append(held("z_rounded%d" % k, [P, PACK * width], BF16))
+            round_planes(nc.vector.tensor_copy if k == LAST else nc.scalar.copy, rounded[k][:], sums[:])
+        z_parts.append(quantize("z_part%d" % k, rounded[k][:]))
 
         numbers = freed[len(sets) % 2] + freed[(len(sets) + 1) % 2]
-        acc = [
-            [psum.tile([P, 2, part.stop - part.start], F32, name="bank%d" % numbers[2 * k + pair]) for pair in range(2)]
-            for k, part in enumerate(PARTS)
-        ]
         for g in range(GROUPS):
             for k, part in enumerate(PARTS):
-                if g == last:
-                    z_codes, z_scales = z_last[k][0][:], z_last[k][1][:]
-                else:
-                    z_codes, z_scales = early[g][1][0][:, part], early[g][1][1][:, part]
+                width = part.stop - part.start
+                z_codes, z_scales = z_parts[k] if g == LAST else early[g][1]
+                cols = slice(0, width) if g == LAST else part
                 for n in range(N // P):
                     wo_codes, wo_scales = columns(early[g][0], P)[n]
                     nc.tensor.matmul_mx(
-                        out=acc[k][n // 2][:, n % 2, :], lhsT=wo_codes.bitcast(FP8X4), lhsT_scale=wo_scales,
-                        rhs=z_codes.bitcast(FP8X4), rhs_scale=z_scales,
-                        start=(g == 0 and n % 2 == 0), stop=(g == last and n % 2 == 1),
+                        out=banks[numbers[2 * k + n // 2]][:, (n % 2) * width : (n % 2 + 1) * width],
+                        lhsT=wo_codes.bitcast(FP8X4), lhsT_scale=wo_scales,
+                        rhs=z_codes[:, cols].bitcast(FP8X4), rhs_scale=z_scales[:, cols],
+                        start=(g == 0 and n % 2 == 0), stop=(g == LAST and n % 2 == 1),
                     )
 
         for k, part in enumerate(PARTS):
+            width = part.stop - part.start
             for pair in range(2):
-                results = place(
-                    "results%d_%d" % (k, pair), [P, 2, part.stop - part.start], F32, AT_STAGE + (2 * k + pair) * 2 * KIB
-                )
+                results = place("results%d_%d" % (k, pair), [P, 2 * width], F32, AT_LIMITS + (2 * k + pair) * 2 * KIB)
                 copy = nc.vector.tensor_copy if k == len(PARTS) - 1 and pair else nc.scalar.copy
-                copy(results[:], acc[k][pair][:])
+                copy(results[:], banks[numbers[2 * k + pair]][:, : 2 * width])
                 rows = out[2 * pair * P : 2 * (pair + 1) * P, part].rearrange("(u p) m -> p u m", u=2)
-                nc.sync.dma_start(out=rows, in_=results[:])
+                nc.sync.dma_start(out=rows, in_=results[:].rearrange("p (u m) -> p u m", u=2))

@@ -41,14 +41,14 @@ AT_TAB = 0
 AT_WO = AT_TAB + 2 * PLANES
 AT_TAB2 = AT_WO + GROUPS * PLANES
 AT_WF = AT_TAB2 + PLANES
-AT_FIRST = AT_WF + 5 * LAST * GROUP - LAP
+AT_FIRST = AT_WF + 5 * GROUP - LAP
 AT_WV = AT_FIRST + WINDOW - LAP
 AT_RING = AT_WV + 2 * LAST * UNIT
 AT_PAIRS = AT_RING + (RING - 1) * WINDOW
 AT_LIMITS = AT_PAIRS + LAST * WINDOW
 AT_WOVEN = AT_LIMITS + LAST * PLANES
 AT_WV_LAST = AT_WOVEN + 5 * WINDOW
-AT_WV_RAW = AT_WV_LAST + WINDOW
+AT_WV_RAW = AT_WV_LAST + WINDOW + KIB
 AT_PICKS = AT_WV_RAW + PLANES
 
 
@@ -106,10 +106,9 @@ def tile_list_mesh_block_refinement_kernel(
                 nc.sync.dma_start(out=raw[:, t, :], in_=rows[t])
             return raw
 
-        def load_wv(g):
-            raw = place("wv_raw%d" % g, [P, PACK, GROUP], F32, (AT_WO + LAST * PLANES, AT_TAB, AT_LIMITS + PLANES)[g])
-            rows = wv[:, g * GROUP : (g + 1) * GROUP].rearrange("(p j) r -> p j r", j=PACK)
-            nc.sync.dma_start(out=raw[:], in_=rows)
+        def load_wv(name, first, width, at):
+            raw = place(name, [P, PACK, width], F32, at)
+            nc.sync.dma_start(out=raw[:], in_=wv[:, first : first + width].rearrange("(p j) r -> p j r", j=PACK))
             return raw
 
         tab_rows = tab_words[0].rearrange("p t i -> p (t i)").bitcast(I32)
@@ -127,7 +126,7 @@ def tile_list_mesh_block_refinement_kernel(
         nc.scalar.dma_start(out=off_rows[0:GROUPS, :], in_=off.rearrange("(g r) -> g r", g=GROUPS))
         nc.sync.dma_start(idx2[:], offs2)
         wf_rows = wf_words[0].rearrange("p t i -> p (t i)").bitcast(I32)
-        wf_first = load_words(place("wf_first", [P, 4 * GROUP], U8, AT_PAIRS), wf_rows[:, :GROUP])
+        wf_first = load_words(place("wf_first", [P, 4 * LAST * GROUP], U8, AT_PAIRS), wf_rows[:, : LAST * GROUP])
         load_scales(wf_s, wf_scales, WF_ROW, nc.sync)
         ws_rest = load_words(place("ws_rest", [P, 2 * LAST * GROUP], U8, AT_PAIRS + WINDOW), ws_rows[:, ws_cut:])
         nc.sync.dma_start(p1[:], pos1)
@@ -137,8 +136,11 @@ def tile_list_mesh_block_refinement_kernel(
         )
         wo_raw.append(load_wo("wo_raw1", 1, slice(0, N), AT_WO + PLANES))
         wo_left = load_wo("wo_left", LAST, slice(0, N // 2), AT_WV_RAW)
-        wf_rest = load_words(held("wf_rest", [P, 4 * LAST * GROUP], U8), wf_rows[:, GROUP:])
-        wv_raw = {g: load_wv(g) for g in (LAST, 0, 1)}
+        wf_last = load_words(held("wf_last", [P, 4 * GROUP], U8), wf_rows[:, LAST * GROUP :])
+        wv_raw = [load_wv("wv_raw0", 0, GROUP, AT_WO + LAST * PLANES)]
+        wv_low = load_wv("wv_low", LAST * GROUP, GROUP // 2, AT_WV_RAW + WINDOW)
+        wv_raw.append(load_wv("wv_raw1", GROUP, GROUP, AT_TAB))
+        wv_high = load_wv("wv_high", H - GROUP // 2, GROUP // 2, AT_TAB + PLANES)
         wo_right = load_wo("wo_right", LAST, slice(N // 2, N), AT_TAB + PLANES + WINDOW)
 
         def reorder(dst, src, count, bytes_per_col):
@@ -219,8 +221,10 @@ def tile_list_mesh_block_refinement_kernel(
             words = place("v_w%d" % half, [P, BANK], U32, AT_WOVEN + half * PLANES)
             nc.vector.tensor_copy(words[:], tab_w[:].indirect(idx[:, half * BANK // 16 : (half + 1) * BANK // 16]))
             v_w.append(words)
-        room = place("wf_head", [P, 5 * GROUP], U8, AT_WV_LAST)
-        wf_slots = reorder_weight(room[:, GROUP:], room[:, :GROUP], wf_first[:], wf_s[:, :GROUP], 1, 4)
+        room = place("wf_head", [P, 5 * LAST * GROUP], U8, AT_WV_LAST)
+        wf_slots = reorder_weight(
+            room[:, LAST * GROUP :], room[:, : LAST * GROUP], wf_first[:], wf_s[:, : LAST * GROUP], LAST, 4
+        )
         room = held("ws_tail", [P, 3 * LAST * GROUP], U8)
         ws_slots.extend(
             reorder_weight(room[:, LAST * GROUP :], room[:, : LAST * GROUP], ws_rest[:], ws_s[:, GROUP:], LAST, 2)
@@ -235,9 +239,9 @@ def tile_list_mesh_block_refinement_kernel(
                     paired(pairs)[:, t // 2, t % 2], raw[:, t, :], off_sign[:, g, t : t + 1], 0.0, ALU.mult, ALU.add
                 )
 
-        def round_wv(copy, grouped, raw):
+        def round_wv(copy, grouped, raw, runs=slice(0, P // RUN)):
             copy(
-                grouped.rearrange("p (t c i j) -> p t c j i", t=PACK, i=RUN, j=PACK),
+                grouped.rearrange("p (t c i j) -> p t c j i", t=PACK, i=RUN, j=PACK)[:, :, runs],
                 raw.rearrange("p j (c t i) -> p t c j i", t=PACK, i=RUN),
             )
 
@@ -279,12 +283,12 @@ def tile_list_mesh_block_refinement_kernel(
             for t in range(PACK):
                 nc.vector.tensor_copy(planes[:, t, :], windows[t][:].indirect(p1[:]))
 
-        def fine(planes, g, backwards=True):
+        def fine(planes, g):
             through_banks([
                 (planes[:, t, :], ACT.Abs, off_size[:, g, t : t + 1], words.bitcast(FP8X4), scales[WF_ROW:P, :],
                  v2_w[:].bitcast(FP8X4), v2_s[TAB2_ROW:P, :])
                 for t, (words, scales) in enumerate(wf_slots[PACK * g : PACK * (g + 1)])
-            ], backwards)
+            ])
 
         picks = [place("picks%d" % g, [P, PACK, M], F32, at) for g, at in enumerate((AT_PICKS, AT_TAB2, AT_WO + PLANES))]
         v2_w = held("v2_w", [P, M], U32)
@@ -294,24 +298,22 @@ def tile_list_mesh_block_refinement_kernel(
                 nc.vector.tensor_copy(v2_w[:], tab2_w[:].indirect(idx2[:]))
             pick(picks[g], windows)
         limits = [place("limits%d" % g, [P, PACK, M], F32, AT_LIMITS + g * PLANES) for g in range(LAST)]
-        fine(limits[0], 0)
+        for g in range(LAST):
+            fine(limits[g], g)
         wv_last = place("wv_last", [P, UNIT], BF16, AT_WV_LAST)
-        round_wv(nc.scalar.copy, wv_last[:], wv_raw[LAST][:])
+        round_wv(nc.scalar.copy, wv_last[:], wv_low[:], slice(0, P // RUN // 2))
 
-        room = place("wf_tail", [P, 5 * LAST * GROUP], U8, AT_WF)
-        wf_slots.extend(
-            reorder_weight(room[:, LAST * GROUP :], room[:, : LAST * GROUP], wf_rest[:], wf_s[:, GROUP:], LAST, 4)
-        )
-        fine(limits[1], 1, backwards=False)
         wv_grouped = place("wv_grouped", [P, LAST * UNIT], BF16, AT_WV)
-        for g in range(LAST):
-            round_wv(nc.vector.tensor_copy, wv_grouped[:, g * UNIT : (g + 1) * UNIT], wv_raw[g][:])
-        wv_slots = []
-        for g in range(LAST):
-            wv_slots.extend(columns(quantize("wv%d" % g, wv_grouped[:, g * UNIT : (g + 1) * UNIT]), P))
+        round_wv(nc.vector.tensor_copy, wv_grouped[:, :UNIT], wv_raw[0][:])
+        room = place("wf_tail", [P, 5 * GROUP], U8, AT_WF)
+        wf_slots.extend(reorder_weight(room[:, GROUP:], room[:, :GROUP], wf_last[:], wf_s[:, LAST * GROUP :], 1, 4))
+        wv_slots = columns(quantize("wv0", wv_grouped[:, :UNIT]), P)
         steps = [place("steps%d" % g, [P, PACK, M], F32, at) for g, at in enumerate((AT_WO + LAST * PLANES, AT_TAB + WINDOW))]
         nc.vector.tensor_tensor(steps[0][:], picks[0][:], limits[0][:], ALU.min)
-        wv_slots.extend(columns(quantize("wv2", wv_last[:], AT_LIMITS), P))
+        round_wv(nc.vector.tensor_copy, wv_grouped[:, UNIT:], wv_raw[1][:])
+        round_wv(nc.vector.tensor_copy, wv_last[:], wv_high[:], slice(P // RUN // 2, P // RUN))
+        wv_slots.extend(columns(quantize("wv1", wv_grouped[:, UNIT:]), P))
+        wv_slots.extend(columns(quantize("wv2", wv_last[:]), P))
         nc.vector.tensor_tensor(steps[1][:], picks[1][:], limits[1][:], ALU.min)
 
         stage = place("stage", [P, LAST * UNIT + UNIT // 2], BF16, AT_LIMITS + WINDOW)

@@ -40,16 +40,16 @@ LAP = KIB // 2
 AT_TAB = 0
 AT_WO = AT_TAB + 2 * PLANES
 AT_TAB2 = AT_WO + GROUPS * PLANES
-AT_WF = AT_TAB2 + PLANES
-AT_FIRST = AT_WF + 5 * GROUP - LAP
-AT_WV = AT_FIRST + WINDOW - LAP
-AT_RING = AT_WV + 2 * LAST * UNIT
-AT_PAIRS = AT_RING + (RING - 1) * WINDOW
+AT_WF_TAIL = AT_TAB2 + PLANES
+AT_WF_HEAD = AT_WF_TAIL + 5 * GROUP - LAP
+AT_WV = AT_WF_HEAD + 5 * LAST * GROUP - LAP
+AT_RING = AT_WV + 2 * GROUPS * UNIT
+AT_PAIRS = AT_RING + RING * WINDOW
 AT_LIMITS = AT_PAIRS + LAST * WINDOW
 AT_WOVEN = AT_LIMITS + LAST * PLANES
-AT_WV_LAST = AT_WOVEN + 5 * WINDOW
-AT_WV_RAW = AT_WV_LAST + WINDOW + KIB
-AT_PICKS = AT_WV_RAW + PLANES
+AT_HALVES = AT_WOVEN + 5 * WINDOW
+AT_PICKS = AT_HALVES + PLANES
+AT_SCALES = AT_PICKS + PLANES
 
 
 def tile_list_mesh_block_refinement_kernel(
@@ -77,7 +77,7 @@ def tile_list_mesh_block_refinement_kernel(
         tab_s = held("tab_s", [P, T], U8)
         tab2_w = place("tab2_w", [P, T2], U32, AT_TAB2)
         tab2_s = held("tab2_s", [P, T2], U8)
-        ws_s = held("ws_s", [P, H], U8)
+        ws_s = place("ws_s", [P, H], U8, AT_SCALES)
         wf_s = held("wf_s", [P, H], U8)
         off_rows = held("off_rows", [P, GROUP], F32)
         ident = held("ident", [P, P], F32)
@@ -135,10 +135,10 @@ def tile_list_mesh_block_refinement_kernel(
             out=tab2_w[:].bitcast(I32), in_=tab2_words[0].rearrange("p t i -> p (t i)").bitcast(I32)
         )
         wo_raw.append(load_wo("wo_raw1", 1, slice(0, N), AT_WO + PLANES))
-        wo_left = load_wo("wo_left", LAST, slice(0, N // 2), AT_WV_RAW)
+        wo_left = load_wo("wo_left", LAST, slice(0, N // 2), AT_HALVES)
         wf_last = load_words(held("wf_last", [P, 4 * GROUP], U8), wf_rows[:, LAST * GROUP :])
         wv_raw = [load_wv("wv_raw0", 0, GROUP, AT_WO + LAST * PLANES)]
-        wv_low = load_wv("wv_low", LAST * GROUP, GROUP // 2, AT_WV_RAW + WINDOW)
+        wv_low = load_wv("wv_low", LAST * GROUP, GROUP // 2, AT_HALVES + WINDOW)
         wv_raw.append(load_wv("wv_raw1", GROUP, GROUP, AT_TAB))
         wv_high = load_wv("wv_high", H - GROUP // 2, GROUP // 2, AT_TAB + PLANES)
         wo_right = load_wo("wo_right", LAST, slice(N // 2, N), AT_TAB + PLANES + WINDOW)
@@ -214,14 +214,12 @@ def tile_list_mesh_block_refinement_kernel(
         nc.vector.tensor_copy(v_s[:], tab_s[:].indirect(idx[:]))
         room = held("ws_head", [P, 3 * GROUP], U8)
         ws_slots = reorder_weight(room[:, GROUP:], room[:, :GROUP], ws_first[:], ws_s[:, :GROUP], 1, 2)
-        v2_s = held("v2_s", [P, M], U8)
-        nc.vector.tensor_copy(v2_s[:], tab2_s[:].indirect(idx2[:]))
         v_w = []
         for half in range(S // BANK):
             words = place("v_w%d" % half, [P, BANK], U32, AT_WOVEN + half * PLANES)
             nc.vector.tensor_copy(words[:], tab_w[:].indirect(idx[:, half * BANK // 16 : (half + 1) * BANK // 16]))
             v_w.append(words)
-        room = place("wf_head", [P, 5 * LAST * GROUP], U8, AT_WV_LAST)
+        room = place("wf_head", [P, 5 * LAST * GROUP], U8, AT_WF_HEAD)
         wf_slots = reorder_weight(
             room[:, LAST * GROUP :], room[:, : LAST * GROUP], wf_first[:], wf_s[:, : LAST * GROUP], LAST, 4
         )
@@ -229,6 +227,8 @@ def tile_list_mesh_block_refinement_kernel(
         ws_slots.extend(
             reorder_weight(room[:, LAST * GROUP :], room[:, : LAST * GROUP], ws_rest[:], ws_s[:, GROUP:], LAST, 2)
         )
+        v2_s = place("v2_s", [P, M], U8, AT_SCALES)
+        nc.vector.tensor_copy(v2_s[:], tab2_s[:].indirect(idx2[:]))
 
         def paired(pairs):
             return pairs.rearrange("p (u n e) -> p u e n", u=2, e=2)
@@ -239,16 +239,16 @@ def tile_list_mesh_block_refinement_kernel(
                     paired(pairs)[:, t // 2, t % 2], raw[:, t, :], off_sign[:, g, t : t + 1], 0.0, ALU.mult, ALU.add
                 )
 
-        def round_wv(copy, grouped, raw, runs=slice(0, P // RUN)):
+        def round_wv(copy, grouped, raw, runs=slice(0, P // RUN), slots=slice(0, PACK)):
             copy(
-                grouped.rearrange("p (t c i j) -> p t c j i", t=PACK, i=RUN, j=PACK)[:, :, runs],
-                raw.rearrange("p j (c t i) -> p t c j i", t=PACK, i=RUN),
+                grouped.rearrange("p (t c i j) -> p t c j i", t=PACK, i=RUN, j=PACK)[:, slots, runs],
+                raw.rearrange("p j (c t i) -> p t c j i", t=PACK, i=RUN)[:, slots],
             )
 
-        def weave(grouped, pairs):
-            nc.scalar.copy(
-                grouped.bitcast(U32).rearrange("p (n u) -> p n u", u=2),
-                pairs.bitcast(U32).rearrange("p (u n) -> p n u", u=2),
+        def weave(grouped, pairs, copy=nc.scalar.copy, word=U32):
+            copy(
+                grouped.bitcast(word).rearrange("p (n u) -> p n u", u=2),
+                pairs.bitcast(word).rearrange("p (u n) -> p n u", u=2),
             )
 
         wo_pairs = place("wo_pairs", [P, LAST * UNIT], BF16, AT_PAIRS)
@@ -257,10 +257,8 @@ def tile_list_mesh_block_refinement_kernel(
         left_pairs = held("left_pairs", [P, UNIT // 2], BF16)
         round_wo(nc.gpsimd, left_pairs[:], wo_left, LAST)
 
-        ring = [place("window0", [P, S], F32, AT_FIRST)]
-        ring.extend(place("window%d" % k, [P, S], F32, AT_RING + (k - 1) * WINDOW) for k in range(1, RING))
-        turns = [0, 1, 2, 3, 4, 5, 6, 0]
-        turns.extend(1 + k % (RING - 1) for k in range(6, 6 + 4 * PACK))
+        ring = [place("window%d" % k, [P, S], F32, AT_RING + k * WINDOW) for k in range(RING)]
+        turns = [k % RING for k in range(2 * GROUPS * PACK)]
 
         def coarse(func, factors, slots, dtype, g):
             windows = [ring[turns.pop(0)] for t in range(PACK)]
@@ -275,7 +273,7 @@ def tile_list_mesh_block_refinement_kernel(
             if not sets:
                 through_banks([jobs[0][0], jobs[1][0], jobs[0][1], jobs[1][1]], backwards=False)
             else:
-                through_banks(jobs[0] + jobs[1])
+                through_banks(jobs[0] + jobs[1], backwards=g > 0)
             through_banks(jobs[2] + jobs[3])
             return windows
 
@@ -300,21 +298,23 @@ def tile_list_mesh_block_refinement_kernel(
         limits = [place("limits%d" % g, [P, PACK, M], F32, AT_LIMITS + g * PLANES) for g in range(LAST)]
         for g in range(LAST):
             fine(limits[g], g)
-        wv_last = place("wv_last", [P, UNIT], BF16, AT_WV_LAST)
-        round_wv(nc.scalar.copy, wv_last[:], wv_low[:], slice(0, P // RUN // 2))
-
-        wv_grouped = place("wv_grouped", [P, LAST * UNIT], BF16, AT_WV)
-        round_wv(nc.vector.tensor_copy, wv_grouped[:, :UNIT], wv_raw[0][:])
-        room = place("wf_tail", [P, 5 * GROUP], U8, AT_WF)
+        wv_grouped = place("wv_grouped", [P, GROUPS * UNIT], BF16, AT_WV)
+        wv_last = wv_grouped[:, LAST * UNIT :]
+        round_wv(nc.scalar.copy, wv_last, wv_low[:], slice(0, P // RUN // 2))
+        for u in range(2):
+            round_wv(nc.vector.tensor_copy, wv_grouped[:, :UNIT], wv_raw[0][:], slots=slice(2 * u, 2 * u + 2))
+        wv_slots = []
+        for u in range(2):
+            wv_slots.extend(columns(quantize("wv0_%d" % u, wv_grouped[:, u * UNIT // 2 : (u + 1) * UNIT // 2]), P))
+        room = place("wf_tail", [P, 5 * GROUP], U8, AT_WF_TAIL)
         wf_slots.extend(reorder_weight(room[:, GROUP:], room[:, :GROUP], wf_last[:], wf_s[:, LAST * GROUP :], 1, 4))
-        wv_slots = columns(quantize("wv0", wv_grouped[:, :UNIT]), P)
         steps = [place("steps%d" % g, [P, PACK, M], F32, at) for g, at in enumerate((AT_WO + LAST * PLANES, AT_TAB + WINDOW))]
         nc.vector.tensor_tensor(steps[0][:], picks[0][:], limits[0][:], ALU.min)
-        round_wv(nc.vector.tensor_copy, wv_grouped[:, UNIT:], wv_raw[1][:])
-        round_wv(nc.vector.tensor_copy, wv_last[:], wv_high[:], slice(P // RUN // 2, P // RUN))
-        wv_slots.extend(columns(quantize("wv1", wv_grouped[:, UNIT:]), P))
-        wv_slots.extend(columns(quantize("wv2", wv_last[:]), P))
+        round_wv(nc.vector.tensor_copy, wv_grouped[:, UNIT : LAST * UNIT], wv_raw[1][:])
+        round_wv(nc.vector.tensor_copy, wv_last, wv_high[:], slice(P // RUN // 2, P // RUN))
+        wv_slots.extend(columns(quantize("wv1", wv_grouped[:, UNIT : LAST * UNIT]), P))
         nc.vector.tensor_tensor(steps[1][:], picks[1][:], limits[1][:], ALU.min)
+        wv_slots.extend(columns(quantize("wv2", wv_last), P))
 
         stage = place("stage", [P, LAST * UNIT + UNIT // 2], BF16, AT_LIMITS + WINDOW)
         right_pairs = stage[:, LAST * UNIT :]
@@ -330,7 +330,7 @@ def tile_list_mesh_block_refinement_kernel(
 
         pick(picks[LAST], coarse(ACT.Abs, off_size, ws_slots, FP4X4, LAST))
         windows = coarse(ACT.Copy, off_sign, wv_slots, FP8X4, LAST)
-        limits.append(place("limits2", [P, PACK, M], F32, AT_WV_RAW))
+        limits.append(place("limits2", [P, PACK, M], F32, AT_HALVES))
         fine(limits[LAST], LAST)
         woven = []
         for g in range(LAST):
@@ -338,7 +338,7 @@ def tile_list_mesh_block_refinement_kernel(
             weave(woven[g][:, :UNIT], wo_pairs[:, g * UNIT : (g + 1) * UNIT])
             weave(woven[g][:, UNIT:], stage[:, g * UNIT : (g + 1) * UNIT])
         woven.append(place("woven2", [P, UNIT], BF16, AT_WOVEN + LAST * PLANES))
-        weave(woven[LAST][:, : UNIT // 2], left_pairs[:])
+        weave(woven[LAST][:, : UNIT // 2], left_pairs[:], nc.vector.tensor_copy, I32)
         weave(woven[LAST][:, UNIT // 2 :], right_pairs)
         steps.append(place("steps2", [P, PACK, M], F32, AT_WO))
         for side in (slice(0, M // 2), slice(M // 2, M)):

@@ -99,9 +99,9 @@ def tile_list_mesh_block_refinement_kernel(
             nc.sync.dma_start(out=raw[:].bitcast(I32), in_=rows)
             return raw
 
-        def load_wo(name, g, cols, at):
-            raw = place(name, [P, PACK, cols.stop - cols.start], F32, at)
-            rows = wo[g * GROUP : (g + 1) * GROUP, cols].rearrange("(c t i) n -> t c i n", t=PACK, i=RUN)
+        def load_wo(g, at):
+            raw = place("wo_raw%d" % g, [P, PACK, N], F32, at)
+            rows = wo[g * GROUP : (g + 1) * GROUP, :].rearrange("(c t i) n -> t c i n", t=PACK, i=RUN)
             for t in range(PACK):
                 nc.sync.dma_start(out=raw[:, t, :], in_=rows[t])
             return raw
@@ -130,18 +130,17 @@ def tile_list_mesh_block_refinement_kernel(
         load_scales(wf_s, wf_scales, WF_ROW, nc.sync)
         ws_rest = load_words(place("ws_rest", [P, 2 * LAST * GROUP], U8, AT_PAIRS + WINDOW), ws_rows[:, ws_cut:])
         nc.sync.dma_start(p1[:], pos1)
-        wo_raw = [load_wo("wo_raw0", 0, slice(0, N), AT_WO)]
+        wo_raw = [load_wo(0, AT_WO)]
         nc.sync.dma_start(
             out=tab2_w[:].bitcast(I32), in_=tab2_words[0].rearrange("p t i -> p (t i)").bitcast(I32)
         )
-        wo_raw.append(load_wo("wo_raw1", 1, slice(0, N), AT_WO + PLANES))
-        wo_left = load_wo("wo_left", LAST, slice(0, N // 2), AT_HALVES)
+        wo_raw.append(load_wo(1, AT_WO + PLANES))
         wf_last = load_words(held("wf_last", [P, 4 * GROUP], U8), wf_rows[:, LAST * GROUP :])
         wv_raw = [load_wv("wv_raw0", 0, GROUP, AT_WO + LAST * PLANES)]
         wv_low = load_wv("wv_low", LAST * GROUP, GROUP // 2, AT_HALVES + WINDOW)
         wv_raw.append(load_wv("wv_raw1", GROUP, GROUP, AT_TAB))
         wv_high = load_wv("wv_high", H - GROUP // 2, GROUP // 2, AT_TAB + PLANES)
-        wo_right = load_wo("wo_right", LAST, slice(N // 2, N), AT_TAB + PLANES + WINDOW)
+        wo_raw.append(load_wo(LAST, AT_WO))
 
         def reorder(dst, src, count, bytes_per_col):
             w = RUN * bytes_per_col // 4
@@ -233,10 +232,10 @@ def tile_list_mesh_block_refinement_kernel(
         def paired(pairs):
             return pairs.rearrange("p (u n e) -> p u e n", u=2, e=2)
 
-        def round_wo(engine, pairs, raw, g):
-            for t in range(PACK):
-                engine.tensor_scalar(
-                    paired(pairs)[:, t // 2, t % 2], raw[:, t, :], off_sign[:, g, t : t + 1], 0.0, ALU.mult, ALU.add
+        def round_wo(pairs, g, slots):
+            for t in slots:
+                nc.gpsimd.tensor_scalar(
+                    paired(pairs)[:, t // 2, t % 2], wo_raw[g][:, t, :], off_sign[:, g, t : t + 1], 0.0, ALU.mult, ALU.add
                 )
 
         def round_wv(copy, grouped, raw, runs=slice(0, P // RUN), slots=slice(0, PACK)):
@@ -253,9 +252,7 @@ def tile_list_mesh_block_refinement_kernel(
 
         wo_pairs = place("wo_pairs", [P, LAST * UNIT], BF16, AT_PAIRS)
         for g in range(LAST):
-            round_wo(nc.gpsimd, wo_pairs[:, g * UNIT : (g + 1) * UNIT], wo_raw[g], g)
-        left_pairs = held("left_pairs", [P, UNIT // 2], BF16)
-        round_wo(nc.gpsimd, left_pairs[:], wo_left, LAST)
+            round_wo(wo_pairs[:, g * UNIT : (g + 1) * UNIT], g, range(PACK))
 
         ring = [place("window%d" % k, [P, S], F32, AT_RING + k * WINDOW) for k in range(RING)]
         turns = [k % RING for k in range(2 * GROUPS * PACK)]
@@ -316,9 +313,9 @@ def tile_list_mesh_block_refinement_kernel(
         nc.vector.tensor_tensor(steps[1][:], picks[1][:], limits[1][:], ALU.min)
         wv_slots.extend(columns(quantize("wv2", wv_last), P))
 
-        stage = place("stage", [P, LAST * UNIT + UNIT // 2], BF16, AT_LIMITS + WINDOW)
-        right_pairs = stage[:, LAST * UNIT :]
-        round_wo(nc.gpsimd, right_pairs, wo_right, LAST)
+        stage = place("stage", [P, GROUPS * UNIT], BF16, AT_LIMITS + WINDOW)
+        last_pairs = stage[:, LAST * UNIT :]
+        round_wo(last_pairs, LAST, range(PACK // 2))
         for g in range(LAST):
             values = picks[1 - g]
             pick(values, coarse(ACT.Copy, off_sign, wv_slots, FP8X4, g))
@@ -335,12 +332,19 @@ def tile_list_mesh_block_refinement_kernel(
         woven = []
         for g in range(LAST):
             woven.append(place("woven%d" % g, [P, 2 * UNIT], BF16, AT_WOVEN + g * PLANES))
-            weave(woven[g][:, :UNIT], wo_pairs[:, g * UNIT : (g + 1) * UNIT])
+            if g == 0:
+                weave(woven[g][:, :UNIT], wo_pairs[:, :UNIT], nc.vector.tensor_copy, I32)
+            else:
+                weave(woven[g][:, :UNIT], wo_pairs[:, UNIT:])
             weave(woven[g][:, UNIT:], stage[:, g * UNIT : (g + 1) * UNIT])
+        for t in range(PACK // 2, PACK):
+            nc.scalar.activation(
+                out=paired(last_pairs)[:, t // 2, t % 2], in_=wo_raw[LAST][:, t, :], func=ACT.Copy,
+                scale=off_sign[:, LAST, t : t + 1],
+            )
         woven.append(place("woven2", [P, UNIT], BF16, AT_WOVEN + LAST * PLANES))
-        weave(woven[LAST][:, : UNIT // 2], left_pairs[:], nc.vector.tensor_copy, I32)
-        weave(woven[LAST][:, UNIT // 2 :], right_pairs)
-        steps.append(place("steps2", [P, PACK, M], F32, AT_WO))
+        weave(woven[LAST][:], last_pairs)
+        steps.append(place("steps2", [P, PACK, M], F32, AT_TAB))
         for side in (slice(0, M // 2), slice(M // 2, M)):
             nc.vector.tensor_tensor(steps[LAST][:, :, side], picks[LAST][:, :, side], limits[LAST][:, :, side], ALU.min)
 

@@ -131,13 +131,13 @@ def tile_list_mesh_block_refinement_kernel(
         ws_rest = load_words(place("ws_rest", [P, 2 * LAST * GROUP], U8, AT_PAIRS + WINDOW), ws_rows[:, ws_cut:])
         nc.sync.dma_start(p1[:], pos1)
         wo_raw = [load_wo(0, AT_WO)]
+        wo_raw.append(load_wo(1, AT_WO + PLANES))
         nc.sync.dma_start(
             out=tab2_w[:].bitcast(I32), in_=tab2_words[0].rearrange("p t i -> p (t i)").bitcast(I32)
         )
-        wo_raw.append(load_wo(1, AT_WO + PLANES))
-        wf_last = load_words(held("wf_last", [P, 4 * GROUP], U8), wf_rows[:, LAST * GROUP :])
         wv_raw = [load_wv("wv_raw0", 0, GROUP, AT_WO + LAST * PLANES)]
         wv_low = load_wv("wv_low", LAST * GROUP, GROUP // 2, AT_HALVES + WINDOW)
+        wf_last = load_words(held("wf_last", [P, 4 * GROUP], U8), wf_rows[:, LAST * GROUP :])
         wv_raw.append(load_wv("wv_raw1", GROUP, GROUP, AT_TAB))
         wv_high = load_wv("wv_high", H - GROUP // 2, GROUP // 2, AT_TAB + PLANES)
         wo_raw.append(load_wo(LAST, AT_WO))
@@ -254,6 +254,13 @@ def tile_list_mesh_block_refinement_kernel(
         for g in range(LAST):
             round_wo(wo_pairs[:, g * UNIT : (g + 1) * UNIT], g, range(PACK))
 
+        wv_first = held("wv_first", [P, UNIT // 2], BF16)
+        nc.gpsimd.tensor_scalar(
+            wv_first[:].rearrange("p (t c i j) -> p c t i j", t=PACK // 2, i=RUN, j=PACK),
+            wv_raw[0][:].rearrange("p j (c t i) -> p c t i j", t=PACK, i=RUN)[:, :, : PACK // 2],
+            1.0, 0.0, ALU.mult, ALU.add,
+        )
+
         ring = [place("window%d" % k, [P, S], F32, AT_RING + k * WINDOW) for k in range(RING)]
         turns = [k % RING for k in range(2 * GROUPS * PACK)]
 
@@ -298,13 +305,11 @@ def tile_list_mesh_block_refinement_kernel(
         wv_grouped = place("wv_grouped", [P, GROUPS * UNIT], BF16, AT_WV)
         wv_last = wv_grouped[:, LAST * UNIT :]
         round_wv(nc.scalar.copy, wv_last, wv_low[:], slice(0, P // RUN // 2))
-        for u in range(2):
-            round_wv(nc.vector.tensor_copy, wv_grouped[:, :UNIT], wv_raw[0][:], slots=slice(2 * u, 2 * u + 2))
-        wv_slots = []
-        for u in range(2):
-            wv_slots.extend(columns(quantize("wv0_%d" % u, wv_grouped[:, u * UNIT // 2 : (u + 1) * UNIT // 2]), P))
+        wv_slots = columns(quantize("wv0_0", wv_first[:], AT_WF_HEAD + 2 * LAP), P)
+        round_wv(nc.vector.tensor_copy, wv_grouped[:, :UNIT], wv_raw[0][:], slots=slice(PACK // 2, PACK))
         room = place("wf_tail", [P, 5 * GROUP], U8, AT_WF_TAIL)
         wf_slots.extend(reorder_weight(room[:, GROUP:], room[:, :GROUP], wf_last[:], wf_s[:, LAST * GROUP :], 1, 4))
+        wv_slots.extend(columns(quantize("wv0_1", wv_grouped[:, UNIT // 2 : UNIT]), P))
         steps = [place("steps%d" % g, [P, PACK, M], F32, at) for g, at in enumerate((AT_WO + LAST * PLANES, AT_TAB + WINDOW))]
         nc.vector.tensor_tensor(steps[0][:], picks[0][:], limits[0][:], ALU.min)
         round_wv(nc.vector.tensor_copy, wv_grouped[:, UNIT : LAST * UNIT], wv_raw[1][:])

from contextlib import ExitStack

import concourse.mybir as mybir
from concourse.masks import make_identity

K, H, N, T, S, T2, M = 512, 1536, 512, 4096, 1024, 2048, 512
FLOPS = 2 * K * H * (2 * S + M) + 2 * H * N * M

F32 = mybir.dt.float32
BF16 = mybir.dt.bfloat16
I32 = mybir.dt.int32
U32 = mybir.dt.uint32
U16 = mybir.dt.uint16
U8 = mybir.dt.uint8
FP8X4 = mybir.dt.float8_e4m3fn_x4
FP4X4 = mybir.dt.float4_e2m1fn_x4
ALU = mybir.AluOpType
ACT = mybir.ActivationFunctionType

P = 128
PACK = 4
RUN = 4
GROUP = P * PACK
GROUPS = H // GROUP
LAST = GROUPS - 1
BANK = 512
SET = 4
UNIT = PACK * M
PARTS = (slice(0, M // 2), slice(M // 2, M // 2 + P), slice(M // 2 + P, M))
TAB_FIRST = T // 4
TAB_LAST = T - T // 4
TAB2_ROW = 4
WF_ROW = 8
RING = 11

KIB = 1024
WINDOW = 4 * KIB
PLANES = 8 * KIB
LAP = KIB // 2
AT_TAB = 0
AT_WO = AT_TAB + 2 * PLANES
AT_TAB2 = AT_WO + GROUPS * PLANES
AT_WF_TAIL = AT_TAB2 + PLANES
AT_WF_HEAD = AT_WF_TAIL + 5 * GROUP - LAP
AT_WV = AT_WF_HEAD + 5 * LAST * GROUP - LAP
AT_RING = AT_WV + 2 * GROUPS * UNIT
AT_PAIRS = AT_RING + RING * WINDOW
AT_LIMITS = AT_PAIRS + LAST * WINDOW
AT_WOVEN = AT_LIMITS + LAST * PLANES
AT_HALVES = AT_WOVEN + 5 * WINDOW
AT_PICKS = AT_HALVES + PLANES
AT_SCALES = AT_PICKS + PLANES


def tile_list_mesh_block_refinement_kernel(
    tc, tab_words, tab_scales, offs, pos1, tab2_words, tab2_scales, offs2, wv,
    ws_words, ws_scales, wf_words, wf_scales, off, wo, out,
):
    nc = tc.nc
    with ExitStack() as ctx:
        keep = ctx.enter_context(tc.tile_pool(name="keep", bufs=1))
        laid = ctx.enter_context(tc.tile_pool(name="laid", bufs=1))
        psum = ctx.enter_context(tc.psum_pool(name="psum", bufs=1))

        def held(name, shape, dtype):
            return keep.tile(shape, dtype, name=name, align_bytes=64)

        def place(name, shape, dtype, at):
            return laid.tile(shape, dtype, name=name, align_bytes=64, offset=at)

        banks = [psum.tile([P, BANK], F32, name="bank%d" % b) for b in range(2 * SET)]

        idx = held("idx", [P, S // 16], U16)
        idx2 = held("idx2", [P, M // 16], U16)
        p1 = held("p1", [P, M // 16], U16)
        tab_w = place("tab_w", [P, T], U32, AT_TAB)
        tab_s = held("tab_s", [P, T], U8)
        tab2_w = place("tab2_w", [P, T2], U32, AT_TAB2)
        tab2_s = held("tab2_s", [P, T2], U8)
        ws_s = place("ws_s", [P, H], U8, AT_SCALES)
        wf_s = held("wf_s", [P, H], U8)
        off_rows = held("off_rows", [P, GROUP], F32)
        ident = held("ident", [P, P], F32)

        nc.gpsimd.memset(off_rows[:], 0.0)
        for plane in (tab_s, ws_s, wf_s):
            nc.vector.memset(plane[:].bitcast(I32), 0)
        make_identity(nc, ident[:])
        nc.gpsimd.memset(tab2_s[:].bitcast(I32), 0)

        def load_scales(plane, scales, row, queue):
            for r in range(4):
                queue.dma_start(
                    out=plane[row + r : P : 32, :].bitcast(I32),
                    in_=scales[0, r : 16 : 4, :].bitcast(I32),
                )

        def load_words(raw, rows):
            nc.sync.dma_start(out=raw[:].bitcast(I32), in_=rows)
            return raw

        def load_wo(g, at):
            raw = place("wo_raw%d" % g, [P, PACK, N], F32, at)
            rows = wo[g * GROUP : (g + 1) * GROUP, :].rearrange("(c t i) n -> t c i n", t=PACK, i=RUN)
            for t in range(PACK):
                nc.sync.dma_start(out=raw[:, t, :], in_=rows[t])
            return raw

        def load_wv(name, first, width, at):
            raw = place(name, [P, PACK, width], F32, at)
            nc.sync.dma_start(out=raw[:], in_=wv[:, first : first + width].rearrange("(p j) r -> p j r", j=PACK))
            return raw

        tab_rows = tab_words[0].rearrange("p t i -> p (t i)").bitcast(I32)
        ws_rows = ws_words[0].bitcast(I32)
        ws_cut = 2 * GROUP // 4

        load_scales(tab2_s, tab2_scales, TAB2_ROW, nc.gpsimd)
        nc.sync.dma_start(idx[:], offs)
        nc.sync.dma_start(out=tab_w[:, :TAB_FIRST].bitcast(I32), in_=tab_rows[:, :TAB_FIRST])
        load_scales(tab_s, tab_scales, 0, nc.sync)
        ws_first = load_words(held("ws_first", [P, 2 * GROUP], U8), ws_rows[:, :ws_cut])
        nc.sync.dma_start(out=tab_w[:, TAB_FIRST:TAB_LAST].bitcast(I32), in_=tab_rows[:, TAB_FIRST:TAB_LAST])
        load_scales(ws_s, ws_scales, 0, nc.sync)
        nc.sync.dma_start(out=tab_w[:, TAB_LAST:].bitcast(I32), in_=tab_rows[:, TAB_LAST:])
        nc.scalar.dma_start(out=off_rows[0:GROUPS, :], in_=off.rearrange("(g r) -> g r", g=GROUPS))
        nc.sync.dma_start(idx2[:], offs2)
        wf_rows = wf_words[0].rearrange("p t i -> p (t i)").bitcast(I32)
        wf_first = load_words(place("wf_first", [P, 4 * LAST * GROUP], U8, AT_PAIRS), wf_rows[:, : LAST * GROUP])
        load_scales(wf_s, wf_scales, WF_ROW, nc.sync)
        ws_rest = load_words(place("ws_rest", [P, 2 * LAST * GROUP], U8, AT_PAIRS + WINDOW), ws_rows[:, ws_cut:])
        nc.sync.dma_start(p1[:], pos1)
        wo_raw = [load_wo(0, AT_WO)]
        wo_raw.append(load_wo(1, AT_WO + PLANES))
        nc.sync.dma_start(
            out=tab2_w[:].bitcast(I32), in_=tab2_words[0].rearrange("p t i -> p (t i)").bitcast(I32)
        )
        wv_raw = [load_wv("wv_raw0", 0, GROUP, AT_WO + LAST * PLANES)]
        wv_low = load_wv("wv_low", LAST * GROUP, GROUP // 2, AT_HALVES + WINDOW)
        wf_last = load_words(held("wf_last", [P, 4 * GROUP], U8), wf_rows[:, LAST * GROUP :])
        wv_raw.append(load_wv("wv_raw1", GROUP, GROUP, AT_TAB))
        wv_high = load_wv("wv_high", H - GROUP // 2, GROUP // 2, AT_TAB + PLANES)
        wo_raw.append(load_wo(LAST, AT_WO))

        def reorder(dst, src, count, bytes_per_col):
            w = RUN * bytes_per_col // 4
            nc.vector.tensor_copy(
                out=dst.bitcast(I32).rearrange("p (g t c w) -> p g t c w", g=count, t=PACK, w=w),
                in_=src.bitcast(I32).rearrange("p (g c t w) -> p g t c w", g=count, t=PACK, w=w),
            )
            return dst

        def reorder_weight(words, scales, raw, plane, count, bytes_per_col):
            reorder(scales, plane, count, 1)
            reorder(words, raw, count, bytes_per_col)
            return [
                (words[:, bytes_per_col * c : bytes_per_col * (c + P)], scales[:, c : c + P])
                for c in range(0, count * GROUP, P)
            ]

        def quantize(name, grouped, at=None):
            width = grouped.shape[1] // PACK
            shape = [P, width]
            codes = held(name + "_codes", shape, U32) if at is None else place(name + "_codes", shape, U32, at)
            scales = held(name + "_scales", [P, width], U8)
            nc.vector.quantize_mx(out=codes[:].bitcast(FP8X4), scales=scales[:], in_=grouped)
            return codes, scales

        def columns(quantized, width):
            codes, scales = quantized
            return [(codes[:, c : c + width], scales[:, c : c + width]) for c in range(0, codes.shape[1], width)]

        def round_planes(copy, grouped, planes):
            copy(
                grouped.rearrange("p (c i t) -> p c t i", i=4, t=PACK),
                planes.rearrange("p t (c i) -> p c t i", i=4),
            )

        freed = [list(range(SET)), list(range(SET, 2 * SET))]
        sets = []

        def through_banks(jobs, backwards=True):
            side = len(sets) % 2
            sets.append(side)
            order = list(reversed(jobs)) if backwards else jobs
            for number, (dst, func, factor, lhs, lhs_s, rhs, rhs_s) in zip(freed[side], order):
                nc.tensor.matmul_mx(
                    out=banks[number][:], lhsT=lhs, lhsT_scale=lhs_s, rhs=rhs, rhs_scale=rhs_s, start=True, stop=True
                )
            if backwards:
                freed[side].reverse()
            for number, job in zip(freed[side], jobs):
                nc.scalar.activation(out=job[0], in_=banks[number][:], func=job[1], scale=job[2])

        off_slots = held("off_slots", [P, GROUP], F32)
        off_col = held("off_col", [P, GROUPS, PACK], F32)
        off_size = held("off_size", [P, GROUPS, PACK], F32)
        off_twice = held("off_twice", [P, GROUPS, PACK], F32)
        off_sign = held("off_sign", [P, GROUPS, PACK], F32)
        nc.scalar.copy(
            off_slots[:].rearrange("p (t c i) -> p t c i", t=PACK, i=RUN),
            off_rows[:].rearrange("p (c t i) -> p t c i", t=PACK, i=RUN),
        )
        off_bank = banks[2 * SET - 1][:].rearrange("p (t c) -> p t c", t=PACK)
        for t in range(PACK):
            nc.tensor.transpose(off_bank[:, t, :], off_slots[:, t * P : (t + 1) * P], ident[:])
        nc.scalar.copy(out=off_col[:].rearrange("p g t -> p t g"), in_=off_bank[:, :, 0:GROUPS])
        nc.scalar.activation(out=off_size[:], in_=off_col[:], func=ACT.Abs)
        nc.gpsimd.tensor_scalar(off_twice[:], off_col[:], 0.0, 2.0, ALU.is_ge, ALU.mult)
        nc.gpsimd.tensor_scalar(off_sign[:], off_twice[:], 1.0, -1.0, ALU.mult, ALU.add)

        v_s = place("v_s", [P, S], U8, AT_WOVEN + 2 * PLANES)
        nc.vector.tensor_copy(v_s[:], tab_s[:].indirect(idx[:]))
        room = held("ws_head", [P, 3 * GROUP], U8)
        ws_slots = reorder_weight(room[:, GROUP:], room[:, :GROUP], ws_first[:], ws_s[:, :GROUP], 1, 2)
        v_w = []
        for half in range(S // BANK):
            words = place("v_w%d" % half, [P, BANK], U32, AT_WOVEN + half * PLANES)
            nc.vector.tensor_copy(words[:], tab_w[:].indirect(idx[:, half * BANK // 16 : (half + 1) * BANK // 16]))
            v_w.append(words)
        room = place("wf_head", [P, 5 * LAST * GROUP], U8, AT_WF_HEAD)
        wf_slots = reorder_weight(
            room[:, LAST * GROUP :], room[:, : LAST * GROUP], wf_first[:], wf_s[:, : LAST * GROUP], LAST, 4
        )
        room = held("ws_tail", [P, 3 * LAST * GROUP], U8)
        ws_slots.extend(
            reorder_weight(room[:, LAST * GROUP :], room[:, : LAST * GROUP], ws_rest[:], ws_s[:, GROUP:], LAST, 2)
        )
        v2_s = place("v2_s", [P, M], U8, AT_SCALES)
        nc.vector.tensor_copy(v2_s[:], tab2_s[:].indirect(idx2[:]))

        def paired(pairs):
            return pairs.rearrange("p (u n e) -> p u e n", u=2, e=2)

        def round_wo(pairs, g, slots):
            for t in slots:
                nc.gpsimd.tensor_scalar(
                    paired(pairs)[:, t // 2, t % 2], wo_raw[g][:, t, :], off_sign[:, g, t : t + 1], 0.0, ALU.mult, ALU.add
                )

        def round_wv(copy, grouped, raw, runs=slice(0, P // RUN), slots=slice(0, PACK)):
            copy(
                grouped.rearrange("p (t c i j) -> p t c j i", t=PACK, i=RUN, j=PACK)[:, slots, runs],
                raw.rearrange("p j (c t i) -> p t c j i", t=PACK, i=RUN)[:, slots],
            )

        def weave(grouped, pairs, copy=nc.scalar.copy, word=U32):
            copy(
                grouped.bitcast(word).rearrange("p (n u) -> p n u", u=2),
                pairs.bitcast(word).rearrange("p (u n) -> p n u", u=2),
            )

        wo_pairs = place("wo_pairs", [P, LAST * UNIT], BF16, AT_PAIRS)
        for g in range(LAST):
            round_wo(wo_pairs[:, g * UNIT : (g + 1) * UNIT], g, range(PACK))

        wv_first = held("wv_first", [P, UNIT // 2], BF16)
        nc.gpsimd.tensor_scalar(
            wv_first[:].rearrange("p (t c i j) -> p c t i j", t=PACK // 2, i=RUN, j=PACK),
            wv_raw[0][:].rearrange("p j (c t i) -> p c t i j", t=PACK, i=RUN)[:, :, : PACK // 2],
            1.0, 0.0, ALU.mult, ALU.add,
        )

        ring = [place("window%d" % k, [P, S], F32, AT_RING + k * WINDOW) for k in range(RING)]
        turns = [k % RING for k in range(2 * GROUPS * PACK)]

        def coarse(func, factors, slots, dtype, g):
            windows = [ring[turns.pop(0)] for t in range(PACK)]
            jobs = [
                [
                    (windows[t][:, c : c + BANK], func, factors[:, g, t : t + 1], lhs.bitcast(dtype), lhs_s,
                     words[:].bitcast(FP8X4), v_s[:, c : c + BANK])
                    for words, c in zip(v_w, range(0, S, BANK))
                ]
                for t, (lhs, lhs_s) in enumerate(slots[PACK * g : PACK * (g + 1)])
            ]
            if not sets:
                through_banks([jobs[0][0], jobs[1][0], jobs[0][1], jobs[1][1]], backwards=False)
            else:
                through_banks(jobs[0] + jobs[1], backwards=g > 0)
            through_banks(jobs[2] + jobs[3])
            return windows

        def pick(planes, windows):
            for t in range(PACK):
                nc.vector.tensor_copy(planes[:, t, :], windows[t][:].indirect(p1[:]))

        def fine(planes, g):
            through_banks([
                (planes[:, t, :], ACT.Abs, off_size[:, g, t : t + 1], words.bitcast(FP8X4), scales[WF_ROW:P, :],
                 v2_w[:].bitcast(FP8X4), v2_s[TAB2_ROW:P, :])
                for t, (words, scales) in enumerate(wf_slots[PACK * g : PACK * (g + 1)])
            ])

        picks = [place("picks%d" % g, [P, PACK, M], F32, at) for g, at in enumerate((AT_PICKS, AT_TAB2, AT_WO + PLANES))]
        v2_w = held("v2_w", [P, M], U32)
        for g in range(LAST):
            windows = coarse(ACT.Abs, off_size, ws_slots, FP4X4, g)
            if g > 0:
                nc.vector.tensor_copy(v2_w[:], tab2_w[:].indirect(idx2[:]))
            pick(picks[g], windows)
        limits = [place("limits%d" % g, [P, PACK, M], F32, AT_LIMITS + g * PLANES) for g in range(LAST)]
        for g in range(LAST):
            fine(limits[g], g)
        wv_grouped = place("wv_grouped", [P, GROUPS * UNIT], BF16, AT_WV)
        wv_last = wv_grouped[:, LAST * UNIT :]
        round_wv(nc.scalar.copy, wv_last, wv_low[:], slice(0, P // RUN // 2))
        wv_slots = columns(quantize("wv0_0", wv_first[:], AT_WF_HEAD + 2 * LAP), P)
        round_wv(nc.vector.tensor_copy, wv_grouped[:, :UNIT], wv_raw[0][:], slots=slice(PACK // 2, PACK))
        room = place("wf_tail", [P, 5 * GROUP], U8, AT_WF_TAIL)
        wf_slots.extend(reorder_weight(room[:, GROUP:], room[:, :GROUP], wf_last[:], wf_s[:, LAST * GROUP :], 1, 4))
        wv_slots.extend(columns(quantize("wv0_1", wv_grouped[:, UNIT // 2 : UNIT]), P))
        steps = [place("steps%d" % g, [P, PACK, M], F32, at) for g, at in enumerate((AT_WO + LAST * PLANES, AT_TAB + WINDOW))]
        nc.vector.tensor_tensor(steps[0][:], picks[0][:], limits[0][:], ALU.min)
        round_wv(nc.vector.tensor_copy, wv_grouped[:, UNIT : LAST * UNIT], wv_raw[1][:])
        round_wv(nc.vector.tensor_copy, wv_last, wv_high[:], slice(P // RUN // 2, P // RUN))
        wv_slots.extend(columns(quantize("wv1", wv_grouped[:, UNIT : LAST * UNIT]), P))
        nc.vector.tensor_tensor(steps[1][:], picks[1][:], limits[1][:], ALU.min)
        wv_slots.extend(columns(quantize("wv2", wv_last), P))

        stage = place("stage", [P, GROUPS * UNIT], BF16, AT_LIMITS + WINDOW)
        last_pairs = stage[:, LAST * UNIT :]
        round_wo(last_pairs, LAST, range(PACK // 2))
        for g in range(LAST):
            values = picks[1 - g]
            pick(values, coarse(ACT.Copy, off_sign, wv_slots, FP8X4, g))
            for u in range(2):
                two = slice(2 * u, 2 * u + 2)
                nc.gpsimd.tensor_tensor(
                    paired(stage[:, g * UNIT : (g + 1) * UNIT])[:, u], values[:, two, :], steps[g][:, two, :], ALU.add
                )

        pick(picks[LAST], coarse(ACT.Abs, off_size, ws_slots, FP4X4, LAST))
        windows = coarse(ACT.Copy, off_sign, wv_slots, FP8X4, LAST)
        limits.append(place("limits2", [P, PACK, M], F32, AT_HALVES))
        fine(limits[LAST], LAST)
        woven = []
        for g in range(LAST):
            woven.append(place("woven%d" % g, [P, 2 * UNIT], BF16, AT_WOVEN + g * PLANES))
            if g == 0:
                weave(woven[g][:, :UNIT], wo_pairs[:, :UNIT], nc.vector.tensor_copy, I32)
            else:
                weave(woven[g][:, :UNIT], wo_pairs[:, UNIT:])
            weave(woven[g][:, UNIT:], stage[:, g * UNIT : (g + 1) * UNIT])
        for t in range(PACK // 2, PACK):
            nc.scalar.activation(
                out=paired(last_pairs)[:, t // 2, t % 2], in_=wo_raw[LAST][:, t, :], func=ACT.Copy,
                scale=off_sign[:, LAST, t : t + 1],
            )
        woven.append(place("woven2", [P, UNIT], BF16, AT_WOVEN + LAST * PLANES))
        weave(woven[LAST][:], last_pairs)
        steps.append(place("steps2", [P, PACK, M], F32, AT_TAB))
        for side in (slice(0, M // 2), slice(M // 2, M)):
            nc.vector.tensor_tensor(steps[LAST][:, :, side], picks[LAST][:, :, side], limits[LAST][:, :, side], ALU.min)

        early = [columns(quantize("wo0_z0", woven[0][:]), M)]
        z_parts, rounded = [], []
        for k, part in enumerate(PARTS):
            width = part.stop - part.start
            sums = place("z_part%d" % k, [P, PACK, width], F32, AT_PICKS + 4 * PACK * part.start)
            offsets = p1[:, part.start // 16 : part.stop // 16]
            for t in range(PACK):
                nc.vector.tensor_tensor(sums[:, t, :], windows[t][:].indirect(offsets), steps[LAST][:, t, part], ALU.add)
            if k < LAST:
                early.append(columns(quantize("early%d" % k, woven[k + 1][:]), M))
            if k > 0:
                z_parts.append(quantize("z_part%d" % (k - 1), rounded[k - 1][:]))
            rounded.append(held("z_rounded%d" % k, [P, PACK * width], BF16))
            round_planes(nc.vector.tensor_copy if k == LAST else nc.scalar.copy, rounded[k][:], sums[:])
        z_parts.append(quantize("z_part%d" % k, rounded[k][:]))

        numbers = freed[len(sets) % 2] + freed[(len(sets) + 1) % 2]
        for g in range(GROUPS):
            for k, part in enumerate(PARTS):
                width = part.stop - part.start
                z_codes, z_scales = z_parts[k] if g == LAST else early[g][1]
                cols = slice(0, width) if g == LAST else part
                for n in range(N // P):
                    wo_codes, wo_scales = columns(early[g][0], P)[n]
                    nc.tensor.matmul_mx(
                        out=banks[numbers[2 * k + n // 2]][:, (n % 2) * width : (n % 2 + 1) * width],
                        lhsT=wo_codes.bitcast(FP8X4), lhsT_scale=wo_scales,
                        rhs=z_codes[:, cols].bitcast(FP8X4), rhs_scale=z_scales[:, cols],
                        start=(g == 0 and n % 2 == 0), stop=(g == LAST and n % 2 == 1),
                    )

        for k, part in enumerate(PARTS):
            width = part.stop - part.start
            for pair in range(2):
                results = place("results%d_%d" % (k, pair), [P, 2 * width], F32, AT_LIMITS + (2 * k + pair) * 2 * KIB)
                copy = nc.vector.tensor_copy if k == len(PARTS) - 1 and pair else nc.scalar.copy
                copy(results[:], banks[numbers[2 * k + pair]][:, : 2 * width])
                rows = out[2 * pair * P : 2 * (pair + 1) * P, part].rearrange("(u p) m -> p u m", u=2)
                nc.sync.dma_start(out=rows, in_=results[:].rearrange("p (u m) -> p u m", u=2))
